import numpy as np
import ml_dtypes


def mxq(x, axis, fmt="e4m3"):
    dtype, down = {"e4m3": (ml_dtypes.float8_e4m3fn, 7), "e5m2": (ml_dtypes.float8_e5m2, 14)}[fmt]
    v = np.moveaxis(np.asarray(x, np.float32).astype(ml_dtypes.bfloat16).astype(np.float64), axis, -1)
    blocks = v.reshape(v.shape[:-1] + (-1, 32))
    amax = np.abs(blocks).max(-1, keepdims=True)
    byte = np.maximum(np.where(amax > 0, np.frexp(amax)[1] - 1 + 127, 0) - down, 1)
    scale = np.exp2(byte - 127.0)
    codes = (blocks / scale).astype(np.float32).astype(dtype).astype(np.float64)
    return np.moveaxis((codes * scale).reshape(v.shape), -1, axis)


WIDE = False


def mx_kscale(k):
    if not WIDE:
        return np.ones(k)
    levels = np.array([10, -10, 5, -5, 0])
    if k % 512:
        return np.exp2(np.random.permutation(np.resize(levels, k // 32))).repeat(32)
    a = np.empty((k // 512, 16))
    for p in range(k // 512):
        a[p, :8] = np.random.permutation(np.resize(levels, 8))
        for g in range(8):
            far = levels[np.abs(levels - a[p, g]) >= 10]
            a[p, g + 8] = far[np.random.randint(len(far))]
    return np.exp2(a.ravel()).repeat(32)


def f64(x):
    return np.asarray(x).astype(np.float64)


def striped(idx):
    return np.tile(idx.reshape(-1, 16).T, (8, 1)).astype(np.uint16)


def unstriped(offs):
    return offs[:16].T.reshape(-1).astype(np.int64)


E2M1 = np.array([0.0, 0.5, 1.0, 1.5, 2.0, 3.0, 4.0, 6.0, -0.0, -0.5, -1.0, -1.5, -2.0, -3.0, -4.0, -6.0])


def pack_weight(w, fmt):
    k, n = w.shape
    w = f64(np.asarray(w, np.float32).astype(ml_dtypes.bfloat16)).reshape(k // 32, 32, n)
    amax = np.abs(w).max(1)
    if fmt == "e4m3":
        byte = np.frexp(amax)[1] - 1 + 127 - 7
    else:
        mant, ex = np.frexp(amax / 6.0)
        byte = np.where(mant > 0.5, ex, ex - 1) + 127
    byte = np.clip(np.where(amax > 0, byte, 1), 1, 254)
    scaled = (w * np.exp2(127.0 - byte)[:, None, :]).reshape(k, n).astype(np.float32)
    by_word = np.ascontiguousarray(scaled.reshape(k // 512, 128, 4, n).transpose(0, 1, 3, 2))
    if fmt == "e4m3":
        words = by_word.astype(ml_dtypes.float8_e4m3fn).view(np.uint8)
    else:
        c = by_word.astype(ml_dtypes.float4_e2m1fn).view(np.uint8) & 0xF
        words = (c[..., 0::2] | (c[..., 1::2] << 4)).reshape(k // 512, 128, 2 * n)
    return np.ascontiguousarray(words), np.ascontiguousarray(byte.astype(np.uint8).reshape(k // 512, 16, n))


def unpack_weight(words, scales, fmt):
    g, _, n = scales.shape
    words = np.ascontiguousarray(words).reshape(g, 128, n, -1)
    if fmt == "e4m3":
        vals = words.view(ml_dtypes.float8_e4m3fn).astype(np.float64)
    else:
        nib = np.empty((g, 128, n, 4), np.uint8)
        nib[..., 0::2] = words & 0xF
        nib[..., 1::2] = words >> 4
        vals = E2M1[nib]
    vals = vals * np.repeat(np.exp2(scales.astype(np.float64) - 127.0), 8, axis=1)[..., None]
    return vals.transpose(0, 1, 3, 2).reshape(g * 512, n)


def gelu(v):
    return 0.5 * v * (1.0 + np.tanh(np.sqrt(2.0 / np.pi) * (v + 0.044715 * v**3)))


K, T, P, K2, T2, S, H, N = 1024, 2048, 512, 512, 1024, 512, 1024, 512

def setup_inputs():
    n = np.random.standard_normal
    s = mx_kscale(K)[:, None]
    s2 = mx_kscale(K2)[:, None]
    u = mx_kscale(H)[:, None]
    tab_words, tab_scales = pack_weight(n((K, T)) * s, "e4m3")
    wb_words, wb_scales = pack_weight(n((K, H)) / np.sqrt(K) / s, "e2m1")
    wd_words, wd_scales = pack_weight(n((H, N)) / np.sqrt(H) / u, "e4m3")
    return {
        "tab_words": tab_words, "tab_scales": tab_scales,
        "offs": striped(np.random.permutation(T)[:P]),
        "offs2": striped(np.random.permutation(T2)[:S]),
        "offs3": striped(np.random.permutation(T2)[:P]),
        "base": (np.round(16 * n((K2, T2))) / 16 * s2).astype(np.float32),
        "xs": (np.round(16 * n((K2, S))) / 16 * s2).astype(np.float32),
        "wa": (n((K2, H)) / np.sqrt(K2) / s2 * u.T).astype(np.float32),
        "wb_words": wb_words, "wb_scales": wb_scales,
        "cal": (np.random.uniform(0.5, 1.5, H) * u[:, 0]).astype(np.float32),
        "wp": (n((H, N)) / np.sqrt(H) / u).astype(np.float32),
        "wd_words": wd_words, "wd_scales": wd_scales,
        "bo": (0.5 * n(N)).astype(np.float32),
    }

def reference(tab_words, tab_scales, offs, offs2, offs3, base, xs, wa, wb_words, wb_scales, cal, wp, wd_words, wd_scales, bo):
    page = f64(base).copy()
    page[:, unstriped(offs2)] = f64(xs)
    a = mxq(f64(wa), 0, "e4m3").T @ mxq(page, 0, "e4m3")
    at = a[:, unstriped(offs3)]
    v = unpack_weight(tab_words, tab_scales, "e4m3")[:, unstriped(offs)]
    b = unpack_weight(wb_words, wb_scales, "e2m1").T @ v
    x1 = mxq(at * b, 0, "e4m3")
    x2 = mxq(at - f64(cal)[:, None] * b, 0, "e4m3")
    y = mxq(f64(wp), 0, "e4m3").T @ x1 + unpack_weight(wd_words, wd_scales, "e4m3").T @ x2
    return y + f64(bo)[:, None]

@@ -1,0 +1,302 @@
+from contextlib import ExitStack
+
+import concourse.mybir as mybir
+
+K, T, S, K2, T2, H, N = 1024, 2048, 512, 512, 1024, 1024, 512
+PAIRS = 512
+FLOPS = 2 * (K2 * H * T2 + K * H * PAIRS + 2 * H * N * PAIRS)
+
+F32 = mybir.dt.float32
+BF16 = mybir.dt.bfloat16
+I32 = mybir.dt.int32
+U32 = mybir.dt.uint32
+U16 = mybir.dt.uint16
+U8 = mybir.dt.uint8
+FP8X4 = mybir.dt.float8_e4m3fn_x4
+FP4X4 = mybir.dt.float4_e2m1fn_x4
+ALU = mybir.AluOpType
+ACT = mybir.ActivationFunctionType
+
+P = 128
+PACK = 4
+LIVE = 100
+
+
+def tile_list_sonobuoy_bearing_pairs_kernel(
+    tc, tab_words, tab_scales, offs, offs2, offs3, base, xs, wa, wb_words, wb_scales, cal, wp, wd_words, wd_scales, bo, out
+):
+    nc = tc.nc
+    with ExitStack() as ctx:
+        keep = ctx.enter_context(tc.tile_pool(name="keep", bufs=1))
+        ring = ctx.enter_context(tc.tile_pool(name="ring", bufs=2))
+        psum = ctx.enter_context(tc.psum_pool(name="psum", bufs=1))
+
+        def sb(shape, dtype, name, tag=None):
+            return keep.tile(shape, dtype, name=name, tag=tag or name, align_bytes=64)
+
+        idx = keep.tile([P, PAIRS // 16], U16, name="idx")
+        idx2 = keep.tile([P, S // 16], U16, name="idx2")
+        idx3 = keep.tile([P, PAIRS // 16], U16, name="idx3")
+
+        tab_sc = sb([P, T], U8, "tab_sc")
+        wb_sc_raw = sb([P, H], U8, "wb_sc_raw")
+        wd_sc = sb([P, N], U8, "wd_sc")
+        v_sc1 = sb([P, PAIRS], U8, "v_sc1")
+        wb_sc1 = sb([P, H], U8, "wb_sc1")
+        for plane in (tab_sc, wb_sc_raw, wd_sc, v_sc1, wb_sc1):
+            nc.vector.memset(plane[:].bitcast(I32), 0)
+
+        def load_scales(plane, scales):
+            for q in range(4):
+                nc.sync.dma_start(
+                    out=plane[32 * q : 32 * q + 8, :].bitcast(I32),
+                    in_=scales[:, 4 * q : 4 * q + 4, :].bitcast(I32),
+                )
+
+        base_rows = base.rearrange("(p i) t -> p i t", i=PACK)
+        xs_rows = xs.rearrange("(p i) j -> p i j", i=PACK)
+        wa_rows = wa.rearrange("(p i) r -> p i r", i=PACK)
+        page = [sb([P, T2], F32, f"page{i}") for i in range(PACK)]
+        incoming = [sb([P, S], F32, f"incoming{i}") for i in range(PACK)]
+        wa_raw = [sb([P, PACK, 512], F32, f"wa_raw{g}") for g in range(2)]
+        wp_raw = [sb([P, PACK, N], F32, f"wp_raw{g}") for g in range(2)]
+        tab_w = [sb([P, T], I32, f"tab_w{a}") for a in range(2)]
+        wb_raw = sb([P, 2, 2 * H], U8, "wb_raw")
+        wd_w = sb([P, 2, N], I32, "wd_w")
+        cal_sb = sb([P, 2, PACK], F32, "cal_sb")
+        bo_sb = sb([P, 4], F32, "bo_sb")
+
+        def load_plane(i):
+            nc.sync.dma_start(out=page[i][:], in_=base_rows[:, i, :])
+            nc.sync.dma_start(out=incoming[i][:], in_=xs_rows[:, i, :])
+
+        nc.sync.dma_start(idx2[:], offs2)
+        load_plane(0)
+        load_plane(1)
+        nc.sync.dma_start(out=wa_raw[0][:], in_=wa_rows[:, :, 0:512])
+        load_plane(2)
+        nc.sync.dma_start(out=wa_raw[1][:], in_=wa_rows[:, :, 512:1024])
+        load_plane(3)
+        nc.sync.dma_start(idx[:], offs)
+        load_scales(tab_sc, tab_scales)
+        for a in range(2):
+            nc.sync.dma_start(out=tab_w[a][:], in_=tab_words[a].rearrange("p t i -> p (t i)").bitcast(I32))
+        load_scales(wb_sc_raw, wb_scales)
+        nc.sync.dma_start(out=wb_raw[:].bitcast(I32), in_=wb_words.rearrange("a p c -> p a c").bitcast(I32))
+        nc.sync.dma_start(idx3[:], offs3)
+        nc.sync.dma_start(out=cal_sb[:], in_=cal.rearrange("(g p t) -> p g t", g=2, t=PACK))
+        for g in range(2):
+            nc.sync.dma_start(
+                out=wp_raw[g][:], in_=wp[512 * g : 512 * (g + 1), :].rearrange("(p i) n -> p i n", i=PACK)
+            )
+        nc.sync.dma_start(out=wd_w[:], in_=wd_words.rearrange("a p c i -> p a (c i)").bitcast(I32))
+        load_scales(wd_sc, wd_scales)
+        with nc.allow_non_contiguous_dma(reason="one bias value a partition"):
+            nc.sync.dma_start(out=bo_sb[:], in_=bo.rearrange("(u p) -> p u", p=P))
+
+        page_pairs = sb([P, 2, T2, 2], BF16, "page_pairs")
+        for i in range(PACK):
+            nc.vector.tensor_copy(page[i][:].indirect(idx2[:]), incoming[i][:])
+            if i < PACK - 1:
+                nc.scalar.copy(out=page_pairs[:, i // 2, :, i % 2], in_=page[i][:])
+
+        wa_codes, wa_sc = [], []
+        for g in range(2):
+            wa_bf = sb([P, PACK, P, PACK], BF16, f"wa_bf{g}")
+            nc.scalar.copy(
+                out=wa_bf[:].rearrange("p t m i -> p m i t"),
+                in_=wa_raw[g][:].rearrange("p i (m t) -> p m i t", t=PACK),
+            )
+            codes = sb([P, 512], U32, f"wa_codes{g}", tag=f"incoming{3 - g}")
+            scales = sb([P, 512], U8, f"wa_sc{g}")
+            nc.vector.quantize_mx(
+                out=codes[:].bitcast(FP8X4), scales=scales[:], in_=wa_bf[:].rearrange("p t m i -> p (t m i)")
+            )
+            wa_codes.append(codes)
+            wa_sc.append(scales)
+
+        v_sc0 = sb([P, PAIRS], U8, "v_sc0")
+        nc.vector.tensor_copy(v_sc0[:], tab_sc[:].indirect(idx[:]))
+        nc.gpsimd.dma_start(out=v_sc1[0:LIVE, :].bitcast(I32), in_=v_sc0[4 : 4 + LIVE, :].bitcast(I32))
+        v_sc = (v_sc0, v_sc1)
+        v_w = [sb([P, PAIRS], U32, f"v_w{a}") for a in range(2)]
+
+        pair_words = page_pairs[:].rearrange("p w t e -> p w (t e)").bitcast(F32)
+        page_codes, page_sc = [], []
+        for h in range(2):
+            cols = slice(512 * h, 512 * (h + 1))
+            nc.vector.tensor_copy(v_w[h][:], tab_w[h][:].bitcast(U32).indirect(idx[:]))
+            nc.scalar.copy(out=page_pairs[:, 1, cols, 1], in_=page[PACK - 1][:, cols])
+            page_bf = sb([P, 512 * PACK], BF16, f"page_bf{h}")
+            nc.scalar.copy(
+                out=page_bf[:].bitcast(F32).rearrange("p (c i w) -> p c w i", i=2, w=2),
+                in_=pair_words[:, :, cols].rearrange("p w (c i) -> p c w i", i=2),
+            )
+            codes = sb([P, 512], U32, f"page_codes{h}", tag=("tab_sc", "page_codes1")[h])
+            scales = sb([P, 512], U8, f"page_sc{h}")
+            nc.vector.quantize_mx(out=codes[:].bitcast(FP8X4), scales=scales[:], in_=page_bf[:])
+            page_codes.append(codes)
+            page_sc.append(scales)
+
+        wb_sc0 = sb([P, H], U8, "wb_sc0")
+        nc.vector.tensor_copy(
+            out=wb_sc0[:].rearrange("p (g t m) -> p g t m", g=2, t=PACK),
+            in_=wb_sc_raw[:].rearrange("p (g m t) -> p g t m", g=2, t=PACK),
+        )
+        nc.gpsimd.dma_start(out=wb_sc1[0:LIVE, :].bitcast(I32), in_=wb_sc0[4 : 4 + LIVE, :].bitcast(I32))
+        wb_sc = (wb_sc0, wb_sc1)
+        wb_w = sb([P, 2, 2 * H], U8, "wb_w")
+        nc.vector.tensor_copy(
+            out=wb_w[:].rearrange("p a c -> p (a c)").bitcast(U16).rearrange("p (ag t mc i) -> p ag mc t i", ag=4, t=PACK, i=8),
+            in_=wb_raw[:].rearrange("p a c -> p (a c)").bitcast(U16).rearrange("p (ag mc i t) -> p ag mc t i", ag=4, t=PACK, i=8),
+        )
+
+        wp_codes, wp_sc = [], []
+
+        def quantise_wp(g):
+            wp_bf = sb([P, N * PACK], BF16, f"wp_bf{g}", tag=f"wa_bf{g}")
+            nc.scalar.copy(
+                out=wp_bf[:].rearrange("p (c e i) -> p c i e", e=2, i=PACK),
+                in_=wp_raw[g][:].rearrange("p i (c e) -> p c i e", e=2),
+            )
+            codes = sb([P, N], U32, f"wp_codes{g}")
+            scales = sb([P, N], U8, f"wp_sc{g}")
+            nc.vector.quantize_mx(out=codes[:].bitcast(FP8X4), scales=scales[:], in_=wp_bf[:])
+            wp_codes.append(codes)
+            wp_sc.append(scales)
+
+        y_banks = [[psum.tile([P, 2, 256], F32, name=f"y{h}{w}") for w in range(2)] for h in range(2)]
+        out_rows = out.rearrange("(u p) j -> p u j", p=P)
+        at = [sb([P, PACK, PAIRS], F32, f"at{g}") for g in range(2)]
+        x_bf = {}
+        x_q = {}
+        for g in range(2):
+            for h in range(2):
+                for s in range(2):
+                    x_bf[g, h, s] = sb([P, 256 * PACK], BF16, f"x_bf{g}{h}{s}")
+
+        def project_page(g, t):
+            a_sb = ring.tile([P, T2], F32, name="a_sb", bufs=6, align_bytes=64)
+            rows = slice(P * t, P * (t + 1))
+            for h in range(2):
+                a_bank = psum.tile([P, 512], F32, name="a_bank", tag="a_bank", bufs=2)
+                nc.tensor.matmul_mx(
+                    out=a_bank[:],
+                    lhsT=wa_codes[g][:, rows].bitcast(FP8X4),
+                    lhsT_scale=wa_sc[g][:, rows],
+                    rhs=page_codes[h][:].bitcast(FP8X4),
+                    rhs_scale=page_sc[h][:],
+                    start=True,
+                    stop=True,
+                )
+                nc.scalar.copy(out=a_sb[:, 512 * h : 512 * (h + 1)], in_=a_bank[:])
+            nc.vector.tensor_copy(at[g][:, t, :], a_sb[:].indirect(idx3[:]))
+
+        def compare(g, jc):
+            h, c = divmod(jc, 2)
+            cols = slice(P * jc, P * (jc + 1))
+            tag = "a_bank" if (g == 1 and h == 0) else "b_bank"
+            b_bank = psum.tile([P, PACK, P], F32, name="b_bank", tag=tag, bufs=2)
+            for t in range(PACK):
+                r0 = 512 * g + P * t
+                for a in range(2):
+                    nc.tensor.matmul_mx(
+                        out=b_bank[:, t, :],
+                        lhsT=wb_w[:, a, 2 * r0 : 2 * (r0 + P)].bitcast(FP4X4),
+                        lhsT_scale=wb_sc[a][:, r0 : r0 + P],
+                        rhs=v_w[a][:, cols].bitcast(FP8X4),
+                        rhs_scale=v_sc[a][:, cols],
+                        start=(a == 0),
+                        stop=(a == 1),
+                    )
+            cal_b = ring.tile([P, PACK, P], F32, name="cal_b", bufs=4, align_bytes=64)
+            for t in range(PACK):
+                nc.scalar.activation(
+                    out=cal_b[:, t, :], in_=b_bank[:, t, :], func=ACT.Copy, scale=cal_sb[:, g, t : t + 1]
+                )
+            walk_in = "p t (c e) -> p c t e"
+            walk_out = "p (c e t) -> p c t e"
+            at_part = at[g][:, :, cols].rearrange(walk_in, e=2)
+            x_cols = slice(512 * c, 512 * (c + 1))
+            nc.vector.tensor_tensor(
+                out=x_bf[g, h, 1][:, x_cols].rearrange(walk_out, e=2, t=PACK),
+                in0=b_bank[:].rearrange(walk_in, e=2),
+                in1=at_part,
+                op=ALU.mult,
+            )
+            nc.vector.tensor_tensor(
+                out=x_bf[g, h, 0][:, x_cols].rearrange(walk_out, e=2, t=PACK),
+                in0=at_part,
+                in1=cal_b[:].rearrange(walk_in, e=2),
+                op=ALU.subtract,
+            )
+
+        def quantise_x(g, h):
+            for s in (1, 0):
+                codes = sb([P, 256], U32, f"x_codes{g}{h}{s}")
+                scales = sb([P, 256], U8, f"x_sc{g}{h}{s}")
+                nc.vector.quantize_mx(out=codes[:].bitcast(FP8X4), scales=scales[:], in_=x_bf[g, h, s][:])
+                x_q[g, h, s] = (codes, scales)
+
+        def accumulate(g, h, s, first, last):
+            codes, scales = x_q[g, h, s]
+            for u in range(4):
+                n_cols = slice(P * u, P * (u + 1))
+                if s == 1:
+                    w_codes, w_sc = wp_codes[g][:, n_cols], wp_sc[g][:, n_cols]
+                else:
+                    w_codes, w_sc = wd_w[:, g, n_cols], wd_sc[4 * g : P, n_cols]
+                nc.tensor.matmul_mx(
+                    out=y_banks[h][u // 2][:, u % 2, :],
+                    lhsT=w_codes.bitcast(FP8X4),
+                    lhsT_scale=w_sc,
+                    rhs=codes[:].bitcast(FP8X4),
+                    rhs_scale=scales[:],
+                    start=(first and u % 2 == 0),
+                    stop=(last and u % 2 == 1),
+                )
+
+        def finish(h):
+            for w in range(2):
+                result = sb([P, 2, 256], F32, f"result{h}{w}")
+                for e in range(2):
+                    u = 2 * w + e
+                    if h == 1 and w == 1:
+                        nc.vector.tensor_scalar(
+                            out=result[:, e, :], in0=y_banks[h][w][:, e, :],
+                            scalar1=bo_sb[:, u : u + 1], scalar2=None, op0=ALU.add,
+                        )
+                    else:
+                        nc.scalar.activation(
+                            out=result[:, e, :], in_=y_banks[h][w][:, e, :],
+                            func=ACT.Identity, bias=bo_sb[:, u : u + 1], scale=1.0,
+                        )
+                nc.sync.dma_start(out=out_rows[:, 2 * w : 2 * w + 2, 256 * h : 256 * (h + 1)], in_=result[:])
+
+        for t in range(PACK):
+            project_page(0, t)
+        project_page(1, 0)
+        project_page(1, 1)
+        compare(0, 0)
+        compare(0, 1)
+        quantise_x(0, 0)
+        project_page(1, 2)
+        compare(0, 2)
+        project_page(1, 3)
+        compare(0, 3)
+        quantise_x(0, 1)
+        compare(1, 0)
+        compare(1, 1)
+        quantise_wp(0)
+        quantise_wp(1)
+        for h in range(2):
+            accumulate(0, h, 0, True, False)
+            accumulate(0, h, 1, False, False)
+        for h in range(2):
+            if h == 1:
+                compare(1, 2)
+                compare(1, 3)
+            quantise_x(1, h)
+            accumulate(1, h, 1, False, False)
+            accumulate(1, h, 0, False, True)
+            finish(h)

@@ -74,15 +74,15 @@ def tile_list_sonobuoy_bearing_pairs_kernel(
         load_plane(0)
         load_plane(1)
         nc.sync.dma_start(out=wa_raw[0][:], in_=wa_rows[:, :, 0:512])
+        load_scales(wb_sc_raw, wb_scales)
         load_plane(2)
         nc.sync.dma_start(out=wa_raw[1][:], in_=wa_rows[:, :, 512:1024])
         load_plane(3)
         nc.sync.dma_start(idx[:], offs)
         load_scales(tab_sc, tab_scales)
-        for a in range(2):
-            nc.sync.dma_start(out=tab_w[a][:], in_=tab_words[a].rearrange("p t i -> p (t i)").bitcast(I32))
-        load_scales(wb_sc_raw, wb_scales)
+        nc.sync.dma_start(out=tab_w[0][:], in_=tab_words[0].rearrange("p t i -> p (t i)").bitcast(I32))
         nc.sync.dma_start(out=wb_raw[:].bitcast(I32), in_=wb_words.rearrange("a p c -> p a c").bitcast(I32))
+        nc.sync.dma_start(out=tab_w[1][:], in_=tab_words[1].rearrange("p t i -> p (t i)").bitcast(I32))
         nc.sync.dma_start(idx3[:], offs3)
         nc.sync.dma_start(out=cal_sb[:], in_=cal.rearrange("(g p t) -> p g t", g=2, t=PACK))
         for g in range(2):
@@ -94,11 +94,12 @@ def tile_list_sonobuoy_bearing_pairs_kernel(
         with nc.allow_non_contiguous_dma(reason="one bias value a partition"):
             nc.sync.dma_start(out=bo_sb[:], in_=bo.rearrange("(u p) -> p u", p=P))
 
-        page_pairs = sb([P, 2, T2, 2], BF16, "page_pairs")
+        page_pairs = [sb([P, 2, 512, 2], BF16, f"page_pairs{h}") for h in range(2)]
         for i in range(PACK):
             nc.vector.tensor_copy(page[i][:].indirect(idx2[:]), incoming[i][:])
             if i < PACK - 1:
-                nc.scalar.copy(out=page_pairs[:, i // 2, :, i % 2], in_=page[i][:])
+                for h in range(2):
+                    nc.scalar.copy(out=page_pairs[h][:, i // 2, :, i % 2], in_=page[i][:, 512 * h : 512 * (h + 1)])
 
         wa_codes, wa_sc = [], []
         for g in range(2):
@@ -121,30 +122,31 @@ def tile_list_sonobuoy_bearing_pairs_kernel(
         v_sc = (v_sc0, v_sc1)
         v_w = [sb([P, PAIRS], U32, f"v_w{a}") for a in range(2)]
 
-        pair_words = page_pairs[:].rearrange("p w t e -> p w (t e)").bitcast(F32)
-        page_codes, page_sc = [], []
-        for h in range(2):
-            cols = slice(512 * h, 512 * (h + 1))
-            nc.vector.tensor_copy(v_w[h][:], tab_w[h][:].bitcast(U32).indirect(idx[:]))
-            nc.scalar.copy(out=page_pairs[:, 1, cols, 1], in_=page[PACK - 1][:, cols])
-            page_bf = sb([P, 512 * PACK], BF16, f"page_bf{h}")
-            nc.scalar.copy(
-                out=page_bf[:].bitcast(F32).rearrange("p (c i w) -> p c w i", i=2, w=2),
-                in_=pair_words[:, :, cols].rearrange("p w (c i) -> p c w i", i=2),
-            )
-            codes = sb([P, 512], U32, f"page_codes{h}", tag=("tab_sc", "page_codes1")[h])
-            scales = sb([P, 512], U8, f"page_sc{h}")
-            nc.vector.quantize_mx(out=codes[:].bitcast(FP8X4), scales=scales[:], in_=page_bf[:])
-            page_codes.append(codes)
-            page_sc.append(scales)
-
         wb_sc0 = sb([P, H], U8, "wb_sc0")
-        nc.vector.tensor_copy(
+        nc.gpsimd.tensor_copy(
             out=wb_sc0[:].rearrange("p (g t m) -> p g t m", g=2, t=PACK),
             in_=wb_sc_raw[:].rearrange("p (g m t) -> p g t m", g=2, t=PACK),
         )
         nc.gpsimd.dma_start(out=wb_sc1[0:LIVE, :].bitcast(I32), in_=wb_sc0[4 : 4 + LIVE, :].bitcast(I32))
         wb_sc = (wb_sc0, wb_sc1)
+        page_codes, page_sc = [], []
+        for h in range(2):
+            cols = slice(512 * h, 512 * (h + 1))
+            nc.scalar.copy(out=page_pairs[h][:, 1, :, 1], in_=page[PACK - 1][:, cols])
+            pair_words = page_pairs[h][:].rearrange("p w t e -> p w (t e)").bitcast(F32)
+            page_bf = sb([P, 512 * PACK], BF16, f"page_bf{h}")
+            nc.scalar.copy(
+                out=page_bf[:].bitcast(F32).rearrange("p (c i w) -> p c w i", i=2, w=2),
+                in_=pair_words.rearrange("p w (c i) -> p c w i", i=2),
+            )
+            codes = sb([P, 512], U32, f"page_codes{h}")
+            scales = sb([P, 512], U8, f"page_sc{h}")
+            nc.vector.quantize_mx(out=codes[:].bitcast(FP8X4), scales=scales[:], in_=page_bf[:])
+            page_codes.append(codes)
+            page_sc.append(scales)
+
+        for a in range(2):
+            nc.vector.tensor_copy(v_w[a][:], tab_w[a][:].bitcast(U32).indirect(idx[:]))
         wb_w = sb([P, 2, 2 * H], U8, "wb_w")
         nc.vector.tensor_copy(
             out=wb_w[:].rearrange("p a c -> p (a c)").bitcast(U16).rearrange("p (ag t mc i) -> p ag mc t i", ag=4, t=PACK, i=8),
@@ -224,7 +226,8 @@ def tile_list_sonobuoy_bearing_pairs_kernel(
                 in1=at_part,
                 op=ALU.mult,
             )
-            nc.vector.tensor_tensor(
+            engine = nc.vector if (g == 1 and h == 1) else nc.gpsimd
+            engine.tensor_tensor(
                 out=x_bf[g, h, 0][:, x_cols].rearrange(walk_out, e=2, t=PACK),
                 in0=at_part,
                 in1=cal_b[:].rearrange(walk_in, e=2),

@@ -19,7 +19,10 @@ ACT = mybir.ActivationFunctionType
 
 P = 128
 PACK = 4
-LIVE = 100
+PASS = P * PACK
+HALF = PAIRS // 2
+LAST_SCALE_ROW = 32 * 3 + 3
+DIFFERENCE, PRODUCT = 0, 1
 
 
 def tile_list_sonobuoy_bearing_pairs_kernel(
@@ -43,120 +46,136 @@ def tile_list_sonobuoy_bearing_pairs_kernel(
         wd_sc = sb([P, N], U8, "wd_sc")
         v_sc1 = sb([P, PAIRS], U8, "v_sc1")
         wb_sc1 = sb([P, H], U8, "wb_sc1")
-        for plane in (tab_sc, wb_sc_raw, wd_sc, v_sc1, wb_sc1):
-            nc.vector.memset(plane[:].bitcast(I32), 0)
+        for scale_tile in (tab_sc, wb_sc_raw, wd_sc, v_sc1, wb_sc1):
+            nc.vector.memset(scale_tile[:].bitcast(I32), 0)
 
-        def load_scales(plane, scales):
-            for q in range(4):
+        def load_scales(scale_tile, scales):
+            for quadrant in range(4):
                 nc.sync.dma_start(
-                    out=plane[32 * q : 32 * q + 8, :].bitcast(I32),
-                    in_=scales[:, 4 * q : 4 * q + 4, :].bitcast(I32),
+                    out=scale_tile[32 * quadrant : 32 * quadrant + 8, :].bitcast(I32),
+                    in_=scales[:, 4 * quadrant : 4 * quadrant + 4, :].bitcast(I32),
                 )
+
+        def second_pass_scales(target, both):
+            rows = LAST_SCALE_ROW + 1
+            nc.gpsimd.dma_start(out=target[0:rows, :].bitcast(I32), in_=both[4 : 4 + rows, :].bitcast(I32))
 
         base_rows = base.rearrange("(p i) t -> p i t", i=PACK)
         xs_rows = xs.rearrange("(p i) j -> p i j", i=PACK)
         wa_rows = wa.rearrange("(p i) r -> p i r", i=PACK)
         page = [sb([P, T2], F32, f"page{i}") for i in range(PACK)]
         incoming = [sb([P, S], F32, f"incoming{i}") for i in range(PACK)]
-        wa_raw = [sb([P, PACK, 512], F32, f"wa_raw{g}") for g in range(2)]
+        wa_raw = [sb([P, PACK, H // 4], F32, f"wa_raw{q}") for q in range(4)]
         wp_raw = [sb([P, PACK, N], F32, f"wp_raw{g}") for g in range(2)]
         tab_w = [sb([P, T], I32, f"tab_w{a}") for a in range(2)]
-        wb_raw = sb([P, 2, 2 * H], U8, "wb_raw")
+        wb_raw = sb([P, 2, H], U16, "wb_raw")
         wd_w = sb([P, 2, N], I32, "wd_w")
         cal_sb = sb([P, 2, PACK], F32, "cal_sb")
-        bo_sb = sb([P, 4], F32, "bo_sb")
+        bo_sb = sb([P, N // P], F32, "bo_sb")
 
-        def load_plane(i):
+        def load_page_rows(i):
             nc.sync.dma_start(out=page[i][:], in_=base_rows[:, i, :])
             nc.sync.dma_start(out=incoming[i][:], in_=xs_rows[:, i, :])
 
+        def load_wa_quarter(q):
+            nc.sync.dma_start(out=wa_raw[q][:], in_=wa_rows[:, :, (H // 4) * q : (H // 4) * (q + 1)])
+
+        def load_table(a):
+            nc.sync.dma_start(out=tab_w[a][:], in_=tab_words[a].rearrange("p t i -> p (t i)").bitcast(I32))
+
         nc.sync.dma_start(idx2[:], offs2)
-        load_plane(0)
-        load_plane(1)
-        nc.sync.dma_start(out=wa_raw[0][:], in_=wa_rows[:, :, 0:512])
+        load_page_rows(0)
+        load_wa_quarter(0)
+        load_page_rows(1)
         load_scales(wb_sc_raw, wb_scales)
-        load_plane(2)
-        nc.sync.dma_start(out=wa_raw[1][:], in_=wa_rows[:, :, 512:1024])
-        load_plane(3)
+        load_wa_quarter(1)
+        load_wa_quarter(2)
+        load_page_rows(2)
+        load_wa_quarter(3)
+        load_page_rows(3)
         nc.sync.dma_start(idx[:], offs)
         load_scales(tab_sc, tab_scales)
-        nc.sync.dma_start(out=tab_w[0][:], in_=tab_words[0].rearrange("p t i -> p (t i)").bitcast(I32))
+        load_table(0)
         nc.sync.dma_start(out=wb_raw[:].bitcast(I32), in_=wb_words.rearrange("a p c -> p a c").bitcast(I32))
-        nc.sync.dma_start(out=tab_w[1][:], in_=tab_words[1].rearrange("p t i -> p (t i)").bitcast(I32))
+        load_table(1)
         nc.sync.dma_start(idx3[:], offs3)
         nc.sync.dma_start(out=cal_sb[:], in_=cal.rearrange("(g p t) -> p g t", g=2, t=PACK))
         for g in range(2):
             nc.sync.dma_start(
-                out=wp_raw[g][:], in_=wp[512 * g : 512 * (g + 1), :].rearrange("(p i) n -> p i n", i=PACK)
+                out=wp_raw[g][:], in_=wp[PASS * g : PASS * (g + 1), :].rearrange("(p i) n -> p i n", i=PACK)
             )
         nc.sync.dma_start(out=wd_w[:], in_=wd_words.rearrange("a p c i -> p a (c i)").bitcast(I32))
         load_scales(wd_sc, wd_scales)
         with nc.allow_non_contiguous_dma(reason="one bias value a partition"):
             nc.sync.dma_start(out=bo_sb[:], in_=bo.rearrange("(u p) -> p u", p=P))
 
-        page_pairs = [sb([P, 2, 512, 2], BF16, f"page_pairs{h}") for h in range(2)]
+        wa_bf = sb([P, 2, PACK, P, PACK], BF16, "wa_bf")
+        for q in range(4):
+            g, part = divmod(q, 2)
+            nc.scalar.copy(
+                out=wa_bf[:, g, :, (P // 2) * part : (P // 2) * (part + 1), :].rearrange("p t c i -> p c i t"),
+                in_=wa_raw[q][:].rearrange("p i (c t) -> p c i t", t=PACK),
+            )
+
+        page_pairs = [sb([P, 2, PASS], F32, f"page_pairs{h}", tag=f"wa_raw{h}") for h in range(2)]
+
+        def round_page_rows(i, h):
+            values = page_pairs[h][:, i // 2, :].bitcast(BF16).rearrange("p (c e) -> p c e", e=2)
+            nc.scalar.copy(out=values[:, :, i % 2], in_=page[i][:, PASS * h : PASS * (h + 1)])
+
         for i in range(PACK):
             nc.vector.tensor_copy(page[i][:].indirect(idx2[:]), incoming[i][:])
             if i < PACK - 1:
                 for h in range(2):
-                    nc.scalar.copy(out=page_pairs[h][:, i // 2, :, i % 2], in_=page[i][:, 512 * h : 512 * (h + 1)])
+                    round_page_rows(i, h)
 
-        wa_codes, wa_sc = [], []
-        for g in range(2):
-            wa_bf = sb([P, PACK, P, PACK], BF16, f"wa_bf{g}")
-            nc.scalar.copy(
-                out=wa_bf[:].rearrange("p t m i -> p m i t"),
-                in_=wa_raw[g][:].rearrange("p i (m t) -> p m i t", t=PACK),
-            )
-            codes = sb([P, 512], U32, f"wa_codes{g}", tag=f"incoming{3 - g}")
-            scales = sb([P, 512], U8, f"wa_sc{g}")
-            nc.vector.quantize_mx(
-                out=codes[:].bitcast(FP8X4), scales=scales[:], in_=wa_bf[:].rearrange("p t m i -> p (t m i)")
-            )
-            wa_codes.append(codes)
-            wa_sc.append(scales)
+        wa_codes = sb([P, H], U32, "wa_codes", tag=f"incoming{PACK - 1}")
+        wa_sc = sb([P, H], U8, "wa_sc")
+        nc.vector.quantize_mx(
+            out=wa_codes[:].bitcast(FP8X4), scales=wa_sc[:], in_=wa_bf[:].rearrange("p g t c i -> p (g t c i)")
+        )
 
         v_sc0 = sb([P, PAIRS], U8, "v_sc0")
         nc.vector.tensor_copy(v_sc0[:], tab_sc[:].indirect(idx[:]))
-        nc.gpsimd.dma_start(out=v_sc1[0:LIVE, :].bitcast(I32), in_=v_sc0[4 : 4 + LIVE, :].bitcast(I32))
+        second_pass_scales(v_sc1, v_sc0)
         v_sc = (v_sc0, v_sc1)
-        v_w = [sb([P, PAIRS], U32, f"v_w{a}") for a in range(2)]
 
         wb_sc0 = sb([P, H], U8, "wb_sc0")
         nc.gpsimd.tensor_copy(
-            out=wb_sc0[:].rearrange("p (g t m) -> p g t m", g=2, t=PACK),
-            in_=wb_sc_raw[:].rearrange("p (g m t) -> p g t m", g=2, t=PACK),
+            out=wb_sc0[:].rearrange("p (g t c) -> p g t c", g=2, t=PACK),
+            in_=wb_sc_raw[:].rearrange("p (g c t) -> p g t c", g=2, t=PACK),
         )
-        nc.gpsimd.dma_start(out=wb_sc1[0:LIVE, :].bitcast(I32), in_=wb_sc0[4 : 4 + LIVE, :].bitcast(I32))
+        second_pass_scales(wb_sc1, wb_sc0)
         wb_sc = (wb_sc0, wb_sc1)
+
         page_codes, page_sc = [], []
         for h in range(2):
-            cols = slice(512 * h, 512 * (h + 1))
-            nc.scalar.copy(out=page_pairs[h][:, 1, :, 1], in_=page[PACK - 1][:, cols])
-            pair_words = page_pairs[h][:].rearrange("p w t e -> p w (t e)").bitcast(F32)
-            page_bf = sb([P, 512 * PACK], BF16, f"page_bf{h}")
-            nc.scalar.copy(
-                out=page_bf[:].bitcast(F32).rearrange("p (c i w) -> p c w i", i=2, w=2),
-                in_=pair_words.rearrange("p w (c i) -> p c w i", i=2),
+            round_page_rows(PACK - 1, h)
+            page_bf = sb([P, PASS, 2], F32, f"page_bf{h}")
+            nc.scalar.copy(out=page_bf[:], in_=page_pairs[h][:].rearrange("p w c -> p c w"))
+            codes = sb([P, PASS], U32, f"page_codes{h}")
+            scales = sb([P, PASS], U8, f"page_sc{h}")
+            nc.vector.quantize_mx(
+                out=codes[:].bitcast(FP8X4),
+                scales=scales[:],
+                in_=page_bf[:].rearrange("p c w -> p (c w)").bitcast(BF16),
             )
-            codes = sb([P, 512], U32, f"page_codes{h}")
-            scales = sb([P, 512], U8, f"page_sc{h}")
-            nc.vector.quantize_mx(out=codes[:].bitcast(FP8X4), scales=scales[:], in_=page_bf[:])
             page_codes.append(codes)
             page_sc.append(scales)
 
+        v_w = [sb([P, PAIRS], U32, "v_w0", tag="page_bf0"), sb([P, PAIRS], U32, "v_w1")]
         for a in range(2):
             nc.vector.tensor_copy(v_w[a][:], tab_w[a][:].bitcast(U32).indirect(idx[:]))
-        wb_w = sb([P, 2, 2 * H], U8, "wb_w")
+        wb_w = sb([P, 2, H], U16, "wb_w", tag="page_bf1")
         nc.vector.tensor_copy(
-            out=wb_w[:].rearrange("p a c -> p (a c)").bitcast(U16).rearrange("p (ag t mc i) -> p ag mc t i", ag=4, t=PACK, i=8),
-            in_=wb_raw[:].rearrange("p a c -> p (a c)").bitcast(U16).rearrange("p (ag mc i t) -> p ag mc t i", ag=4, t=PACK, i=8),
+            out=wb_w[:].rearrange("p a c -> p (a c)").rearrange("p (ag t c e) -> p ag c t e", ag=4, t=PACK, e=8),
+            in_=wb_raw[:].rearrange("p a c -> p (a c)").rearrange("p (ag c e t) -> p ag c t e", ag=4, t=PACK, e=8),
         )
 
         wp_codes, wp_sc = [], []
 
         def quantise_wp(g):
-            wp_bf = sb([P, N * PACK], BF16, f"wp_bf{g}", tag=f"wa_bf{g}")
+            wp_bf = sb([P, N * PACK], BF16, f"wp_bf{g}")
             nc.scalar.copy(
                 out=wp_bf[:].rearrange("p (c e i) -> p c i e", e=2, i=PACK),
                 in_=wp_raw[g][:].rearrange("p i (c e) -> p c i e", e=2),
@@ -167,44 +186,44 @@ def tile_list_sonobuoy_bearing_pairs_kernel(
             wp_codes.append(codes)
             wp_sc.append(scales)
 
-        y_banks = [[psum.tile([P, 2, 256], F32, name=f"y{h}{w}") for w in range(2)] for h in range(2)]
+        y_half = [psum.tile([P, 2, HALF], F32, name=f"y_half{w}") for w in range(2)]
+        y_quarter = [psum.tile([P, N // P, P], F32, name=f"y_quarter{c}") for c in range(2)]
         out_rows = out.rearrange("(u p) j -> p u j", p=P)
         at = [sb([P, PACK, PAIRS], F32, f"at{g}") for g in range(2)]
         x_bf = {}
-        x_q = {}
         for g in range(2):
             for h in range(2):
-                for s in range(2):
-                    x_bf[g, h, s] = sb([P, 256 * PACK], BF16, f"x_bf{g}{h}{s}")
+                for kind in (DIFFERENCE, PRODUCT):
+                    x_bf[g, h, kind] = sb([P, HALF * PACK], BF16, f"x_bf{g}{h}{kind}")
 
         def project_page(g, t):
             a_sb = ring.tile([P, T2], F32, name="a_sb", bufs=6, align_bytes=64)
-            rows = slice(P * t, P * (t + 1))
+            rows = slice(PASS * g + P * t, PASS * g + P * (t + 1))
             for h in range(2):
-                a_bank = psum.tile([P, 512], F32, name="a_bank", tag="a_bank", bufs=2)
+                a_bank = psum.tile([P, PASS], F32, name="a_bank", tag="a_bank", bufs=2)
                 nc.tensor.matmul_mx(
                     out=a_bank[:],
-                    lhsT=wa_codes[g][:, rows].bitcast(FP8X4),
-                    lhsT_scale=wa_sc[g][:, rows],
+                    lhsT=wa_codes[:, rows].bitcast(FP8X4),
+                    lhsT_scale=wa_sc[:, rows],
                     rhs=page_codes[h][:].bitcast(FP8X4),
                     rhs_scale=page_sc[h][:],
                     start=True,
                     stop=True,
                 )
-                nc.scalar.copy(out=a_sb[:, 512 * h : 512 * (h + 1)], in_=a_bank[:])
+                nc.scalar.copy(out=a_sb[:, PASS * h : PASS * (h + 1)], in_=a_bank[:])
             nc.vector.tensor_copy(at[g][:, t, :], a_sb[:].indirect(idx3[:]))
 
-        def compare(g, jc):
-            h, c = divmod(jc, 2)
-            cols = slice(P * jc, P * (jc + 1))
+        def compare(g, quarter):
+            h, c = divmod(quarter, 2)
+            cols = slice(P * quarter, P * (quarter + 1))
             tag = "a_bank" if (g == 1 and h == 0) else "b_bank"
             b_bank = psum.tile([P, PACK, P], F32, name="b_bank", tag=tag, bufs=2)
             for t in range(PACK):
-                r0 = 512 * g + P * t
+                r0 = PASS * g + P * t
                 for a in range(2):
                     nc.tensor.matmul_mx(
                         out=b_bank[:, t, :],
-                        lhsT=wb_w[:, a, 2 * r0 : 2 * (r0 + P)].bitcast(FP4X4),
+                        lhsT=wb_w[:, a, r0 : r0 + P].bitcast(FP4X4),
                         lhsT_scale=wb_sc[a][:, r0 : r0 + P],
                         rhs=v_w[a][:, cols].bitcast(FP8X4),
                         rhs_scale=v_sc[a][:, cols],
@@ -219,87 +238,102 @@ def tile_list_sonobuoy_bearing_pairs_kernel(
             walk_in = "p t (c e) -> p c t e"
             walk_out = "p (c e t) -> p c t e"
             at_part = at[g][:, :, cols].rearrange(walk_in, e=2)
-            x_cols = slice(512 * c, 512 * (c + 1))
+            x_cols = slice(PASS * c, PASS * (c + 1))
             nc.vector.tensor_tensor(
-                out=x_bf[g, h, 1][:, x_cols].rearrange(walk_out, e=2, t=PACK),
+                out=x_bf[g, h, PRODUCT][:, x_cols].rearrange(walk_out, e=2, t=PACK),
                 in0=b_bank[:].rearrange(walk_in, e=2),
                 in1=at_part,
                 op=ALU.mult,
             )
             engine = nc.vector if (g == 1 and h == 1) else nc.gpsimd
             engine.tensor_tensor(
-                out=x_bf[g, h, 0][:, x_cols].rearrange(walk_out, e=2, t=PACK),
+                out=x_bf[g, h, DIFFERENCE][:, x_cols].rearrange(walk_out, e=2, t=PACK),
                 in0=at_part,
                 in1=cal_b[:].rearrange(walk_in, e=2),
                 op=ALU.subtract,
             )
 
-        def quantise_x(g, h):
-            for s in (1, 0):
-                codes = sb([P, 256], U32, f"x_codes{g}{h}{s}")
-                scales = sb([P, 256], U8, f"x_sc{g}{h}{s}")
-                nc.vector.quantize_mx(out=codes[:].bitcast(FP8X4), scales=scales[:], in_=x_bf[g, h, s][:])
-                x_q[g, h, s] = (codes, scales)
+        def quantise_x(g, h, kind, cols):
+            width = cols.stop - cols.start
+            name = f"{g}{h}{kind}{cols.start}"
+            codes = sb([P, width], U32, "x_codes" + name)
+            scales = sb([P, width], U8, "x_sc" + name)
+            nc.vector.quantize_mx(
+                out=codes[:].bitcast(FP8X4),
+                scales=scales[:],
+                in_=x_bf[g, h, kind][:, PACK * cols.start : PACK * cols.stop],
+            )
+            return codes, scales
 
-        def accumulate(g, h, s, first, last):
-            codes, scales = x_q[g, h, s]
-            for u in range(4):
+        def accumulate(targets, g, kind, x, cols, first, last):
+            codes, scales = x
+            for u, (target, opens, closes) in enumerate(targets):
                 n_cols = slice(P * u, P * (u + 1))
-                if s == 1:
+                if kind == PRODUCT:
                     w_codes, w_sc = wp_codes[g][:, n_cols], wp_sc[g][:, n_cols]
                 else:
                     w_codes, w_sc = wd_w[:, g, n_cols], wd_sc[4 * g : P, n_cols]
                 nc.tensor.matmul_mx(
-                    out=y_banks[h][u // 2][:, u % 2, :],
+                    out=target,
                     lhsT=w_codes.bitcast(FP8X4),
                     lhsT_scale=w_sc,
-                    rhs=codes[:].bitcast(FP8X4),
-                    rhs_scale=scales[:],
-                    start=(first and u % 2 == 0),
-                    stop=(last and u % 2 == 1),
+                    rhs=codes[:, cols].bitcast(FP8X4),
+                    rhs_scale=scales[:, cols],
+                    start=(first and opens),
+                    stop=(last and closes),
                 )
 
-        def finish(h):
-            for w in range(2):
-                result = sb([P, 2, 256], F32, f"result{h}{w}")
-                for e in range(2):
-                    u = 2 * w + e
-                    if h == 1 and w == 1:
-                        nc.vector.tensor_scalar(
-                            out=result[:, e, :], in0=y_banks[h][w][:, e, :],
-                            scalar1=bo_sb[:, u : u + 1], scalar2=None, op0=ALU.add,
-                        )
-                    else:
-                        nc.scalar.activation(
-                            out=result[:, e, :], in_=y_banks[h][w][:, e, :],
-                            func=ACT.Identity, bias=bo_sb[:, u : u + 1], scale=1.0,
-                        )
-                nc.sync.dma_start(out=out_rows[:, 2 * w : 2 * w + 2, 256 * h : 256 * (h + 1)], in_=result[:])
+        half_targets = [(y_half[u // 2][:, u % 2, :], u % 2 == 0, u % 2 == 1) for u in range(4)]
+        quarter_targets = [[(y_quarter[c][:, u, :], u == 0, u == 3) for u in range(4)] for c in range(2)]
+        whole = slice(0, HALF)
+        parts = [slice(0, P), slice(P, 2 * P)]
 
+        def add_bias(result, target, u):
+            nc.scalar.activation(out=result, in_=target, func=ACT.Identity, bias=bo_sb[:, u : u + 1], scale=1.0)
+
+        x0 = {}
         for t in range(PACK):
             project_page(0, t)
         project_page(1, 0)
         project_page(1, 1)
         compare(0, 0)
         compare(0, 1)
-        quantise_x(0, 0)
+        for kind in (PRODUCT, DIFFERENCE):
+            x0[0, kind] = quantise_x(0, 0, kind, whole)
         project_page(1, 2)
         compare(0, 2)
         project_page(1, 3)
         compare(0, 3)
-        quantise_x(0, 1)
+        for kind in (PRODUCT, DIFFERENCE):
+            x0[1, kind] = quantise_x(0, 1, kind, whole)
+
         compare(1, 0)
         compare(1, 1)
         quantise_wp(0)
         quantise_wp(1)
-        for h in range(2):
-            accumulate(0, h, 0, True, False)
-            accumulate(0, h, 1, False, False)
-        for h in range(2):
-            if h == 1:
-                compare(1, 2)
-                compare(1, 3)
-            quantise_x(1, h)
-            accumulate(1, h, 1, False, False)
-            accumulate(1, h, 0, False, True)
-            finish(h)
+        for kind in (DIFFERENCE, PRODUCT):
+            accumulate(half_targets, 0, kind, x0[0, kind], whole, kind == DIFFERENCE, False)
+        for kind in (DIFFERENCE, PRODUCT):
+            for c in range(2):
+                accumulate(quarter_targets[c], 0, kind, x0[1, kind], parts[c], kind == DIFFERENCE, False)
+        for kind in (PRODUCT, DIFFERENCE):
+            accumulate(half_targets, 1, kind, quantise_x(1, 0, kind, whole), whole, False, kind == DIFFERENCE)
+        for w in range(2):
+            result = sb([P, 2, HALF], F32, f"result_half{w}")
+            for e in range(2):
+                add_bias(result[:, e, :], y_half[w][:, e, :], 2 * w + e)
+            nc.sync.dma_start(out=out_rows[:, 2 * w : 2 * w + 2, whole], in_=result[:])
+
+        for c in range(2):
+            compare(1, 2 + c)
+            for kind in (PRODUCT, DIFFERENCE):
+                x = quantise_x(1, 1, kind, parts[c])
+                accumulate(quarter_targets[c], 1, kind, x, parts[0], False, kind == DIFFERENCE)
+            result = sb([P, N // P, P], F32, f"result_quarter{c}")
+            if c == 0:
+                for u in range(N // P):
+                    add_bias(result[:, u, :], y_quarter[c][:, u, :], u)
+            else:
+                bias = bo_sb[:].unsqueeze(2).to_broadcast([P, N // P, P])
+                nc.vector.tensor_tensor(out=result[:], in0=y_quarter[c][:], in1=bias, op=ALU.add)
+            nc.sync.dma_start(out=out_rows[:, :, HALF + P * c : HALF + P * (c + 1)], in_=result[:])

@@ -93,10 +93,10 @@ def tile_list_sonobuoy_bearing_pairs_kernel(
         load_page_rows(2)
         load_wa_quarter(3)
         load_page_rows(3)
+        nc.sync.dma_start(out=wb_raw[:].bitcast(I32), in_=wb_words.rearrange("a p c -> p a c").bitcast(I32))
         nc.sync.dma_start(idx[:], offs)
         load_scales(tab_sc, tab_scales)
         load_table(0)
-        nc.sync.dma_start(out=wb_raw[:].bitcast(I32), in_=wb_words.rearrange("a p c -> p a c").bitcast(I32))
         load_table(1)
         nc.sync.dma_start(idx3[:], offs3)
         nc.sync.dma_start(out=cal_sb[:], in_=cal.rearrange("(g p t) -> p g t", g=2, t=PACK))
@@ -166,8 +166,8 @@ def tile_list_sonobuoy_bearing_pairs_kernel(
         v_w = [sb([P, PAIRS], U32, "v_w0", tag="page_bf0"), sb([P, PAIRS], U32, "v_w1")]
         for a in range(2):
             nc.vector.tensor_copy(v_w[a][:], tab_w[a][:].bitcast(U32).indirect(idx[:]))
-        wb_w = sb([P, 2, H], U16, "wb_w", tag="page_bf1")
-        nc.vector.tensor_copy(
+        wb_w = sb([P, 2, H], U16, "wb_w")
+        nc.gpsimd.tensor_copy(
             out=wb_w[:].rearrange("p a c -> p (a c)").rearrange("p (ag t c e) -> p ag c t e", ag=4, t=PACK, e=8),
             in_=wb_raw[:].rearrange("p a c -> p (a c)").rearrange("p (ag c e t) -> p ag c t e", ag=4, t=PACK, e=8),
         )
@@ -237,19 +237,19 @@ def tile_list_sonobuoy_bearing_pairs_kernel(
                 )
             walk_in = "p t (c e) -> p c t e"
             walk_out = "p (c e t) -> p c t e"
-            at_part = at[g][:, :, cols].rearrange(walk_in, e=2)
+            at_part = at[g][:, :, cols].rearrange(walk_in, e=4)
             x_cols = slice(PASS * c, PASS * (c + 1))
             nc.vector.tensor_tensor(
-                out=x_bf[g, h, PRODUCT][:, x_cols].rearrange(walk_out, e=2, t=PACK),
-                in0=b_bank[:].rearrange(walk_in, e=2),
+                out=x_bf[g, h, PRODUCT][:, x_cols].rearrange(walk_out, e=4, t=PACK),
+                in0=b_bank[:].rearrange(walk_in, e=4),
                 in1=at_part,
                 op=ALU.mult,
             )
             engine = nc.vector if (g == 1 and h == 1) else nc.gpsimd
             engine.tensor_tensor(
-                out=x_bf[g, h, DIFFERENCE][:, x_cols].rearrange(walk_out, e=2, t=PACK),
+                out=x_bf[g, h, DIFFERENCE][:, x_cols].rearrange(walk_out, e=4, t=PACK),
                 in0=at_part,
-                in1=cal_b[:].rearrange(walk_in, e=2),
+                in1=cal_b[:].rearrange(walk_in, e=4),
                 op=ALU.subtract,
             )
 

@@ -22,7 +22,7 @@ PACK = 4
 PASS = P * PACK
 HALF = PAIRS // 2
 LAST_SCALE_ROW = 32 * 3 + 3
-DIFFERENCE, PRODUCT = 0, 1
+LINE = 4
 
 
 def tile_list_sonobuoy_bearing_pairs_kernel(
@@ -31,7 +31,6 @@ def tile_list_sonobuoy_bearing_pairs_kernel(
     nc = tc.nc
     with ExitStack() as ctx:
         keep = ctx.enter_context(tc.tile_pool(name="keep", bufs=1))
-        ring = ctx.enter_context(tc.tile_pool(name="ring", bufs=2))
         psum = ctx.enter_context(tc.psum_pool(name="psum", bufs=1))
 
         def sb(shape, dtype, name, tag=None):
@@ -56,9 +55,9 @@ def tile_list_sonobuoy_bearing_pairs_kernel(
                     in_=scales[:, 4 * quadrant : 4 * quadrant + 4, :].bitcast(I32),
                 )
 
-        def second_pass_scales(target, both):
+        def second_pass_scales(queue, target, both):
             rows = LAST_SCALE_ROW + 1
-            nc.gpsimd.dma_start(out=target[0:rows, :].bitcast(I32), in_=both[4 : 4 + rows, :].bitcast(I32))
+            queue.dma_start(out=target[0:rows, :].bitcast(I32), in_=both[4 : 4 + rows, :].bitcast(I32))
 
         base_rows = base.rearrange("(p i) t -> p i t", i=PACK)
         xs_rows = xs.rearrange("(p i) j -> p i j", i=PACK)
@@ -137,7 +136,7 @@ def tile_list_sonobuoy_bearing_pairs_kernel(
 
         v_sc0 = sb([P, PAIRS], U8, "v_sc0")
         nc.vector.tensor_copy(v_sc0[:], tab_sc[:].indirect(idx[:]))
-        second_pass_scales(v_sc1, v_sc0)
+        second_pass_scales(nc.gpsimd, v_sc1, v_sc0)
         v_sc = (v_sc0, v_sc1)
 
         wb_sc0 = sb([P, H], U8, "wb_sc0")
@@ -145,14 +144,17 @@ def tile_list_sonobuoy_bearing_pairs_kernel(
             out=wb_sc0[:].rearrange("p (g t c) -> p g t c", g=2, t=PACK),
             in_=wb_sc_raw[:].rearrange("p (g c t) -> p g t c", g=2, t=PACK),
         )
-        second_pass_scales(wb_sc1, wb_sc0)
+        second_pass_scales(nc.gpsimd, wb_sc1, wb_sc0)
         wb_sc = (wb_sc0, wb_sc1)
 
         page_codes, page_sc = [], []
         for h in range(2):
             round_page_rows(PACK - 1, h)
             page_bf = sb([P, PASS, 2], F32, f"page_bf{h}")
-            nc.scalar.copy(out=page_bf[:], in_=page_pairs[h][:].rearrange("p w c -> p c w"))
+            nc.scalar.copy(
+                out=page_bf[:].rearrange("p (c e) w -> p c w e", e=LINE),
+                in_=page_pairs[h][:].rearrange("p w (c e) -> p c w e", e=LINE),
+            )
             codes = sb([P, PASS], U32, f"page_codes{h}")
             scales = sb([P, PASS], U8, f"page_sc{h}")
             nc.vector.quantize_mx(
@@ -172,35 +174,39 @@ def tile_list_sonobuoy_bearing_pairs_kernel(
             in_=wb_raw[:].rearrange("p a c -> p (a c)").rearrange("p (ag c e t) -> p ag c t e", ag=4, t=PACK, e=8),
         )
 
-        wp_codes, wp_sc = [], []
+        def quantise(name, source, scales):
+            codes = sb([P, scales.shape[1]], U32, name)
+            nc.vector.quantize_mx(out=codes[:].bitcast(FP8X4), scales=scales, in_=source)
+            return codes, scales
 
-        def quantise_wp(g):
-            wp_bf = sb([P, N * PACK], BF16, f"wp_bf{g}")
-            nc.scalar.copy(
-                out=wp_bf[:].rearrange("p (c e i) -> p c i e", e=2, i=PACK),
-                in_=wp_raw[g][:].rearrange("p i (c e) -> p c i e", e=2),
-            )
-            codes = sb([P, N], U32, f"wp_codes{g}")
-            scales = sb([P, N], U8, f"wp_sc{g}")
-            nc.vector.quantize_mx(out=codes[:].bitcast(FP8X4), scales=scales[:], in_=wp_bf[:])
-            wp_codes.append(codes)
-            wp_sc.append(scales)
+        def wp_views(g, tag):
+            wp_bf = sb([P, N * PACK], BF16, f"wp_bf{g}", tag=tag)
+            rounded = wp_bf[:].rearrange("p (c e i) -> p c i e", e=LINE, i=PACK)
+            return wp_bf, rounded, wp_raw[g][:].rearrange("p i (c e) -> p c i e", e=LINE)
 
-        y_half = [psum.tile([P, 2, HALF], F32, name=f"y_half{w}") for w in range(2)]
-        y_quarter = [psum.tile([P, N // P, P], F32, name=f"y_quarter{c}") for c in range(2)]
+        wp_bf0 = sb([P, N * PACK], BF16, "wp_bf0", tag="page_bf1")
+        nc.gpsimd.tensor_scalar(
+            out=wp_bf0[:].rearrange("p (c i) -> p c i", i=PACK),
+            in0=wp_raw[0][:].rearrange("p i c -> p c i"),
+            scalar1=1.0,
+            scalar2=0.0,
+            op0=ALU.mult,
+            op1=ALU.add,
+        )
+
+        def bank(name, shape, number):
+            return psum.tile(shape, F32, name=name, tag=f"bank{number}")
+
         out_rows = out.rearrange("(u p) j -> p u j", p=P)
         at = [sb([P, PACK, PAIRS], F32, f"at{g}") for g in range(2)]
-        x_bf = {}
-        for g in range(2):
-            for h in range(2):
-                for kind in (DIFFERENCE, PRODUCT):
-                    x_bf[g, h, kind] = sb([P, HALF * PACK], BF16, f"x_bf{g}{h}{kind}")
+        walk_in = "p t (c e) -> p c t e"
+        walk_out = "p (c e t) -> p c t e"
 
         def project_page(g, t):
-            a_sb = ring.tile([P, T2], F32, name="a_sb", bufs=6, align_bytes=64)
+            a_sb = sb([P, T2], F32, f"a_sb{PACK * g + t}")
             rows = slice(PASS * g + P * t, PASS * g + P * (t + 1))
             for h in range(2):
-                a_bank = psum.tile([P, PASS], F32, name="a_bank", tag="a_bank", bufs=2)
+                a_bank = bank(f"a_bank{g}{t}{h}", [P, PASS], h)
                 nc.tensor.matmul_mx(
                     out=a_bank[:],
                     lhsT=wa_codes[:, rows].bitcast(FP8X4),
@@ -213,11 +219,11 @@ def tile_list_sonobuoy_bearing_pairs_kernel(
                 nc.scalar.copy(out=a_sb[:, PASS * h : PASS * (h + 1)], in_=a_bank[:])
             nc.vector.tensor_copy(at[g][:, t, :], a_sb[:].indirect(idx3[:]))
 
-        def compare(g, quarter):
-            h, c = divmod(quarter, 2)
+        b_banks, cal_b = {}, {}
+
+        def project_table(g, quarter, number):
             cols = slice(P * quarter, P * (quarter + 1))
-            tag = "a_bank" if (g == 1 and h == 0) else "b_bank"
-            b_bank = psum.tile([P, PACK, P], F32, name="b_bank", tag=tag, bufs=2)
+            b_bank = bank(f"b_bank{g}{quarter}", [P, PACK, P], number)
             for t in range(PACK):
                 r0 = PASS * g + P * t
                 for a in range(2):
@@ -230,53 +236,65 @@ def tile_list_sonobuoy_bearing_pairs_kernel(
                         start=(a == 0),
                         stop=(a == 1),
                     )
-            cal_b = ring.tile([P, PACK, P], F32, name="cal_b", bufs=4, align_bytes=64)
+            scaled = sb([P, PACK, P], F32, f"cal_b{g}{quarter}")
             for t in range(PACK):
                 nc.scalar.activation(
-                    out=cal_b[:, t, :], in_=b_bank[:, t, :], func=ACT.Copy, scale=cal_sb[:, g, t : t + 1]
+                    out=scaled[:, t, :], in_=b_bank[:, t, :], func=ACT.Copy, scale=cal_sb[:, g, t : t + 1]
                 )
-            walk_in = "p t (c e) -> p c t e"
-            walk_out = "p (c e t) -> p c t e"
-            at_part = at[g][:, :, cols].rearrange(walk_in, e=4)
-            x_cols = slice(PASS * c, PASS * (c + 1))
-            nc.vector.tensor_tensor(
-                out=x_bf[g, h, PRODUCT][:, x_cols].rearrange(walk_out, e=4, t=PACK),
-                in0=b_bank[:].rearrange(walk_in, e=4),
-                in1=at_part,
-                op=ALU.mult,
-            )
-            engine = nc.vector if (g == 1 and h == 1) else nc.gpsimd
+            b_banks[g, quarter], cal_b[g, quarter] = b_bank, scaled
+
+        x1_bf = [sb([P, PAIRS * PACK], BF16, f"x1_bf{g}") for g in range(2)]
+        x2_bf = [sb([P, PAIRS * PACK], BF16, f"x2_bf{g}") for g in range(2)]
+
+        def compare(engine, x_bf, g, quarter, first, second, op):
             engine.tensor_tensor(
-                out=x_bf[g, h, DIFFERENCE][:, x_cols].rearrange(walk_out, e=4, t=PACK),
-                in0=at_part,
-                in1=cal_b[:].rearrange(walk_in, e=4),
-                op=ALU.subtract,
+                out=x_bf[g][:, PASS * quarter : PASS * (quarter + 1)].rearrange(walk_out, e=LINE, t=PACK),
+                in0=first.rearrange(walk_in, e=LINE),
+                in1=second.rearrange(walk_in, e=LINE),
+                op=op,
             )
 
-        def quantise_x(g, h, kind, cols):
-            width = cols.stop - cols.start
-            name = f"{g}{h}{kind}{cols.start}"
-            codes = sb([P, width], U32, "x_codes" + name)
-            scales = sb([P, width], U8, "x_sc" + name)
-            nc.vector.quantize_mx(
-                out=codes[:].bitcast(FP8X4),
-                scales=scales[:],
-                in_=x_bf[g, h, kind][:, PACK * cols.start : PACK * cols.stop],
-            )
-            return codes, scales
+        def product(g, quarter):
+            picked = at[g][:, :, P * quarter : P * (quarter + 1)]
+            compare(nc.vector, x1_bf, g, quarter, b_banks[g, quarter][:], picked, ALU.mult)
 
-        def accumulate(targets, g, kind, x, cols, first, last):
+        def difference(engine, g, quarter):
+            picked = at[g][:, :, P * quarter : P * (quarter + 1)]
+            compare(engine, x2_bf, g, quarter, picked, cal_b[g, quarter][:], ALU.subtract)
+
+        for t in range(PACK):
+            project_page(0, t)
+        for quarter in range(4):
+            project_table(0, quarter, 2 + quarter)
+            difference(nc.gpsimd, 0, quarter)
+            if quarter < 2:
+                project_page(1, quarter)
+        for quarter in range(4):
+            product(0, quarter)
+        project_page(1, 2)
+
+        early_sc = sb([P, 3, PAIRS], U8, "early_sc", tag="a_sb6")
+        wp_0 = quantise("wp_codes0", wp_bf0[:], early_sc[:, 0, :])
+        x1_0 = quantise("x1_codes0", x1_bf[0][:], early_sc[:, 1, :])
+        x2_0 = quantise("x2_codes0", x2_bf[0][:], early_sc[:, 2, :])
+        project_page(1, 3)
+        for quarter, number in enumerate((6, 7, 2, 3)):
+            project_table(1, quarter, number)
+        wp_bf1, rounded, raw = wp_views(1, "a_sb5")
+        nc.scalar.copy(out=rounded, in_=raw)
+
+        y_half = [bank(f"y_half{w}", [P, 2, HALF], 4 + w) for w in range(2)]
+        y_quarter = [bank(f"y_quarter{c}", [P, N // P, P], c) for c in range(2)]
+
+        def accumulate(targets, weights, x, cols, first, last):
+            w_codes, w_sc = weights
             codes, scales = x
             for u, (target, opens, closes) in enumerate(targets):
                 n_cols = slice(P * u, P * (u + 1))
-                if kind == PRODUCT:
-                    w_codes, w_sc = wp_codes[g][:, n_cols], wp_sc[g][:, n_cols]
-                else:
-                    w_codes, w_sc = wd_w[:, g, n_cols], wd_sc[4 * g : P, n_cols]
                 nc.tensor.matmul_mx(
                     out=target,
-                    lhsT=w_codes.bitcast(FP8X4),
-                    lhsT_scale=w_sc,
+                    lhsT=w_codes[:, n_cols].bitcast(FP8X4),
+                    lhsT_scale=w_sc[:, n_cols],
                     rhs=codes[:, cols].bitcast(FP8X4),
                     rhs_scale=scales[:, cols],
                     start=(first and opens),
@@ -285,50 +303,42 @@ def tile_list_sonobuoy_bearing_pairs_kernel(
 
         half_targets = [(y_half[u // 2][:, u % 2, :], u % 2 == 0, u % 2 == 1) for u in range(4)]
         quarter_targets = [[(y_quarter[c][:, u, :], u == 0, u == 3) for u in range(4)] for c in range(2)]
-        whole = slice(0, HALF)
-        parts = [slice(0, P), slice(P, 2 * P)]
+        first_half = slice(0, HALF)
+        wd_pass = [(wd_w[:, g, :], wd_sc[4 * g : P, :]) for g in range(2)]
 
         def add_bias(result, target, u):
             nc.scalar.activation(out=result, in_=target, func=ACT.Identity, bias=bo_sb[:, u : u + 1], scale=1.0)
 
-        x0 = {}
-        for t in range(PACK):
-            project_page(0, t)
-        project_page(1, 0)
-        project_page(1, 1)
-        compare(0, 0)
-        compare(0, 1)
-        for kind in (PRODUCT, DIFFERENCE):
-            x0[0, kind] = quantise_x(0, 0, kind, whole)
-        project_page(1, 2)
-        compare(0, 2)
-        project_page(1, 3)
-        compare(0, 3)
-        for kind in (PRODUCT, DIFFERENCE):
-            x0[1, kind] = quantise_x(0, 1, kind, whole)
-
-        compare(1, 0)
-        compare(1, 1)
-        quantise_wp(0)
-        quantise_wp(1)
-        for kind in (DIFFERENCE, PRODUCT):
-            accumulate(half_targets, 0, kind, x0[0, kind], whole, kind == DIFFERENCE, False)
-        for kind in (DIFFERENCE, PRODUCT):
+        for weights, x, first in ((wp_0, x1_0, True), (wd_pass[0], x2_0, False)):
+            accumulate(half_targets, weights, x, first_half, first, False)
             for c in range(2):
-                accumulate(quarter_targets[c], 0, kind, x0[1, kind], parts[c], kind == DIFFERENCE, False)
-        for kind in (PRODUCT, DIFFERENCE):
-            accumulate(half_targets, 1, kind, quantise_x(1, 0, kind, whole), whole, False, kind == DIFFERENCE)
+                accumulate(quarter_targets[c], weights, x, slice(HALF + P * c, HALF + P * (c + 1)), first, False)
+
+        for quarter in range(4):
+            if quarter < 2:
+                difference(nc.gpsimd, 1, quarter)
+            product(1, quarter)
+        late_sc = sb([P, 3, PAIRS], U8, "late_sc", tag="a_sb7")
+        wp_1 = quantise("wp_codes1", wp_bf1[:], late_sc[:, 0, :])
+        x1_1 = quantise("x1_codes1", x1_bf[1][:, 0 : HALF * PACK], late_sc[:, 1, first_half])
+        x2_1 = quantise("x2_codes1", x2_bf[1][:, 0 : HALF * PACK], late_sc[:, 2, first_half])
+        accumulate(half_targets, wp_1, x1_1, first_half, False, False)
+        accumulate(half_targets, wd_pass[1], x2_1, first_half, False, True)
         for w in range(2):
             result = sb([P, 2, HALF], F32, f"result_half{w}")
             for e in range(2):
                 add_bias(result[:, e, :], y_half[w][:, e, :], 2 * w + e)
-            nc.sync.dma_start(out=out_rows[:, 2 * w : 2 * w + 2, whole], in_=result[:])
+            nc.sync.dma_start(out=out_rows[:, 2 * w : 2 * w + 2, first_half], in_=result[:])
 
+        difference(nc.vector, 1, 2)
+        x1_rest = quantise("x1_codes1r", x1_bf[1][:, HALF * PACK :], late_sc[:, 1, HALF:])
+        difference(nc.vector, 1, 3)
         for c in range(2):
-            compare(1, 2 + c)
-            for kind in (PRODUCT, DIFFERENCE):
-                x = quantise_x(1, 1, kind, parts[c])
-                accumulate(quarter_targets[c], 1, kind, x, parts[0], False, kind == DIFFERENCE)
+            accumulate(quarter_targets[c], wp_1, x1_rest, slice(P * c, P * (c + 1)), False, False)
+        for c in range(2):
+            cols = slice(HALF + P * c, HALF + P * (c + 1))
+            x2_q = quantise(f"x2_codes1q{c}", x2_bf[1][:, PACK * cols.start : PACK * cols.stop], late_sc[:, 2, cols])
+            accumulate(quarter_targets[c], wd_pass[1], x2_q, slice(0, P), False, True)
             result = sb([P, N // P, P], F32, f"result_quarter{c}")
             if c == 0:
                 for u in range(N // P):
@@ -336,4 +346,4 @@ def tile_list_sonobuoy_bearing_pairs_kernel(
             else:
                 bias = bo_sb[:].unsqueeze(2).to_broadcast([P, N // P, P])
                 nc.vector.tensor_tensor(out=result[:], in0=y_quarter[c][:], in1=bias, op=ALU.add)
-            nc.sync.dma_start(out=out_rows[:, :, HALF + P * c : HALF + P * (c + 1)], in_=result[:])
+            nc.sync.dma_start(out=out_rows[:, :, cols], in_=result[:])

@@ -43,9 +43,8 @@ def tile_list_sonobuoy_bearing_pairs_kernel(
         tab_sc = sb([P, T], U8, "tab_sc")
         wb_sc_raw = sb([P, H], U8, "wb_sc_raw")
         wd_sc = sb([P, N], U8, "wd_sc")
-        v_sc1 = sb([P, PAIRS], U8, "v_sc1")
         wb_sc1 = sb([P, H], U8, "wb_sc1")
-        for scale_tile in (tab_sc, wb_sc_raw, wd_sc, v_sc1, wb_sc1):
+        for scale_tile in (tab_sc, wb_sc_raw, wd_sc, wb_sc1):
             nc.vector.memset(scale_tile[:].bitcast(I32), 0)
 
         def load_scales(scale_tile, scales):
@@ -128,16 +127,8 @@ def tile_list_sonobuoy_bearing_pairs_kernel(
                 for h in range(2):
                     round_page_rows(i, h)
 
-        wa_codes = sb([P, H], U32, "wa_codes", tag=f"incoming{PACK - 1}")
-        wa_sc = sb([P, H], U8, "wa_sc")
-        nc.vector.quantize_mx(
-            out=wa_codes[:].bitcast(FP8X4), scales=wa_sc[:], in_=wa_bf[:].rearrange("p g t c i -> p (g t c i)")
-        )
-
         v_sc0 = sb([P, PAIRS], U8, "v_sc0")
         nc.vector.tensor_copy(v_sc0[:], tab_sc[:].indirect(idx[:]))
-        second_pass_scales(nc.gpsimd, v_sc1, v_sc0)
-        v_sc = (v_sc0, v_sc1)
 
         wb_sc0 = sb([P, H], U8, "wb_sc0")
         nc.gpsimd.tensor_copy(
@@ -147,32 +138,42 @@ def tile_list_sonobuoy_bearing_pairs_kernel(
         second_pass_scales(nc.gpsimd, wb_sc1, wb_sc0)
         wb_sc = (wb_sc0, wb_sc1)
 
+        v_w = [sb([P, PAIRS], U32, f"v_w{a}") for a in range(2)]
+        nc.vector.tensor_copy(v_w[0][:], tab_w[0][:].bitcast(U32).indirect(idx[:]))
+
+        first_codes = sb([P, H + T2], U32, "first_codes", tag="tab_w0")
+        wa_codes = first_codes[:, 0:H]
+        wa_sc = sb([P, H], U8, "wa_sc")
+        nc.vector.quantize_mx(
+            out=wa_codes.bitcast(FP8X4), scales=wa_sc[:], in_=wa_bf[:].rearrange("p g t c i -> p (g t c i)")
+        )
+
         page_codes, page_sc = [], []
         for h in range(2):
             round_page_rows(PACK - 1, h)
             page_bf = sb([P, PASS, 2], F32, f"page_bf{h}")
-            nc.scalar.copy(
-                out=page_bf[:].rearrange("p (c e) w -> p c w e", e=LINE),
-                in_=page_pairs[h][:].rearrange("p w (c e) -> p c w e", e=LINE),
-            )
-            codes = sb([P, PASS], U32, f"page_codes{h}")
+            nc.scalar.copy(out=page_bf[:], in_=page_pairs[h][:].rearrange("p w c -> p c w"))
+            codes = first_codes[:, H + PASS * h : H + PASS * (h + 1)]
             scales = sb([P, PASS], U8, f"page_sc{h}")
             nc.vector.quantize_mx(
-                out=codes[:].bitcast(FP8X4),
+                out=codes.bitcast(FP8X4),
                 scales=scales[:],
                 in_=page_bf[:].rearrange("p c w -> p (c w)").bitcast(BF16),
             )
             page_codes.append(codes)
             page_sc.append(scales)
 
-        v_w = [sb([P, PAIRS], U32, "v_w0", tag="page_bf0"), sb([P, PAIRS], U32, "v_w1")]
-        for a in range(2):
-            nc.vector.tensor_copy(v_w[a][:], tab_w[a][:].bitcast(U32).indirect(idx[:]))
+        nc.vector.tensor_copy(v_w[1][:], tab_w[1][:].bitcast(U32).indirect(idx[:]))
         wb_w = sb([P, 2, H], U16, "wb_w")
         nc.gpsimd.tensor_copy(
             out=wb_w[:].rearrange("p a c -> p (a c)").rearrange("p (ag t c e) -> p ag c t e", ag=4, t=PACK, e=8),
             in_=wb_raw[:].rearrange("p a c -> p (a c)").rearrange("p (ag c e t) -> p ag c t e", ag=4, t=PACK, e=8),
         )
+
+        v_sc1 = sb([P, PAIRS], U8, "v_sc1", tag="wb_raw")
+        nc.gpsimd.memset(v_sc1[:].bitcast(I32), 0)
+        second_pass_scales(nc.gpsimd, v_sc1, v_sc0)
+        v_sc = (v_sc0, v_sc1)
 
         def quantise(name, source, scales):
             codes = sb([P, scales.shape[1]], U32, name)
@@ -206,12 +207,12 @@ def tile_list_sonobuoy_bearing_pairs_kernel(
             a_sb = sb([P, T2], F32, f"a_sb{PACK * g + t}")
             rows = slice(PASS * g + P * t, PASS * g + P * (t + 1))
             for h in range(2):
-                a_bank = bank(f"a_bank{g}{t}{h}", [P, PASS], h)
+                a_bank = bank(f"a_bank{g}{t}{h}", [P, PASS], h + (6 if g == 0 and t % 2 else 0))
                 nc.tensor.matmul_mx(
                     out=a_bank[:],
                     lhsT=wa_codes[:, rows].bitcast(FP8X4),
                     lhsT_scale=wa_sc[:, rows],
-                    rhs=page_codes[h][:].bitcast(FP8X4),
+                    rhs=page_codes[h].bitcast(FP8X4),
                     rhs_scale=page_sc[h][:],
                     start=True,
                     stop=True,
@@ -224,17 +225,17 @@ def tile_list_sonobuoy_bearing_pairs_kernel(
         def project_table(g, quarter, number):
             cols = slice(P * quarter, P * (quarter + 1))
             b_bank = bank(f"b_bank{g}{quarter}", [P, PACK, P], number)
-            for t in range(PACK):
-                r0 = PASS * g + P * t
-                for a in range(2):
+            for a in range(2):
+                for t in range(PACK):
+                    r0 = PASS * g + P * t
                     nc.tensor.matmul_mx(
                         out=b_bank[:, t, :],
                         lhsT=wb_w[:, a, r0 : r0 + P].bitcast(FP4X4),
                         lhsT_scale=wb_sc[a][:, r0 : r0 + P],
                         rhs=v_w[a][:, cols].bitcast(FP8X4),
                         rhs_scale=v_sc[a][:, cols],
-                        start=(a == 0),
-                        stop=(a == 1),
+                        start=(a == 0 and t == 0),
+                        stop=(a == 1 and t == PACK - 1),
                     )
             scaled = sb([P, PACK, P], F32, f"cal_b{g}{quarter}")
             for t in range(PACK):

@@ -244,25 +244,31 @@ def tile_list_sonobuoy_bearing_pairs_kernel(
                 )
             b_banks[g, quarter], cal_b[g, quarter] = b_bank, scaled
 
-        x1_bf = [sb([P, PAIRS * PACK], BF16, f"x1_bf{g}") for g in range(2)]
-        x2_bf = [sb([P, PAIRS * PACK], BF16, f"x2_bf{g}") for g in range(2)]
+        x_bf = {}
 
-        def compare(engine, x_bf, g, quarter, first, second, op):
+        def compare(engine, kind, g, quarter, first, second, op):
             engine.tensor_tensor(
-                out=x_bf[g][:, PASS * quarter : PASS * (quarter + 1)].rearrange(walk_out, e=LINE, t=PACK),
+                out=x_bf[kind, g, quarter].rearrange(walk_out, e=LINE, t=PACK),
                 in0=first.rearrange(walk_in, e=LINE),
                 in1=second.rearrange(walk_in, e=LINE),
                 op=op,
             )
 
+        def values_tile(name, pieces, tag):
+            tile = sb([P, PASS * len(pieces)], BF16, name, tag=tag)
+            for place, piece in enumerate(pieces):
+                x_bf[piece] = tile[:, PASS * place : PASS * (place + 1)]
+            return tile
+
         def product(g, quarter):
             picked = at[g][:, :, P * quarter : P * (quarter + 1)]
-            compare(nc.vector, x1_bf, g, quarter, b_banks[g, quarter][:], picked, ALU.mult)
+            compare(nc.vector, 1, g, quarter, b_banks[g, quarter][:], picked, ALU.mult)
 
         def difference(engine, g, quarter):
             picked = at[g][:, :, P * quarter : P * (quarter + 1)]
-            compare(engine, x2_bf, g, quarter, picked, cal_b[g, quarter][:], ALU.subtract)
+            compare(engine, 2, g, quarter, picked, cal_b[g, quarter][:], ALU.subtract)
 
+        early_bf = values_tile("early_bf", [(2, 0, q) for q in range(4)] + [(1, 0, q) for q in range(2)], "x_bf")
         for t in range(PACK):
             project_page(0, t)
         for quarter in range(4):
@@ -270,22 +276,29 @@ def tile_list_sonobuoy_bearing_pairs_kernel(
             difference(nc.gpsimd, 0, quarter)
             if quarter < 2:
                 project_page(1, quarter)
-        for quarter in range(4):
+        for quarter in range(2):
             product(0, quarter)
         project_page(1, 2)
-
-        early_sc = sb([P, 3, PAIRS], U8, "early_sc", tag="a_sb6")
-        wp_0 = quantise("wp_codes0", wp_bf0[:], early_sc[:, 0, :])
-        x1_0 = quantise("x1_codes0", x1_bf[0][:], early_sc[:, 1, :])
-        x2_0 = quantise("x2_codes0", x2_bf[0][:], early_sc[:, 2, :])
         project_page(1, 3)
         for quarter, number in enumerate((6, 7, 2, 3)):
             project_table(1, quarter, number)
         wp_bf1, rounded, raw = wp_views(1, "a_sb5")
         nc.scalar.copy(out=rounded, in_=raw)
 
-        y_half = [bank(f"y_half{w}", [P, 2, HALF], 4 + w) for w in range(2)]
-        y_quarter = [bank(f"y_quarter{c}", [P, N // P, P], c) for c in range(2)]
+        early_sc = sb([P, 3, PAIRS], U8, "early_sc", tag="a_sb7")
+        wp_0 = quantise("wp_codes0", wp_bf0[:], early_sc[:, 0, :])
+        x1_0 = quantise("x1_codes0", early_bf[:, 4 * PASS :], early_sc[:, 1, 0:HALF])
+        x2_0 = quantise("x2_codes0", early_bf[:, 0 : 4 * PASS], early_sc[:, 2, :])
+
+        late_pieces = [(1, 1, 0), (1, 1, 1), (1, 0, 2), (1, 0, 3), (2, 1, 0), (2, 1, 1)]
+        late_bf = values_tile("late_bf", late_pieces, "x_bf")
+        for quarter in range(2):
+            difference(nc.gpsimd, 1, quarter)
+        for kind, g, quarter in late_pieces[:4]:
+            product(g, quarter)
+
+        y_half = [bank(f"y_half{w}", [P, 2, HALF], w) for w in range(2)]
+        y_quarter = [bank(f"y_quarter{c}", [P, N // P, P], 6 + c) for c in range(2)]
 
         def accumulate(targets, weights, x, cols, first, last):
             w_codes, w_sc = weights
@@ -310,36 +323,39 @@ def tile_list_sonobuoy_bearing_pairs_kernel(
         def add_bias(result, target, u):
             nc.scalar.activation(out=result, in_=target, func=ACT.Identity, bias=bo_sb[:, u : u + 1], scale=1.0)
 
-        for weights, x, first in ((wp_0, x1_0, True), (wd_pass[0], x2_0, False)):
-            accumulate(half_targets, weights, x, first_half, first, False)
-            for c in range(2):
-                accumulate(quarter_targets[c], weights, x, slice(HALF + P * c, HALF + P * (c + 1)), first, False)
+        accumulate(half_targets, wp_0, x1_0, first_half, True, False)
+        accumulate(half_targets, wd_pass[0], x2_0, first_half, False, False)
+        for c in range(2):
+            accumulate(quarter_targets[c], wd_pass[0], x2_0, slice(HALF + P * c, HALF + P * (c + 1)), True, False)
 
-        for quarter in range(4):
-            if quarter < 2:
-                difference(nc.gpsimd, 1, quarter)
-            product(1, quarter)
-        late_sc = sb([P, 3, PAIRS], U8, "late_sc", tag="a_sb7")
+        late_sc = sb([P, 4, PAIRS], U8, "late_sc", tag="cal_b11")
         wp_1 = quantise("wp_codes1", wp_bf1[:], late_sc[:, 0, :])
-        x1_1 = quantise("x1_codes1", x1_bf[1][:, 0 : HALF * PACK], late_sc[:, 1, first_half])
-        x2_1 = quantise("x2_codes1", x2_bf[1][:, 0 : HALF * PACK], late_sc[:, 2, first_half])
-        accumulate(half_targets, wp_1, x1_1, first_half, False, False)
-        accumulate(half_targets, wd_pass[1], x2_1, first_half, False, True)
+        x2_1 = quantise("x2_codes1", late_bf[:, 4 * PASS : 6 * PASS], late_sc[:, 2, first_half])
+        x1_mixed = quantise("x1_codes1", late_bf[:, 0 : 4 * PASS], late_sc[:, 1, :])
+        accumulate(half_targets, wd_pass[1], x2_1, first_half, False, False)
+        accumulate(half_targets, wp_1, x1_mixed, first_half, False, True)
         for w in range(2):
             result = sb([P, 2, HALF], F32, f"result_half{w}")
             for e in range(2):
                 add_bias(result[:, e, :], y_half[w][:, e, :], 2 * w + e)
             nc.sync.dma_start(out=out_rows[:, 2 * w : 2 * w + 2, first_half], in_=result[:])
-
-        difference(nc.vector, 1, 2)
-        x1_rest = quantise("x1_codes1r", x1_bf[1][:, HALF * PACK :], late_sc[:, 1, HALF:])
-        difference(nc.vector, 1, 3)
         for c in range(2):
-            accumulate(quarter_targets[c], wp_1, x1_rest, slice(P * c, P * (c + 1)), False, False)
+            accumulate(quarter_targets[c], wp_0, x1_mixed, slice(HALF + P * c, HALF + P * (c + 1)), False, False)
+
+        last_bf = values_tile("last_bf", [(1, 1, 2), (2, 1, 2), (1, 1, 3), (2, 1, 3)], "a_sb5")
+        product(1, 2)
+        difference(nc.vector, 1, 2)
+        product(1, 3)
+        three = quantise("x_codes_three", last_bf[:, 0 : 2 * PASS], late_sc[:, 3, 0:HALF])
+        x1_last = quantise("x1_codes_last", last_bf[:, 2 * PASS : 3 * PASS], late_sc[:, 3, HALF : HALF + P])
+        difference(nc.vector, 1, 3)
+        x2_last = quantise("x2_codes_last", last_bf[:, 3 * PASS :], late_sc[:, 3, HALF + P :])
+        accumulate(quarter_targets[0], wp_1, three, slice(0, P), False, False)
+        accumulate(quarter_targets[0], wd_pass[1], three, slice(P, 2 * P), False, True)
+        accumulate(quarter_targets[1], wp_1, x1_last, slice(0, P), False, False)
+        accumulate(quarter_targets[1], wd_pass[1], x2_last, slice(0, P), False, True)
         for c in range(2):
             cols = slice(HALF + P * c, HALF + P * (c + 1))
-            x2_q = quantise(f"x2_codes1q{c}", x2_bf[1][:, PACK * cols.start : PACK * cols.stop], late_sc[:, 2, cols])
-            accumulate(quarter_targets[c], wd_pass[1], x2_q, slice(0, P), False, True)
             result = sb([P, N // P, P], F32, f"result_quarter{c}")
             if c == 0:
                 for u in range(N // P):

@@ -180,10 +180,14 @@ def tile_list_sonobuoy_bearing_pairs_kernel(
             nc.vector.quantize_mx(out=codes[:].bitcast(FP8X4), scales=scales, in_=source)
             return codes, scales
 
-        def wp_views(g, tag):
-            wp_bf = sb([P, N * PACK], BF16, f"wp_bf{g}", tag=tag)
-            rounded = wp_bf[:].rearrange("p (c e i) -> p c i e", e=LINE, i=PACK)
-            return wp_bf, rounded, wp_raw[g][:].rearrange("p i (c e) -> p c i e", e=LINE)
+        def round_wp_piece(part, tag):
+            cols = slice(HALF * part, HALF * (part + 1))
+            wp_bf = sb([P, HALF * PACK], BF16, f"wp_bf1{part}", tag=tag)
+            nc.scalar.copy(
+                out=wp_bf[:].rearrange("p (c e i) -> p c i e", e=2, i=PACK),
+                in_=wp_raw[1][:, :, cols].rearrange("p i (c e) -> p c i e", e=2),
+            )
+            return wp_bf
 
         wp_bf0 = sb([P, N * PACK], BF16, "wp_bf0", tag="page_bf1")
         nc.gpsimd.tensor_scalar(
@@ -203,8 +207,8 @@ def tile_list_sonobuoy_bearing_pairs_kernel(
         walk_in = "p t (c e) -> p c t e"
         walk_out = "p (c e t) -> p c t e"
 
-        def project_page(g, t):
-            a_sb = sb([P, T2], F32, f"a_sb{PACK * g + t}")
+        def project_page(g, t, tag=None):
+            a_sb = sb([P, T2], F32, f"a_sb{PACK * g + t}", tag=tag)
             rows = slice(PASS * g + P * t, PASS * g + P * (t + 1))
             for h in range(2):
                 a_bank = bank(f"a_bank{g}{t}{h}", [P, PASS], h + (6 if g == 0 and t % 2 else 0))
@@ -266,39 +270,44 @@ def tile_list_sonobuoy_bearing_pairs_kernel(
 
         def difference(engine, g, quarter):
             picked = at[g][:, :, P * quarter : P * (quarter + 1)]
-            compare(engine, 2, g, quarter, picked, cal_b[g, quarter][:], ALU.subtract)
+            if engine is nc.vector:
+                compare(engine, 2, g, quarter, picked, cal_b[g, quarter][:], ALU.subtract)
+            else:
+                engine.tensor_tensor(
+                    out=x_bf[2, g, quarter].rearrange("p (c t) -> p c t", t=PACK),
+                    in0=picked.rearrange("p t c -> p c t"),
+                    in1=cal_b[g, quarter][:].rearrange("p t c -> p c t"),
+                    op=ALU.subtract,
+                )
 
-        early_bf = values_tile("early_bf", [(2, 0, q) for q in range(4)] + [(1, 0, q) for q in range(2)], "x_bf")
+        def half_tile(g, h):
+            return values_tile(f"x_bf{g}{h}", [(kind, g, 2 * h + c) for kind in (1, 2) for c in range(2)], "x_bf")
+
+        bf_0 = values_tile("x_bf0", [(kind, 0, q) for kind in (1, 2) for q in range(4)], "x_bf")
         for t in range(PACK):
             project_page(0, t)
         for quarter in range(4):
             project_table(0, quarter, 2 + quarter)
             difference(nc.gpsimd, 0, quarter)
-            if quarter < 2:
-                project_page(1, quarter)
-        for quarter in range(2):
             product(0, quarter)
-        project_page(1, 2)
-        project_page(1, 3)
-        for quarter, number in enumerate((6, 7, 2, 3)):
+            project_page(1, quarter)
+        for quarter, number in enumerate((6, 7, 4, 5)):
             project_table(1, quarter, number)
-        wp_bf1, rounded, raw = wp_views(1, "a_sb5")
-        nc.scalar.copy(out=rounded, in_=raw)
+        wp_bf1 = [round_wp_piece(part, f"cal_b0{1 + part}") for part in range(2)]
+        early_sc = sb([P, 3 * PAIRS], U8, "early_sc", tag="a_sb7")
+        wp_0 = quantise("wp_codes0", wp_bf0[:], early_sc[:, 0:N])
+        x1_0 = quantise("x1_codes0", bf_0[:, 0 : 4 * PASS], early_sc[:, N : N + PAIRS])
+        x2_0 = quantise("x2_codes0", bf_0[:, 4 * PASS :], early_sc[:, N + PAIRS :])
 
-        early_sc = sb([P, 3, PAIRS], U8, "early_sc", tag="a_sb7")
-        wp_0 = quantise("wp_codes0", wp_bf0[:], early_sc[:, 0, :])
-        x1_0 = quantise("x1_codes0", early_bf[:, 4 * PASS :], early_sc[:, 1, 0:HALF])
-        x2_0 = quantise("x2_codes0", early_bf[:, 0 : 4 * PASS], early_sc[:, 2, :])
+        bf_10 = half_tile(1, 0)
+        last_bf = values_tile("last_bf", [(1, 1, 2), (2, 1, 2), (1, 1, 3), (2, 1, 3)], "page_bf1")
+        difference(nc.gpsimd, 1, 0)
+        for quarter in range(3):
+            product(1, quarter)
+        difference(nc.vector, 1, 1)
 
-        late_pieces = [(1, 1, 0), (1, 1, 1), (1, 0, 2), (1, 0, 3), (2, 1, 0), (2, 1, 1)]
-        late_bf = values_tile("late_bf", late_pieces, "x_bf")
-        for quarter in range(2):
-            difference(nc.gpsimd, 1, quarter)
-        for kind, g, quarter in late_pieces[:4]:
-            product(g, quarter)
-
-        y_half = [bank(f"y_half{w}", [P, 2, HALF], w) for w in range(2)]
-        y_quarter = [bank(f"y_quarter{c}", [P, N // P, P], 6 + c) for c in range(2)]
+        y_half = [bank(f"y_half{w}", [P, 2, HALF], 2 + w) for w in range(2)]
+        y_quarter = [bank(f"y_quarter{c}", [P, N // P, P], c) for c in range(2)]
 
         def accumulate(targets, weights, x, cols, first, last):
             w_codes, w_sc = weights
@@ -323,27 +332,26 @@ def tile_list_sonobuoy_bearing_pairs_kernel(
         def add_bias(result, target, u):
             nc.scalar.activation(out=result, in_=target, func=ACT.Identity, bias=bo_sb[:, u : u + 1], scale=1.0)
 
-        accumulate(half_targets, wp_0, x1_0, first_half, True, False)
-        accumulate(half_targets, wd_pass[0], x2_0, first_half, False, False)
-        for c in range(2):
-            accumulate(quarter_targets[c], wd_pass[0], x2_0, slice(HALF + P * c, HALF + P * (c + 1)), True, False)
+        second_half = slice(HALF, PAIRS)
+        for weights, x, first in ((wp_0, x1_0, True), (wd_pass[0], x2_0, False)):
+            accumulate(half_targets, weights, x, first_half, first, False)
+            for c in range(2):
+                accumulate(quarter_targets[c], weights, x, slice(HALF + P * c, HALF + P * (c + 1)), first, False)
 
-        late_sc = sb([P, 4, PAIRS], U8, "late_sc", tag="cal_b11")
-        wp_1 = quantise("wp_codes1", wp_bf1[:], late_sc[:, 0, :])
-        x2_1 = quantise("x2_codes1", late_bf[:, 4 * PASS : 6 * PASS], late_sc[:, 2, first_half])
-        x1_mixed = quantise("x1_codes1", late_bf[:, 0 : 4 * PASS], late_sc[:, 1, :])
-        accumulate(half_targets, wd_pass[1], x2_1, first_half, False, False)
-        accumulate(half_targets, wp_1, x1_mixed, first_half, False, True)
+        late_sc = sb([P, 4, PAIRS], U8, "late_sc", tag="cal_b10")
+        wp_codes1 = sb([P, N], U32, "wp_codes1")
+        for part in range(2):
+            cols = slice(HALF * part, HALF * (part + 1))
+            nc.vector.quantize_mx(out=wp_codes1[:, cols].bitcast(FP8X4), scales=late_sc[:, 0, cols], in_=wp_bf1[part][:])
+        wp_1 = (wp_codes1, late_sc[:, 0, :])
+        x_10 = quantise("x_codes10", bf_10[:], late_sc[:, 1, :])
+        accumulate(half_targets, wp_1, x_10, first_half, False, False)
+        accumulate(half_targets, wd_pass[1], x_10, second_half, False, True)
         for w in range(2):
             result = sb([P, 2, HALF], F32, f"result_half{w}")
             for e in range(2):
                 add_bias(result[:, e, :], y_half[w][:, e, :], 2 * w + e)
             nc.sync.dma_start(out=out_rows[:, 2 * w : 2 * w + 2, first_half], in_=result[:])
-        for c in range(2):
-            accumulate(quarter_targets[c], wp_0, x1_mixed, slice(HALF + P * c, HALF + P * (c + 1)), False, False)
-
-        last_bf = values_tile("last_bf", [(1, 1, 2), (2, 1, 2), (1, 1, 3), (2, 1, 3)], "a_sb5")
-        product(1, 2)
         difference(nc.vector, 1, 2)
         product(1, 3)
         three = quantise("x_codes_three", last_bf[:, 0 : 2 * PASS], late_sc[:, 3, 0:HALF])

@@ -270,15 +270,7 @@ def tile_list_sonobuoy_bearing_pairs_kernel(
 
         def difference(engine, g, quarter):
             picked = at[g][:, :, P * quarter : P * (quarter + 1)]
-            if engine is nc.vector:
-                compare(engine, 2, g, quarter, picked, cal_b[g, quarter][:], ALU.subtract)
-            else:
-                engine.tensor_tensor(
-                    out=x_bf[2, g, quarter].rearrange("p (c t) -> p c t", t=PACK),
-                    in0=picked.rearrange("p t c -> p c t"),
-                    in1=cal_b[g, quarter][:].rearrange("p t c -> p c t"),
-                    op=ALU.subtract,
-                )
+            compare(engine, 2, g, quarter, picked, cal_b[g, quarter][:], ALU.subtract)
 
         def half_tile(g, h):
             return values_tile(f"x_bf{g}{h}", [(kind, g, 2 * h + c) for kind in (1, 2) for c in range(2)], "x_bf")
@@ -307,7 +299,8 @@ def tile_list_sonobuoy_bearing_pairs_kernel(
         difference(nc.vector, 1, 1)
 
         y_half = [bank(f"y_half{w}", [P, 2, HALF], 2 + w) for w in range(2)]
-        y_quarter = [bank(f"y_quarter{c}", [P, N // P, P], c) for c in range(2)]
+        y_third = bank("y_third", [P, N // P, P], 0)
+        y_last = [bank(f"y_last{w}", [P, 2, P], number) for w, number in enumerate((1, 6))]
 
         def accumulate(targets, weights, x, cols, first, last):
             w_codes, w_sc = weights
@@ -325,7 +318,10 @@ def tile_list_sonobuoy_bearing_pairs_kernel(
                 )
 
         half_targets = [(y_half[u // 2][:, u % 2, :], u % 2 == 0, u % 2 == 1) for u in range(4)]
-        quarter_targets = [[(y_quarter[c][:, u, :], u == 0, u == 3) for u in range(4)] for c in range(2)]
+        quarter_targets = [
+            [(y_third[:, u, :], u == 0, u == 3) for u in range(4)],
+            [(y_last[u // 2][:, u % 2, :], u % 2 == 0, u % 2 == 1) for u in range(4)],
+        ]
         first_half = slice(0, HALF)
         wd_pass = [(wd_w[:, g, :], wd_sc[4 * g : P, :]) for g in range(2)]
 
@@ -362,13 +358,16 @@ def tile_list_sonobuoy_bearing_pairs_kernel(
         accumulate(quarter_targets[0], wd_pass[1], three, slice(P, 2 * P), False, True)
         accumulate(quarter_targets[1], wp_1, x1_last, slice(0, P), False, False)
         accumulate(quarter_targets[1], wd_pass[1], x2_last, slice(0, P), False, True)
-        for c in range(2):
-            cols = slice(HALF + P * c, HALF + P * (c + 1))
-            result = sb([P, N // P, P], F32, f"result_quarter{c}")
-            if c == 0:
-                for u in range(N // P):
-                    add_bias(result[:, u, :], y_quarter[c][:, u, :], u)
+        result = sb([P, N // P, P], F32, "result_third")
+        for u in range(N // P):
+            add_bias(result[:, u, :], y_third[:, u, :], u)
+        nc.sync.dma_start(out=out_rows[:, :, HALF : HALF + P], in_=result[:])
+        for w in range(2):
+            result = sb([P, 2, P], F32, f"result_last{w}")
+            if w == 0:
+                bias = bo_sb[:, 0:2].unsqueeze(2).to_broadcast([P, 2, P])
+                nc.vector.tensor_tensor(out=result[:], in0=y_last[0][:], in1=bias, op=ALU.add)
             else:
-                bias = bo_sb[:].unsqueeze(2).to_broadcast([P, N // P, P])
-                nc.vector.tensor_tensor(out=result[:], in0=y_quarter[c][:], in1=bias, op=ALU.add)
-            nc.sync.dma_start(out=out_rows[:, :, cols], in_=result[:])
+                for e in range(2):
+                    add_bias(result[:, e, :], y_last[1][:, e, :], 2 + e)
+            nc.sync.dma_start(out=out_rows[:, 2 * w : 2 * w + 2, HALF + P :], in_=result[:])

@@ -241,12 +241,17 @@ def tile_list_sonobuoy_bearing_pairs_kernel(
                         start=(a == 0 and t == 0),
                         stop=(a == 1 and t == PACK - 1),
                     )
-            scaled = sb([P, PACK, P], F32, f"cal_b{g}{quarter}")
-            for t in range(PACK):
-                nc.scalar.activation(
-                    out=scaled[:, t, :], in_=b_bank[:, t, :], func=ACT.Copy, scale=cal_sb[:, g, t : t + 1]
-                )
-            b_banks[g, quarter], cal_b[g, quarter] = b_bank, scaled
+            b_banks[g, quarter] = b_bank
+
+        def calibrate(g, h, tiles, quarters):
+            for c in quarters:
+                for t in tiles:
+                    nc.scalar.activation(
+                        out=cal_b[g, 2 * h + c][:, t, :],
+                        in_=b_banks[g, 2 * h + c][:, t, :],
+                        func=ACT.Copy,
+                        scale=cal_sb[:, g, t : t + 1],
+                    )
 
         x_bf = {}
 
@@ -268,39 +273,60 @@ def tile_list_sonobuoy_bearing_pairs_kernel(
             picked = at[g][:, :, P * quarter : P * (quarter + 1)]
             compare(nc.vector, 1, g, quarter, b_banks[g, quarter][:], picked, ALU.mult)
 
-        def difference(engine, g, quarter):
-            picked = at[g][:, :, P * quarter : P * (quarter + 1)]
-            compare(engine, 2, g, quarter, picked, cal_b[g, quarter][:], ALU.subtract)
+        def difference(engine, target, g, h, tiles, cols, scaled):
+            engine.tensor_tensor(
+                out=target[:, PACK * cols.start : PACK * cols.stop].rearrange(walk_out, e=LINE, t=PACK)[:, :, tiles, :],
+                in0=at[g][:, tiles, HALF * h + cols.start : HALF * h + cols.stop].rearrange(walk_in, e=LINE),
+                in1=scaled[:, tiles, :].rearrange(walk_in, e=LINE),
+                op=ALU.subtract,
+            )
 
-        def half_tile(g, h):
-            return values_tile(f"x_bf{g}{h}", [(kind, g, 2 * h + c) for kind in (1, 2) for c in range(2)], "x_bf")
+        cal_half = [sb([P, PACK, HALF], F32, f"cal_b0{h}") for h in range(2)]
+        for quarter in range(4):
+            cal_b[0, quarter] = cal_half[quarter // 2][:, :, P * (quarter % 2) : P * (quarter % 2 + 1)]
+            cal_b[1, quarter] = sb([P, PACK, P], F32, f"cal_b1{quarter}")[:]
+        first_half = slice(0, HALF)
+        low, high, every = slice(0, 2), slice(2, 4), slice(0, 4)
 
         bf_0 = values_tile("x_bf0", [(kind, 0, q) for kind in (1, 2) for q in range(4)], "x_bf")
-        for t in range(PACK):
+        x2_half = [bf_0[:, (4 + 2 * h) * PASS : (6 + 2 * h) * PASS] for h in range(2)]
+        for t in range(3):
             project_page(0, t)
         for quarter in range(4):
             project_table(0, quarter, 2 + quarter)
-            difference(nc.gpsimd, 0, quarter)
-            product(0, quarter)
-            project_page(1, quarter)
-        for quarter, number in enumerate((6, 7, 4, 5)):
+        calibrate(0, 0, (0, 1), (0, 1))
+        difference(nc.gpsimd, x2_half[0], 0, 0, low, first_half, cal_half[0])
+        project_page(0, 3)
+        calibrate(0, 1, (0, 1), (0, 1))
+        difference(nc.gpsimd, x2_half[1], 0, 1, low, first_half, cal_half[1])
+        for h in range(2):
+            calibrate(0, h, (2, 3), (0, 1))
+            difference(nc.gpsimd, x2_half[h], 0, h, high, first_half, cal_half[h])
+            for c in range(2):
+                product(0, 2 * h + c)
+            project_page(1, h)
+        for t in range(2, PACK):
+            project_page(1, t)
+        for quarter, number in enumerate((6, 7, 0, 1)):
             project_table(1, quarter, number)
-        wp_bf1 = [round_wp_piece(part, f"cal_b0{1 + part}") for part in range(2)]
+        for h in range(2):
+            calibrate(1, h, range(PACK), (0, 1))
+        wp_bf1 = [round_wp_piece(part, f"cal_b0{part}") for part in range(2)]
         early_sc = sb([P, 3 * PAIRS], U8, "early_sc", tag="a_sb7")
+        x2_0 = quantise("x2_codes0", bf_0[:, 4 * PASS :], early_sc[:, N + PAIRS :])
         wp_0 = quantise("wp_codes0", wp_bf0[:], early_sc[:, 0:N])
         x1_0 = quantise("x1_codes0", bf_0[:, 0 : 4 * PASS], early_sc[:, N : N + PAIRS])
-        x2_0 = quantise("x2_codes0", bf_0[:, 4 * PASS :], early_sc[:, N + PAIRS :])
 
-        bf_10 = half_tile(1, 0)
+        bf_10 = values_tile("x_bf10", [(kind, 1, c) for kind in (1, 2) for c in range(2)], "x_bf")
         last_bf = values_tile("last_bf", [(1, 1, 2), (2, 1, 2), (1, 1, 3), (2, 1, 3)], "page_bf1")
-        difference(nc.gpsimd, 1, 0)
+        difference(nc.gpsimd, bf_10[:, 2 * PASS :], 1, 0, every, slice(0, P), cal_b[1, 0])
         for quarter in range(3):
             product(1, quarter)
-        difference(nc.vector, 1, 1)
+        difference(nc.vector, bf_10[:, 2 * PASS :], 1, 0, every, slice(P, HALF), cal_b[1, 1])
 
         y_half = [bank(f"y_half{w}", [P, 2, HALF], 2 + w) for w in range(2)]
-        y_third = bank("y_third", [P, N // P, P], 0)
-        y_last = [bank(f"y_last{w}", [P, 2, P], number) for w, number in enumerate((1, 6))]
+        y_third = bank("y_third", [P, N // P, P], 4)
+        y_last = [bank(f"y_last{w}", [P, 2, P], number) for w, number in enumerate((5, 6))]
 
         def accumulate(targets, weights, x, cols, first, last):
             w_codes, w_sc = weights
@@ -322,14 +348,13 @@ def tile_list_sonobuoy_bearing_pairs_kernel(
             [(y_third[:, u, :], u == 0, u == 3) for u in range(4)],
             [(y_last[u // 2][:, u % 2, :], u % 2 == 0, u % 2 == 1) for u in range(4)],
         ]
-        first_half = slice(0, HALF)
         wd_pass = [(wd_w[:, g, :], wd_sc[4 * g : P, :]) for g in range(2)]
 
         def add_bias(result, target, u):
             nc.scalar.activation(out=result, in_=target, func=ACT.Identity, bias=bo_sb[:, u : u + 1], scale=1.0)
 
         second_half = slice(HALF, PAIRS)
-        for weights, x, first in ((wp_0, x1_0, True), (wd_pass[0], x2_0, False)):
+        for weights, x, first in ((wd_pass[0], x2_0, True), (wp_0, x1_0, False)):
             accumulate(half_targets, weights, x, first_half, first, False)
             for c in range(2):
                 accumulate(quarter_targets[c], weights, x, slice(HALF + P * c, HALF + P * (c + 1)), first, False)
@@ -348,11 +373,11 @@ def tile_list_sonobuoy_bearing_pairs_kernel(
             for e in range(2):
                 add_bias(result[:, e, :], y_half[w][:, e, :], 2 * w + e)
             nc.sync.dma_start(out=out_rows[:, 2 * w : 2 * w + 2, first_half], in_=result[:])
-        difference(nc.vector, 1, 2)
+        difference(nc.vector, last_bf[:, PASS:], 1, 1, every, slice(0, P), cal_b[1, 2])
         product(1, 3)
         three = quantise("x_codes_three", last_bf[:, 0 : 2 * PASS], late_sc[:, 3, 0:HALF])
         x1_last = quantise("x1_codes_last", last_bf[:, 2 * PASS : 3 * PASS], late_sc[:, 3, HALF : HALF + P])
-        difference(nc.vector, 1, 3)
+        difference(nc.vector, last_bf[:, 2 * PASS :], 1, 1, every, slice(P, HALF), cal_b[1, 3])
         x2_last = quantise("x2_codes_last", last_bf[:, 3 * PASS :], late_sc[:, 3, HALF + P :])
         accumulate(quarter_targets[0], wp_1, three, slice(0, P), False, False)
         accumulate(quarter_targets[0], wd_pass[1], three, slice(P, 2 * P), False, True)

@@ -297,14 +297,16 @@ def tile_list_sonobuoy_bearing_pairs_kernel(
         calibrate(0, 0, (0, 1), (0, 1))
         difference(nc.gpsimd, x2_half[0], 0, 0, low, first_half, cal_half[0])
         project_page(0, 3)
-        calibrate(0, 1, (0, 1), (0, 1))
-        difference(nc.gpsimd, x2_half[1], 0, 1, low, first_half, cal_half[1])
-        for h in range(2):
-            calibrate(0, h, (2, 3), (0, 1))
-            difference(nc.gpsimd, x2_half[h], 0, h, high, first_half, cal_half[h])
-            for c in range(2):
-                product(0, 2 * h + c)
-            project_page(1, h)
+        calibrate(0, 0, (2, 3), (0, 1))
+        difference(nc.gpsimd, x2_half[0], 0, 0, high, first_half, cal_half[0])
+        for c in range(2):
+            product(0, c)
+        for c in range(2):
+            project_page(1, c)
+            calibrate(0, 1, range(PACK), (c,))
+            cols = slice(P * c, P * (c + 1))
+            difference(nc.gpsimd, x2_half[1], 0, 1, every, cols, cal_b[0, 2 + c])
+            product(0, 2 + c)
         for t in range(2, PACK):
             project_page(1, t)
         for quarter, number in enumerate((6, 7, 0, 1)):

@@ -22,6 +22,7 @@ PACK = 4
 PASS = P * PACK
 HALF = PAIRS // 2
 LAST_SCALE_ROW = 32 * 3 + 3
+PAGE_PIECES = ((slice(0, PASS),), (slice(0, PASS // 2), slice(PASS // 2, PASS)))
 LINE = 4
 
 
@@ -41,10 +42,9 @@ def tile_list_sonobuoy_bearing_pairs_kernel(
         idx3 = keep.tile([P, PAIRS // 16], U16, name="idx3")
 
         tab_sc = sb([P, T], U8, "tab_sc")
-        wb_sc_raw = sb([P, H], U8, "wb_sc_raw")
+        wb_sc_raw = sb([P, 2, H], U8, "wb_sc_raw")
         wd_sc = sb([P, N], U8, "wd_sc")
-        wb_sc1 = sb([P, H], U8, "wb_sc1")
-        for scale_tile in (tab_sc, wb_sc_raw, wd_sc, wb_sc1):
+        for scale_tile in (tab_sc, wb_sc_raw, wd_sc):
             nc.vector.memset(scale_tile[:].bitcast(I32), 0)
 
         def load_scales(scale_tile, scales):
@@ -85,14 +85,18 @@ def tile_list_sonobuoy_bearing_pairs_kernel(
         load_page_rows(0)
         load_wa_quarter(0)
         load_page_rows(1)
-        load_scales(wb_sc_raw, wb_scales)
+        for quadrant in range(4):
+            nc.sync.dma_start(
+                out=wb_sc_raw[32 * quadrant : 32 * quadrant + 4, :, :].bitcast(I32),
+                in_=wb_scales[:, 4 * quadrant : 4 * quadrant + 4, :].rearrange("a r c -> r a c").bitcast(I32),
+            )
+        nc.sync.dma_start(idx[:], offs)
         load_wa_quarter(1)
-        load_wa_quarter(2)
         load_page_rows(2)
+        load_wa_quarter(2)
         load_wa_quarter(3)
         load_page_rows(3)
         nc.sync.dma_start(out=wb_raw[:].bitcast(I32), in_=wb_words.rearrange("a p c -> p a c").bitcast(I32))
-        nc.sync.dma_start(idx[:], offs)
         load_scales(tab_sc, tab_scales)
         load_table(0)
         load_table(1)
@@ -127,41 +131,48 @@ def tile_list_sonobuoy_bearing_pairs_kernel(
                 for h in range(2):
                     round_page_rows(i, h)
 
+        wa_sc = sb([P, H], U8, "wa_sc")
+
+        def quantise_wa(g, codes):
+            nc.vector.quantize_mx(
+                out=codes.bitcast(FP8X4),
+                scales=wa_sc[:, PASS * g : PASS * (g + 1)],
+                in_=wa_bf[:, g].rearrange("p t c i -> p (t c i)"),
+            )
+            return codes
+
+
         v_sc0 = sb([P, PAIRS], U8, "v_sc0")
         nc.vector.tensor_copy(v_sc0[:], tab_sc[:].indirect(idx[:]))
 
-        wb_sc0 = sb([P, H], U8, "wb_sc0")
+        wa_codes = [quantise_wa(0, sb([P, PASS], U32, "wa_codes0", tag="tab_sc")[:])]
+
+        wb_sc_both = sb([P, 2, H], U8, "wb_sc_both")
         nc.gpsimd.tensor_copy(
-            out=wb_sc0[:].rearrange("p (g t c) -> p g t c", g=2, t=PACK),
-            in_=wb_sc_raw[:].rearrange("p (g c t) -> p g t c", g=2, t=PACK),
+            out=wb_sc_both[:].rearrange("p a (g t c) -> p (a g) t c", g=2, t=PACK),
+            in_=wb_sc_raw[:].rearrange("p a (g c t) -> p (a g) t c", g=2, t=PACK),
         )
-        second_pass_scales(nc.gpsimd, wb_sc1, wb_sc0)
-        wb_sc = (wb_sc0, wb_sc1)
+        wb_sc = [wb_sc_both[:, a, :] for a in range(2)]
 
         v_w = [sb([P, PAIRS], U32, f"v_w{a}") for a in range(2)]
         nc.vector.tensor_copy(v_w[0][:], tab_w[0][:].bitcast(U32).indirect(idx[:]))
 
-        first_codes = sb([P, H + T2], U32, "first_codes", tag="tab_w0")
-        wa_codes = first_codes[:, 0:H]
-        wa_sc = sb([P, H], U8, "wa_sc")
-        nc.vector.quantize_mx(
-            out=wa_codes.bitcast(FP8X4), scales=wa_sc[:], in_=wa_bf[:].rearrange("p g t c i -> p (g t c i)")
-        )
-
-        page_codes, page_sc = [], []
         for h in range(2):
             round_page_rows(PACK - 1, h)
+        all_codes = sb([P, T2 + PASS], U32, "page_codes", tag="tab_w0")
+        wa_codes.append(quantise_wa(1, all_codes[:, T2:]))
+        all_sc = sb([P, T2], U8, "page_sc")
+        page_codes = [all_codes[:, PASS * h : PASS * (h + 1)] for h in range(2)]
+        page_sc = [all_sc[:, PASS * h : PASS * (h + 1)] for h in range(2)]
+        for h in range(2):
             page_bf = sb([P, PASS, 2], F32, f"page_bf{h}")
-            nc.scalar.copy(out=page_bf[:], in_=page_pairs[h][:].rearrange("p w c -> p c w"))
-            codes = first_codes[:, H + PASS * h : H + PASS * (h + 1)]
-            scales = sb([P, PASS], U8, f"page_sc{h}")
-            nc.vector.quantize_mx(
-                out=codes.bitcast(FP8X4),
-                scales=scales[:],
-                in_=page_bf[:].rearrange("p c w -> p (c w)").bitcast(BF16),
-            )
-            page_codes.append(codes)
-            page_sc.append(scales)
+            for cols in PAGE_PIECES[h]:
+                nc.scalar.copy(out=page_bf[:, cols, :], in_=page_pairs[h][:, :, cols].rearrange("p w c -> p c w"))
+                nc.vector.quantize_mx(
+                    out=page_codes[h][:, cols].bitcast(FP8X4),
+                    scales=page_sc[h][:, cols],
+                    in_=page_bf[:, cols, :].rearrange("p c w -> p (c w)").bitcast(BF16),
+                )
 
         nc.vector.tensor_copy(v_w[1][:], tab_w[1][:].bitcast(U32).indirect(idx[:]))
         wb_w = sb([P, 2, H], U16, "wb_w")
@@ -212,15 +223,16 @@ def tile_list_sonobuoy_bearing_pairs_kernel(
             rows = slice(PASS * g + P * t, PASS * g + P * (t + 1))
             for h in range(2):
                 a_bank = bank(f"a_bank{g}{t}{h}", [P, PASS], h + (6 if g == 0 and t % 2 else 0))
-                nc.tensor.matmul_mx(
-                    out=a_bank[:],
-                    lhsT=wa_codes[:, rows].bitcast(FP8X4),
-                    lhsT_scale=wa_sc[:, rows],
-                    rhs=page_codes[h].bitcast(FP8X4),
-                    rhs_scale=page_sc[h][:],
-                    start=True,
-                    stop=True,
-                )
+                for cols in PAGE_PIECES[h] if (g, t) == (0, 0) else PAGE_PIECES[0]:
+                    nc.tensor.matmul_mx(
+                        out=a_bank[:, cols],
+                        lhsT=wa_codes[g][:, P * t : P * (t + 1)].bitcast(FP8X4),
+                        lhsT_scale=wa_sc[:, rows],
+                        rhs=page_codes[h][:, cols].bitcast(FP8X4),
+                        rhs_scale=page_sc[h][:, cols],
+                        start=True,
+                        stop=True,
+                    )
                 nc.scalar.copy(out=a_sb[:, PASS * h : PASS * (h + 1)], in_=a_bank[:])
             nc.vector.tensor_copy(at[g][:, t, :], a_sb[:].indirect(idx3[:]))
 

@@ -21,8 +21,7 @@ P = 128
 PACK = 4
 PASS = P * PACK
 HALF = PAIRS // 2
-LAST_SCALE_ROW = 32 * 3 + 3
-PAGE_PIECES = ((slice(0, PASS),), (slice(0, PASS // 2), slice(PASS // 2, PASS)))
+A_BANKS = ((4, 6, 0, 6), (0, 6, 0, 0))
 LINE = 4
 
 
@@ -37,33 +36,28 @@ def tile_list_sonobuoy_bearing_pairs_kernel(
         def sb(shape, dtype, name, tag=None):
             return keep.tile(shape, dtype, name=name, tag=tag or name, align_bytes=64)
 
+        def bank(name, shape, number):
+            return psum.tile(shape, F32, name=name, tag=f"bank{number}")
+
         idx = keep.tile([P, PAIRS // 16], U16, name="idx")
         idx2 = keep.tile([P, S // 16], U16, name="idx2")
         idx3 = keep.tile([P, PAIRS // 16], U16, name="idx3")
 
         tab_sc = sb([P, T], U8, "tab_sc")
+        for rows in (slice(32, 64), slice(64, P)):
+            nc.vector.memset(tab_sc[rows, :].bitcast(I32), 0)
         wb_sc_raw = sb([P, 2, H], U8, "wb_sc_raw")
+        v_sc = sb([P, 2, PAIRS], U8, "v_sc")
         wd_sc = sb([P, N], U8, "wd_sc")
-        for scale_tile in (tab_sc, wb_sc_raw, wd_sc):
+        for scale_tile in (wb_sc_raw, v_sc, wd_sc):
             nc.vector.memset(scale_tile[:].bitcast(I32), 0)
-
-        def load_scales(scale_tile, scales):
-            for quadrant in range(4):
-                nc.sync.dma_start(
-                    out=scale_tile[32 * quadrant : 32 * quadrant + 8, :].bitcast(I32),
-                    in_=scales[:, 4 * quadrant : 4 * quadrant + 4, :].bitcast(I32),
-                )
-
-        def second_pass_scales(queue, target, both):
-            rows = LAST_SCALE_ROW + 1
-            queue.dma_start(out=target[0:rows, :].bitcast(I32), in_=both[4 : 4 + rows, :].bitcast(I32))
 
         base_rows = base.rearrange("(p i) t -> p i t", i=PACK)
         xs_rows = xs.rearrange("(p i) j -> p i j", i=PACK)
         wa_rows = wa.rearrange("(p i) r -> p i r", i=PACK)
         page = [sb([P, T2], F32, f"page{i}") for i in range(PACK)]
         incoming = [sb([P, S], F32, f"incoming{i}") for i in range(PACK)]
-        wa_raw = [sb([P, PACK, H // 4], F32, f"wa_raw{q}") for q in range(4)]
+        wa_raw = [sb([P, PACK, PASS], F32, f"wa_raw{g}") for g in range(2)]
         wp_raw = [sb([P, PACK, N], F32, f"wp_raw{g}") for g in range(2)]
         tab_w = [sb([P, T], I32, f"tab_w{a}") for a in range(2)]
         wb_raw = sb([P, 2, H], U16, "wb_raw")
@@ -75,31 +69,35 @@ def tile_list_sonobuoy_bearing_pairs_kernel(
             nc.sync.dma_start(out=page[i][:], in_=base_rows[:, i, :])
             nc.sync.dma_start(out=incoming[i][:], in_=xs_rows[:, i, :])
 
-        def load_wa_quarter(q):
-            nc.sync.dma_start(out=wa_raw[q][:], in_=wa_rows[:, :, (H // 4) * q : (H // 4) * (q + 1)])
+        def load_wa(g):
+            nc.sync.dma_start(out=wa_raw[g][:], in_=wa_rows[:, :, PASS * g : PASS * (g + 1)])
 
-        def load_table(a):
-            nc.sync.dma_start(out=tab_w[a][:], in_=tab_words[a].rearrange("p t i -> p (t i)").bitcast(I32))
-
+        nc.sync.dma_start(out=tab_sc[0:32, :].bitcast(I32), in_=tab_scales.rearrange("a q t -> q a t").bitcast(I32))
+        nc.sync.dma_start(idx[:], offs)
         nc.sync.dma_start(idx2[:], offs2)
         load_page_rows(0)
-        load_wa_quarter(0)
+        nc.sync.dma_start(out=wb_raw[:].bitcast(I32), in_=wb_words.rearrange("a p c -> p a c").bitcast(I32))
         load_page_rows(1)
         for quadrant in range(4):
             nc.sync.dma_start(
                 out=wb_sc_raw[32 * quadrant : 32 * quadrant + 4, :, :].bitcast(I32),
                 in_=wb_scales[:, 4 * quadrant : 4 * quadrant + 4, :].rearrange("a r c -> r a c").bitcast(I32),
             )
-        nc.sync.dma_start(idx[:], offs)
-        load_wa_quarter(1)
+        load_wa(0)
         load_page_rows(2)
-        load_wa_quarter(2)
-        load_wa_quarter(3)
+
+        picked_sc = sb([P, PAIRS], U8, "picked_sc")
+        nc.vector.tensor_copy(picked_sc[:], tab_sc[:].indirect(idx[:]))
+        for quadrant in range(4):
+            nc.sync.dma_start(
+                out=v_sc[32 * quadrant : 32 * quadrant + 4, :, :].bitcast(I32),
+                in_=picked_sc[8 * quadrant : 8 * quadrant + 8, :].bitcast(I32),
+            )
+
+        load_wa(1)
         load_page_rows(3)
-        nc.sync.dma_start(out=wb_raw[:].bitcast(I32), in_=wb_words.rearrange("a p c -> p a c").bitcast(I32))
-        load_scales(tab_sc, tab_scales)
-        load_table(0)
-        load_table(1)
+        for a in range(2):
+            nc.sync.dma_start(out=tab_w[a][:], in_=tab_words[a].rearrange("p t i -> p (t i)").bitcast(I32))
         nc.sync.dma_start(idx3[:], offs3)
         nc.sync.dma_start(out=cal_sb[:], in_=cal.rearrange("(g p t) -> p g t", g=2, t=PACK))
         for g in range(2):
@@ -107,300 +105,258 @@ def tile_list_sonobuoy_bearing_pairs_kernel(
                 out=wp_raw[g][:], in_=wp[PASS * g : PASS * (g + 1), :].rearrange("(p i) n -> p i n", i=PACK)
             )
         nc.sync.dma_start(out=wd_w[:], in_=wd_words.rearrange("a p c i -> p a (c i)").bitcast(I32))
-        load_scales(wd_sc, wd_scales)
+        for quadrant in range(4):
+            nc.sync.dma_start(
+                out=wd_sc[32 * quadrant : 32 * quadrant + 8, :].bitcast(I32),
+                in_=wd_scales[:, 4 * quadrant : 4 * quadrant + 4, :].bitcast(I32),
+            )
         with nc.allow_non_contiguous_dma(reason="one bias value a partition"):
             nc.sync.dma_start(out=bo_sb[:], in_=bo.rearrange("(u p) -> p u", p=P))
 
-        wa_bf = sb([P, 2, PACK, P, PACK], BF16, "wa_bf")
-        for q in range(4):
-            g, part = divmod(q, 2)
-            nc.scalar.copy(
-                out=wa_bf[:, g, :, (P // 2) * part : (P // 2) * (part + 1), :].rearrange("p t c i -> p c i t"),
-                in_=wa_raw[q][:].rearrange("p i (c t) -> p c i t", t=PACK),
-            )
+        def round_on_gpsimd(target, source):
+            nc.gpsimd.tensor_scalar(out=target, in0=source, scalar1=1.0, scalar2=0.0, op0=ALU.mult, op1=ALU.add)
 
-        page_pairs = [sb([P, 2, PASS], F32, f"page_pairs{h}", tag=f"wa_raw{h}") for h in range(2)]
-
-        def round_page_rows(i, h):
-            values = page_pairs[h][:, i // 2, :].bitcast(BF16).rearrange("p (c e) -> p c e", e=2)
-            nc.scalar.copy(out=values[:, :, i % 2], in_=page[i][:, PASS * h : PASS * (h + 1)])
-
-        for i in range(PACK):
-            nc.vector.tensor_copy(page[i][:].indirect(idx2[:]), incoming[i][:])
-            if i < PACK - 1:
-                for h in range(2):
-                    round_page_rows(i, h)
-
-        wa_sc = sb([P, H], U8, "wa_sc")
-
-        def quantise_wa(g, codes):
-            nc.vector.quantize_mx(
-                out=codes.bitcast(FP8X4),
-                scales=wa_sc[:, PASS * g : PASS * (g + 1)],
-                in_=wa_bf[:, g].rearrange("p t c i -> p (t c i)"),
-            )
-            return codes
-
-
-        v_sc0 = sb([P, PAIRS], U8, "v_sc0")
-        nc.vector.tensor_copy(v_sc0[:], tab_sc[:].indirect(idx[:]))
-
-        wa_codes = [quantise_wa(0, sb([P, PASS], U32, "wa_codes0", tag="tab_sc")[:])]
-
-        wb_sc_both = sb([P, 2, H], U8, "wb_sc_both")
-        nc.gpsimd.tensor_copy(
-            out=wb_sc_both[:].rearrange("p a (g t c) -> p (a g) t c", g=2, t=PACK),
-            in_=wb_sc_raw[:].rearrange("p a (g c t) -> p (a g) t c", g=2, t=PACK),
-        )
-        wb_sc = [wb_sc_both[:, a, :] for a in range(2)]
-
-        v_w = [sb([P, PAIRS], U32, f"v_w{a}") for a in range(2)]
-        nc.vector.tensor_copy(v_w[0][:], tab_w[0][:].bitcast(U32).indirect(idx[:]))
-
-        for h in range(2):
-            round_page_rows(PACK - 1, h)
-        all_codes = sb([P, T2 + PASS], U32, "page_codes", tag="tab_w0")
-        wa_codes.append(quantise_wa(1, all_codes[:, T2:]))
-        all_sc = sb([P, T2], U8, "page_sc")
-        page_codes = [all_codes[:, PASS * h : PASS * (h + 1)] for h in range(2)]
-        page_sc = [all_sc[:, PASS * h : PASS * (h + 1)] for h in range(2)]
-        for h in range(2):
-            page_bf = sb([P, PASS, 2], F32, f"page_bf{h}")
-            for cols in PAGE_PIECES[h]:
-                nc.scalar.copy(out=page_bf[:, cols, :], in_=page_pairs[h][:, :, cols].rearrange("p w c -> p c w"))
-                nc.vector.quantize_mx(
-                    out=page_codes[h][:, cols].bitcast(FP8X4),
-                    scales=page_sc[h][:, cols],
-                    in_=page_bf[:, cols, :].rearrange("p c w -> p (c w)").bitcast(BF16),
-                )
-
-        nc.vector.tensor_copy(v_w[1][:], tab_w[1][:].bitcast(U32).indirect(idx[:]))
         wb_w = sb([P, 2, H], U16, "wb_w")
         nc.gpsimd.tensor_copy(
             out=wb_w[:].rearrange("p a c -> p (a c)").rearrange("p (ag t c e) -> p ag c t e", ag=4, t=PACK, e=8),
             in_=wb_raw[:].rearrange("p a c -> p (a c)").rearrange("p (ag c e t) -> p ag c t e", ag=4, t=PACK, e=8),
         )
-
-        v_sc1 = sb([P, PAIRS], U8, "v_sc1", tag="wb_raw")
-        nc.gpsimd.memset(v_sc1[:].bitcast(I32), 0)
-        second_pass_scales(nc.gpsimd, v_sc1, v_sc0)
-        v_sc = (v_sc0, v_sc1)
-
-        def quantise(name, source, scales):
-            codes = sb([P, scales.shape[1]], U32, name)
-            nc.vector.quantize_mx(out=codes[:].bitcast(FP8X4), scales=scales, in_=source)
-            return codes, scales
-
-        def round_wp_piece(part, tag):
-            cols = slice(HALF * part, HALF * (part + 1))
-            wp_bf = sb([P, HALF * PACK], BF16, f"wp_bf1{part}", tag=tag)
-            nc.scalar.copy(
-                out=wp_bf[:].rearrange("p (c e i) -> p c i e", e=2, i=PACK),
-                in_=wp_raw[1][:, :, cols].rearrange("p i (c e) -> p c i e", e=2),
-            )
-            return wp_bf
-
-        wp_bf0 = sb([P, N * PACK], BF16, "wp_bf0", tag="page_bf1")
-        nc.gpsimd.tensor_scalar(
-            out=wp_bf0[:].rearrange("p (c i) -> p c i", i=PACK),
-            in0=wp_raw[0][:].rearrange("p i c -> p c i"),
-            scalar1=1.0,
-            scalar2=0.0,
-            op0=ALU.mult,
-            op1=ALU.add,
+        wb_sc = sb([P, 2, H], U8, "wb_sc")
+        nc.gpsimd.tensor_copy(
+            out=wb_sc[:].rearrange("p a (g t c) -> p (a g) t c", g=2, t=PACK),
+            in_=wb_sc_raw[:].rearrange("p a (g c t) -> p (a g) t c", g=2, t=PACK),
         )
 
-        def bank(name, shape, number):
-            return psum.tile(shape, F32, name=name, tag=f"bank{number}")
+        wa_bf = [sb([P, PACK, P, PACK], BF16, f"wa_bf{g}") for g in range(2)]
 
-        out_rows = out.rearrange("(u p) j -> p u j", p=P)
+        def round_wa(g):
+            nc.scalar.copy(
+                out=wa_bf[g][:].rearrange("p t c i -> p c i t"),
+                in_=wa_raw[g][:].rearrange("p i (c t) -> p c i t", t=PACK),
+            )
+
+        wa_sc = sb([P, H], U8, "wa_sc")
+
+        def quantise(codes, scales, values):
+            nc.vector.quantize_mx(out=codes.bitcast(FP8X4), scales=scales, in_=values)
+            return codes, scales
+
+        def quantise_wa(g, codes):
+            return quantise(codes, wa_sc[:, PASS * g : PASS * (g + 1)], wa_bf[g][:].rearrange("p t c i -> p (t c i)"))
+
+        page_bf = [sb([P, PASS, PACK], BF16, f"page_bf{h}") for h in range(2)]
+        wa_q = []
+        for i in range(PACK):
+            nc.vector.tensor_copy(page[i][:].indirect(idx2[:]), incoming[i][:])
+            nc.scalar.copy(out=page_bf[0][:, :, i], in_=page[i][:, 0:PASS])
+            round_on_gpsimd(page_bf[1][:, :, i], page[i][:, PASS:])
+            if i in (1, 2):
+                round_wa(i - 1)
+            if i == 2:
+                wa_q.append(quantise_wa(0, sb([P, PASS], U32, "wa_codes0", tag="incoming2")[:]))
+
+        v_w = [sb([P, PAIRS], U32, f"v_w{a}") for a in range(2)]
+        for a in range(2):
+            nc.vector.tensor_copy(v_w[a][:], tab_w[a][:].bitcast(U32).indirect(idx[:]))
+
+        late_codes = sb([P, T2 + PASS], U32, "late_codes", tag="tab_w1")
+        page_sc = sb([P, T2], U8, "page_sc")
+        page_q = []
+        for h in range(2):
+            cols = slice(PASS * h, PASS * (h + 1))
+            page_q.append(quantise(late_codes[:, cols], page_sc[:, cols], page_bf[h][:].rearrange("p c i -> p (c i)")))
+        wa_q.append(quantise_wa(1, late_codes[:, T2:]))
+
+        def multiply(target, stationary, dtype, moving, start, stop):
+            nc.tensor.matmul_mx(
+                out=target,
+                lhsT=stationary[0].bitcast(dtype),
+                lhsT_scale=stationary[1],
+                rhs=moving[0].bitcast(FP8X4),
+                rhs_scale=moving[1],
+                start=start,
+                stop=stop,
+            )
+
+        def columns(operand, cols):
+            return operand[0][:, cols], operand[1][:, cols]
+
+        wp_bf0 = sb([P, N, PACK], BF16, "wp_bf0", tag="page_bf1")
+        round_on_gpsimd(wp_bf0[:], wp_raw[0][:].rearrange("p i c -> p c i"))
+        wp_bf1_low = sb([P, HALF, PACK], BF16, "wp_bf1_low", tag="page_bf0")
+
         at = [sb([P, PACK, PAIRS], F32, f"at{g}") for g in range(2)]
-        walk_in = "p t (c e) -> p c t e"
-        walk_out = "p (c e t) -> p c t e"
+        a_sb = {}
 
-        def project_page(g, t, tag=None):
-            a_sb = sb([P, T2], F32, f"a_sb{PACK * g + t}", tag=tag)
-            rows = slice(PASS * g + P * t, PASS * g + P * (t + 1))
+        def project_page(g, t):
+            a_sb[g, t] = sb([P, T2], F32, f"a_sb{g}{t}", tag=f"page{t}" if g == 0 else None)
             for h in range(2):
-                a_bank = bank(f"a_bank{g}{t}{h}", [P, PASS], h + (6 if g == 0 and t % 2 else 0))
-                for cols in PAGE_PIECES[h] if (g, t) == (0, 0) else PAGE_PIECES[0]:
-                    nc.tensor.matmul_mx(
-                        out=a_bank[:, cols],
-                        lhsT=wa_codes[g][:, P * t : P * (t + 1)].bitcast(FP8X4),
-                        lhsT_scale=wa_sc[:, rows],
-                        rhs=page_codes[h][:, cols].bitcast(FP8X4),
-                        rhs_scale=page_sc[h][:, cols],
-                        start=True,
-                        stop=True,
-                    )
-                nc.scalar.copy(out=a_sb[:, PASS * h : PASS * (h + 1)], in_=a_bank[:])
-            nc.vector.tensor_copy(at[g][:, t, :], a_sb[:].indirect(idx3[:]))
+                a_bank = bank(f"a_bank{g}{t}{h}", [P, PASS], h + A_BANKS[g][t])
+                multiply(a_bank[:], columns(wa_q[g], slice(P * t, P * (t + 1))), FP8X4, page_q[h], True, True)
+                nc.scalar.copy(out=a_sb[g, t][:, PASS * h : PASS * (h + 1)], in_=a_bank[:])
 
-        b_banks, cal_b = {}, {}
+        def pick(g, t):
+            nc.vector.tensor_copy(at[g][:, t, :], a_sb[g, t][:].indirect(idx3[:]))
 
-        def project_table(g, quarter, number):
+        b_banks = {}
+
+        def project_table(g, quarter):
             cols = slice(P * quarter, P * (quarter + 1))
-            b_bank = bank(f"b_bank{g}{quarter}", [P, PACK, P], number)
+            b_bank = bank(f"b_bank{g}{quarter}", [P, PACK, P], 2 + quarter)
             for a in range(2):
                 for t in range(PACK):
-                    r0 = PASS * g + P * t
-                    nc.tensor.matmul_mx(
-                        out=b_bank[:, t, :],
-                        lhsT=wb_w[:, a, r0 : r0 + P].bitcast(FP4X4),
-                        lhsT_scale=wb_sc[a][:, r0 : r0 + P],
-                        rhs=v_w[a][:, cols].bitcast(FP8X4),
-                        rhs_scale=v_sc[a][:, cols],
-                        start=(a == 0 and t == 0),
-                        stop=(a == 1 and t == PACK - 1),
+                    rows = slice(PASS * g + P * t, PASS * g + P * (t + 1))
+                    multiply(
+                        b_bank[:, t, :],
+                        (wb_w[:, a, rows], wb_sc[:, a, rows]),
+                        FP4X4,
+                        (v_w[a][:, cols], v_sc[:, a, cols]),
+                        a == 0 and t == 0,
+                        a == 1 and t == PACK - 1,
                     )
             b_banks[g, quarter] = b_bank
 
-        def calibrate(g, h, tiles, quarters):
-            for c in quarters:
-                for t in tiles:
-                    nc.scalar.activation(
-                        out=cal_b[g, 2 * h + c][:, t, :],
-                        in_=b_banks[g, 2 * h + c][:, t, :],
-                        func=ACT.Copy,
-                        scale=cal_sb[:, g, t : t + 1],
-                    )
+        cal_b = {(g, h): sb([P, PACK, HALF], F32, f"cal_b{g}{h}") for g in range(2) for h in range(2)}
+        pairs = {(g, h): sb([P, 2, HALF], F32, f"pairs{g}{h}") for g in range(2) for h in range(2)}
 
-        x_bf = {}
+        def calibrate(g, h, t):
+            for c in range(2):
+                nc.scalar.activation(
+                    out=cal_b[g, h][:, t, P * c : P * (c + 1)],
+                    in_=b_banks[g, 2 * h + c][:, t, :],
+                    func=ACT.Copy,
+                    scale=cal_sb[:, g, t : t + 1],
+                )
 
-        def compare(engine, kind, g, quarter, first, second, op):
-            engine.tensor_tensor(
-                out=x_bf[kind, g, quarter].rearrange(walk_out, e=LINE, t=PACK),
-                in0=first.rearrange(walk_in, e=LINE),
-                in1=second.rearrange(walk_in, e=LINE),
-                op=op,
-            )
-
-        def values_tile(name, pieces, tag):
-            tile = sb([P, PASS * len(pieces)], BF16, name, tag=tag)
-            for place, piece in enumerate(pieces):
-                x_bf[piece] = tile[:, PASS * place : PASS * (place + 1)]
-            return tile
-
-        def product(g, quarter):
-            picked = at[g][:, :, P * quarter : P * (quarter + 1)]
-            compare(nc.vector, 1, g, quarter, b_banks[g, quarter][:], picked, ALU.mult)
-
-        def difference(engine, target, g, h, tiles, cols, scaled):
-            engine.tensor_tensor(
-                out=target[:, PACK * cols.start : PACK * cols.stop].rearrange(walk_out, e=LINE, t=PACK)[:, :, tiles, :],
-                in0=at[g][:, tiles, HALF * h + cols.start : HALF * h + cols.stop].rearrange(walk_in, e=LINE),
-                in1=scaled[:, tiles, :].rearrange(walk_in, e=LINE),
+        def difference(g, h, t):
+            values = pairs[g, h][:, t // 2, :].bitcast(BF16).rearrange("p (c e) -> p c e", e=2)
+            nc.gpsimd.tensor_tensor(
+                out=values[:, :, t % 2],
+                in0=at[g][:, t, HALF * h : HALF * (h + 1)],
+                in1=cal_b[g, h][:, t, :],
                 op=ALU.subtract,
             )
 
-        cal_half = [sb([P, PACK, HALF], F32, f"cal_b0{h}") for h in range(2)]
-        for quarter in range(4):
-            cal_b[0, quarter] = cal_half[quarter // 2][:, :, P * (quarter % 2) : P * (quarter % 2 + 1)]
-            cal_b[1, quarter] = sb([P, PACK, P], F32, f"cal_b1{quarter}")[:]
-        first_half = slice(0, HALF)
-        low, high, every = slice(0, 2), slice(2, 4), slice(0, 4)
+        x1_bf = [sb([P, PAIRS * PACK], BF16, f"x1_bf{g}") for g in range(2)]
+        x2_bf = {(g, h): sb([P, HALF, 2], F32, f"x2_bf{g}{h}") for g in range(2) for h in range(2)}
 
-        bf_0 = values_tile("x_bf0", [(kind, 0, q) for kind in (1, 2) for q in range(4)], "x_bf")
-        x2_half = [bf_0[:, (4 + 2 * h) * PASS : (6 + 2 * h) * PASS] for h in range(2)]
-        for t in range(3):
+        def weave(g, h):
+            nc.scalar.copy(out=x2_bf[g, h][:], in_=pairs[g, h][:].rearrange("p w c -> p c w"))
+
+        def x2_values(g, h):
+            return x2_bf[g, h][:].rearrange("p c w -> p (c w)").bitcast(BF16)
+
+        def product(g, quarter):
+            nc.vector.tensor_tensor(
+                out=x1_bf[g][:, PASS * quarter : PASS * (quarter + 1)].rearrange("p (c e t) -> p c t e", e=LINE, t=PACK),
+                in0=b_banks[g, quarter][:].rearrange("p t (c e) -> p c t e", e=LINE),
+                in1=at[g][:, :, P * quarter : P * (quarter + 1)].rearrange("p t (c e) -> p c t e", e=LINE),
+                op=ALU.mult,
+            )
+
+        for quarter in range(2):
+            project_table(0, quarter)
+        for t in range(PACK):
             project_page(0, t)
-        for quarter in range(4):
-            project_table(0, quarter, 2 + quarter)
-        calibrate(0, 0, (0, 1), (0, 1))
-        difference(nc.gpsimd, x2_half[0], 0, 0, low, first_half, cal_half[0])
-        project_page(0, 3)
-        calibrate(0, 0, (2, 3), (0, 1))
-        difference(nc.gpsimd, x2_half[0], 0, 0, high, first_half, cal_half[0])
-        for c in range(2):
-            product(0, c)
-        for c in range(2):
-            project_page(1, c)
-            calibrate(0, 1, range(PACK), (c,))
-            cols = slice(P * c, P * (c + 1))
-            difference(nc.gpsimd, x2_half[1], 0, 1, every, cols, cal_b[0, 2 + c])
-            product(0, 2 + c)
-        for t in range(2, PACK):
-            project_page(1, t)
-        for quarter, number in enumerate((6, 7, 0, 1)):
-            project_table(1, quarter, number)
+            pick(0, t)
+        for quarter in range(2, 4):
+            project_table(0, quarter)
         for h in range(2):
-            calibrate(1, h, range(PACK), (0, 1))
-        wp_bf1 = [round_wp_piece(part, f"cal_b0{part}") for part in range(2)]
-        early_sc = sb([P, 3 * PAIRS], U8, "early_sc", tag="a_sb7")
-        x2_0 = quantise("x2_codes0", bf_0[:, 4 * PASS :], early_sc[:, N + PAIRS :])
-        wp_0 = quantise("wp_codes0", wp_bf0[:], early_sc[:, 0:N])
-        x1_0 = quantise("x1_codes0", bf_0[:, 0 : 4 * PASS], early_sc[:, N : N + PAIRS])
+            for t in range(PACK):
+                calibrate(0, h, t)
+                difference(0, h, t)
+                if h == 0 and t in (1, 2):
+                    cols = slice(P * (t - 1), P * t)
+                    round_on_gpsimd(wp_bf1_low[:, cols, :], wp_raw[1][:, :, cols].rearrange("p i c -> p c i"))
+        for quarter in range(4):
+            product(0, quarter)
+            project_table(1, quarter)
 
-        bf_10 = values_tile("x_bf10", [(kind, 1, c) for kind in (1, 2) for c in range(2)], "x_bf")
-        last_bf = values_tile("last_bf", [(1, 1, 2), (2, 1, 2), (1, 1, 3), (2, 1, 3)], "page_bf1")
-        difference(nc.gpsimd, bf_10[:, 2 * PASS :], 1, 0, every, slice(0, P), cal_b[1, 0])
-        for quarter in range(3):
-            product(1, quarter)
-        difference(nc.vector, bf_10[:, 2 * PASS :], 1, 0, every, slice(P, HALF), cal_b[1, 1])
+        project_page(1, 0)
+        pick(1, 0)
+        first_half, second_half = slice(0, HALF), slice(HALF, PAIRS)
+        mid_sc = sb([P, PAIRS], U8, "mid_sc")
+        x1_codes0 = sb([P, PAIRS], U32, "x1_codes0")
+        quantise(x1_codes0[:, first_half], mid_sc[:, first_half], x1_bf[0][:, 0 : 2 * PASS])
+        wp_0 = quantise(sb([P, N], U32, "wp_codes0")[:], mid_sc[4:P, :], wp_bf0[:].rearrange("p c i -> p (c i)"))
+        quantise(x1_codes0[:, second_half], mid_sc[:, second_half], x1_bf[0][:, 2 * PASS :])
+        x1_0 = (x1_codes0[:], mid_sc[:])
+        wp_1 = (sb([P, N], U32, "wp_codes1")[:], sb([P, N], U8, "wp_sc1", tag="a_sb10")[:])
+        quantise(*columns(wp_1, first_half), wp_bf1_low[:].rearrange("p c i -> p (c i)"))
 
-        y_half = [bank(f"y_half{w}", [P, 2, HALF], 2 + w) for w in range(2)]
-        y_third = bank("y_third", [P, N // P, P], 4)
-        y_last = [bank(f"y_last{w}", [P, 2, P], number) for w, number in enumerate((5, 6))]
+        x2_codes0 = sb([P, PAIRS], U32, "x2_codes0")
+        x2_sc0 = sb([P, PAIRS], U8, "x2_sc0")
+        for t in range(1, PACK):
+            project_page(1, t)
+            if t == 1:
+                for h, cols in enumerate((first_half, second_half)):
+                    weave(0, h)
+                    quantise(x2_codes0[:, cols], x2_sc0[:, cols], x2_values(0, h))
+            pick(1, t)
+            for h in range(2):
+                calibrate(1, h, t - 1)
+                difference(1, h, t - 1)
+        x2_0 = (x2_codes0[:], x2_sc0[:])
+        for h in range(2):
+            calibrate(1, h, PACK - 1)
+            difference(1, h, PACK - 1)
+        wp_bf1_high = sb([P, HALF, PACK], BF16, "wp_bf1_high", tag="a_sb12")
+        nc.scalar.copy(
+            out=wp_bf1_high[:].rearrange("p (c e) i -> p c i e", e=2),
+            in_=wp_raw[1][:, :, second_half].rearrange("p i (c e) -> p c i e", e=2),
+        )
+        for h in range(2):
+            weave(1, h)
 
-        def accumulate(targets, weights, x, cols, first, last):
-            w_codes, w_sc = weights
-            codes, scales = x
-            for u, (target, opens, closes) in enumerate(targets):
-                n_cols = slice(P * u, P * (u + 1))
-                nc.tensor.matmul_mx(
-                    out=target,
-                    lhsT=w_codes[:, n_cols].bitcast(FP8X4),
-                    lhsT_scale=w_sc[:, n_cols],
-                    rhs=codes[:, cols].bitcast(FP8X4),
-                    rhs_scale=scales[:, cols],
-                    start=(first and opens),
-                    stop=(last and closes),
-                )
-
+        out_rows = out.rearrange("(u p) j -> p u j", p=P)
+        y_half = [bank(f"y_half{w}", [P, 2, HALF], w) for w in range(2)]
+        y_third = bank("y_third", [P, N // P, P], 6)
+        y_last = [bank(f"y_last{w}", [P, 2, P], number) for w, number in enumerate((7, 2))]
         half_targets = [(y_half[u // 2][:, u % 2, :], u % 2 == 0, u % 2 == 1) for u in range(4)]
-        quarter_targets = [
-            [(y_third[:, u, :], u == 0, u == 3) for u in range(4)],
-            [(y_last[u // 2][:, u % 2, :], u % 2 == 0, u % 2 == 1) for u in range(4)],
-        ]
-        wd_pass = [(wd_w[:, g, :], wd_sc[4 * g : P, :]) for g in range(2)]
+        third_targets = [(y_third[:, u, :], u == 0, u == 3) for u in range(4)]
+        last_targets = [(y_last[u // 2][:, u % 2, :], u % 2 == 0, u % 2 == 1) for u in range(4)]
+        third, last = slice(HALF, HALF + P), slice(HALF + P, PAIRS)
+        wd_q = [(wd_w[:, g, :], wd_sc[4 * g : P, :]) for g in range(2)]
+
+        def accumulate(targets, weights, x, first, final):
+            for u, (target, opens, closes) in enumerate(targets):
+                multiply(target, columns(weights, slice(P * u, P * (u + 1))), FP8X4, x, first and opens, final and closes)
+
+        for targets, cols in ((third_targets, third), (half_targets, first_half)):
+            accumulate(targets, wp_0, columns(x1_0, cols), True, False)
+            accumulate(targets, wd_q[0], columns(x2_0, cols), False, False)
+
+        for quarter in range(2):
+            product(1, quarter)
+        accumulate(last_targets, wp_0, columns(x1_0, last), True, False)
+        accumulate(last_targets, wd_q[0], columns(x2_0, last), False, False)
+        late_sc = sb([P, 2, PAIRS], U8, "late_sc")
+        x1_1 = (sb([P, PAIRS], U32, "x1_codes1")[:], late_sc[:, 0, :])
+        x2_1 = (sb([P, PAIRS], U32, "x2_codes1")[:], late_sc[:, 1, :])
+        quantise(*columns(wp_1, second_half), wp_bf1_high[:].rearrange("p c i -> p (c i)"))
+        quantise(*columns(x1_1, first_half), x1_bf[1][:, 0 : 2 * PASS])
+        accumulate(half_targets, wp_1, columns(x1_1, first_half), False, False)
 
         def add_bias(result, target, u):
             nc.scalar.activation(out=result, in_=target, func=ACT.Identity, bias=bo_sb[:, u : u + 1], scale=1.0)
 
-        second_half = slice(HALF, PAIRS)
-        for weights, x, first in ((wd_pass[0], x2_0, True), (wp_0, x1_0, False)):
-            accumulate(half_targets, weights, x, first_half, first, False)
-            for c in range(2):
-                accumulate(quarter_targets[c], weights, x, slice(HALF + P * c, HALF + P * (c + 1)), first, False)
-
-        late_sc = sb([P, 4, PAIRS], U8, "late_sc", tag="cal_b10")
-        wp_codes1 = sb([P, N], U32, "wp_codes1")
-        for part in range(2):
-            cols = slice(HALF * part, HALF * (part + 1))
-            nc.vector.quantize_mx(out=wp_codes1[:, cols].bitcast(FP8X4), scales=late_sc[:, 0, cols], in_=wp_bf1[part][:])
-        wp_1 = (wp_codes1, late_sc[:, 0, :])
-        x_10 = quantise("x_codes10", bf_10[:], late_sc[:, 1, :])
-        accumulate(half_targets, wp_1, x_10, first_half, False, False)
-        accumulate(half_targets, wd_pass[1], x_10, second_half, False, True)
+        quantise(*columns(x2_1, first_half), x2_values(1, 0))
+        accumulate(half_targets, wd_q[1], columns(x2_1, first_half), False, True)
         for w in range(2):
             result = sb([P, 2, HALF], F32, f"result_half{w}")
             for e in range(2):
                 add_bias(result[:, e, :], y_half[w][:, e, :], 2 * w + e)
             nc.sync.dma_start(out=out_rows[:, 2 * w : 2 * w + 2, first_half], in_=result[:])
-        difference(nc.vector, last_bf[:, PASS:], 1, 1, every, slice(0, P), cal_b[1, 2])
-        product(1, 3)
-        three = quantise("x_codes_three", last_bf[:, 0 : 2 * PASS], late_sc[:, 3, 0:HALF])
-        x1_last = quantise("x1_codes_last", last_bf[:, 2 * PASS : 3 * PASS], late_sc[:, 3, HALF : HALF + P])
-        difference(nc.vector, last_bf[:, 2 * PASS :], 1, 1, every, slice(P, HALF), cal_b[1, 3])
-        x2_last = quantise("x2_codes_last", last_bf[:, 3 * PASS :], late_sc[:, 3, HALF + P :])
-        accumulate(quarter_targets[0], wp_1, three, slice(0, P), False, False)
-        accumulate(quarter_targets[0], wd_pass[1], three, slice(P, 2 * P), False, True)
-        accumulate(quarter_targets[1], wp_1, x1_last, slice(0, P), False, False)
-        accumulate(quarter_targets[1], wd_pass[1], x2_last, slice(0, P), False, True)
+        for c, (targets, cols) in enumerate(((third_targets, third), (last_targets, last))):
+            product(1, 2 + c)
+            quantise(*columns(x2_1, cols), x2_values(1, 1)[:, PASS * c : PASS * (c + 1)])
+            accumulate(targets, wd_q[1], columns(x2_1, cols), False, False)
+            quantise(*columns(x1_1, cols), x1_bf[1][:, PASS * (2 + c) : PASS * (3 + c)])
+            accumulate(targets, wp_1, columns(x1_1, cols), False, True)
         result = sb([P, N // P, P], F32, "result_third")
         for u in range(N // P):
             add_bias(result[:, u, :], y_third[:, u, :], u)
-        nc.sync.dma_start(out=out_rows[:, :, HALF : HALF + P], in_=result[:])
+        nc.sync.dma_start(out=out_rows[:, :, third], in_=result[:])
         for w in range(2):
             result = sb([P, 2, P], F32, f"result_last{w}")
             if w == 0:
@@ -409,4 +365,4 @@ def tile_list_sonobuoy_bearing_pairs_kernel(
             else:
                 for e in range(2):
                     add_bias(result[:, e, :], y_last[1][:, e, :], 2 + e)
-            nc.sync.dma_start(out=out_rows[:, 2 * w : 2 * w + 2, HALF + P :], in_=result[:])
+            nc.sync.dma_start(out=out_rows[:, 2 * w : 2 * w + 2, last], in_=result[:])

@@ -21,7 +21,7 @@ P = 128
 PACK = 4
 PASS = P * PACK
 HALF = PAIRS // 2
-A_BANKS = ((4, 6, 0, 6), (0, 6, 0, 0))
+A_BANKS = ((4, 6, 0, 6), (0, 0, 0, 0))
 LINE = 4
 
 
@@ -137,15 +137,19 @@ def tile_list_sonobuoy_bearing_pairs_kernel(
 
         wa_sc = sb([P, H], U8, "wa_sc")
 
-        def quantise(codes, scales, values):
+        def quantise_into(codes, scales, values):
             nc.vector.quantize_mx(out=codes.bitcast(FP8X4), scales=scales, in_=values)
             return codes, scales
 
-        def quantise_wa(g, codes):
-            return quantise(codes, wa_sc[:, PASS * g : PASS * (g + 1)], wa_bf[g][:].rearrange("p t c i -> p (t c i)"))
+        wa_codes = {}
+
+        def quantise_wa(g, tiles, codes):
+            rows = slice(PASS * g + P * tiles.start, PASS * g + P * tiles.stop)
+            quantise_into(codes, wa_sc[:, rows], wa_bf[g][:, tiles].rearrange("p t c i -> p (t c i)"))
+            for t in range(tiles.start, tiles.stop):
+                wa_codes[g, t] = codes[:, P * (t - tiles.start) : P * (t - tiles.start + 1)]
 
         page_bf = [sb([P, PASS, PACK], BF16, f"page_bf{h}") for h in range(2)]
-        wa_q = []
         for i in range(PACK):
             nc.vector.tensor_copy(page[i][:].indirect(idx2[:]), incoming[i][:])
             nc.scalar.copy(out=page_bf[0][:, :, i], in_=page[i][:, 0:PASS])
@@ -153,210 +157,235 @@ def tile_list_sonobuoy_bearing_pairs_kernel(
             if i in (1, 2):
                 round_wa(i - 1)
             if i == 2:
-                wa_q.append(quantise_wa(0, sb([P, PASS], U32, "wa_codes0", tag="incoming2")[:]))
+                quantise_wa(0, slice(0, 1), sb([P, P], U32, "wa_codes0", tag="incoming2")[:])
 
         v_w = [sb([P, PAIRS], U32, f"v_w{a}") for a in range(2)]
         for a in range(2):
             nc.vector.tensor_copy(v_w[a][:], tab_w[a][:].bitcast(U32).indirect(idx[:]))
 
-        late_codes = sb([P, T2 + PASS], U32, "late_codes", tag="tab_w1")
+        late_codes = sb([P, T2 + H - P], U32, "late_codes", tag="tab_w1")
         page_sc = sb([P, T2], U8, "page_sc")
         page_q = []
         for h in range(2):
             cols = slice(PASS * h, PASS * (h + 1))
-            page_q.append(quantise(late_codes[:, cols], page_sc[:, cols], page_bf[h][:].rearrange("p c i -> p (c i)")))
-        wa_q.append(quantise_wa(1, late_codes[:, T2:]))
+            page_q.append(quantise_into(late_codes[:, cols], page_sc[:, cols], page_bf[h][:].rearrange("p c i -> p (c i)")))
+        for g, tiles in ((0, slice(1, 3)), (0, slice(3, 4)), (1, slice(0, 4))):
+            first = T2 + PASS * g + P * (tiles.start - 1)
+            quantise_wa(g, tiles, late_codes[:, first : first + P * (tiles.stop - tiles.start)])
 
-        def multiply(target, stationary, dtype, moving, start, stop):
-            nc.tensor.matmul_mx(
-                out=target,
-                lhsT=stationary[0].bitcast(dtype),
-                lhsT_scale=stationary[1],
-                rhs=moving[0].bitcast(FP8X4),
-                rhs_scale=moving[1],
-                start=start,
-                stop=stop,
+        def quantise(name, source, scales):
+            codes = sb([P, scales.shape[1]], U32, name)
+            nc.vector.quantize_mx(out=codes[:].bitcast(FP8X4), scales=scales, in_=source)
+            return codes, scales
+
+        def round_wp_piece(part, tag):
+            cols = slice(HALF * part, HALF * (part + 1))
+            wp_bf = sb([P, HALF * PACK], BF16, f"wp_bf1{part}", tag=tag)
+            nc.scalar.copy(
+                out=wp_bf[:].rearrange("p (c e i) -> p c i e", e=2, i=PACK),
+                in_=wp_raw[1][:, :, cols].rearrange("p i (c e) -> p c i e", e=2),
             )
+            return wp_bf
 
-        def columns(operand, cols):
-            return operand[0][:, cols], operand[1][:, cols]
+        wp_bf0 = sb([P, N * PACK], BF16, "wp_bf0", tag="page_bf1")
+        nc.gpsimd.tensor_scalar(
+            out=wp_bf0[:].rearrange("p (c i) -> p c i", i=PACK),
+            in0=wp_raw[0][:].rearrange("p i c -> p c i"),
+            scalar1=1.0,
+            scalar2=0.0,
+            op0=ALU.mult,
+            op1=ALU.add,
+        )
 
-        wp_bf0 = sb([P, N, PACK], BF16, "wp_bf0", tag="page_bf1")
-        round_on_gpsimd(wp_bf0[:], wp_raw[0][:].rearrange("p i c -> p c i"))
-        wp_bf1_low = sb([P, HALF, PACK], BF16, "wp_bf1_low", tag="page_bf0")
-
+        out_rows = out.rearrange("(u p) j -> p u j", p=P)
         at = [sb([P, PACK, PAIRS], F32, f"at{g}") for g in range(2)]
-        a_sb = {}
+        walk_in = "p t (c e) -> p c t e"
+        walk_out = "p (c e t) -> p c t e"
 
-        def project_page(g, t):
-            a_sb[g, t] = sb([P, T2], F32, f"a_sb{g}{t}", tag=f"page{t}" if g == 0 else None)
+        def project_page(g, t, tag=None):
+            a_sb = sb([P, T2], F32, f"a_sb{PACK * g + t}", tag=tag)
+            rows = slice(PASS * g + P * t, PASS * g + P * (t + 1))
             for h in range(2):
                 a_bank = bank(f"a_bank{g}{t}{h}", [P, PASS], h + A_BANKS[g][t])
-                multiply(a_bank[:], columns(wa_q[g], slice(P * t, P * (t + 1))), FP8X4, page_q[h], True, True)
-                nc.scalar.copy(out=a_sb[g, t][:, PASS * h : PASS * (h + 1)], in_=a_bank[:])
+                nc.tensor.matmul_mx(
+                    out=a_bank[:],
+                    lhsT=wa_codes[g, t].bitcast(FP8X4),
+                    lhsT_scale=wa_sc[:, rows],
+                    rhs=page_q[h][0].bitcast(FP8X4),
+                    rhs_scale=page_q[h][1],
+                    start=True,
+                    stop=True,
+                )
+                nc.scalar.copy(out=a_sb[:, PASS * h : PASS * (h + 1)], in_=a_bank[:])
+            nc.vector.tensor_copy(at[g][:, t, :], a_sb[:].indirect(idx3[:]))
 
-        def pick(g, t):
-            nc.vector.tensor_copy(at[g][:, t, :], a_sb[g, t][:].indirect(idx3[:]))
+        b_banks, cal_b = {}, {}
 
-        b_banks = {}
-
-        def project_table(g, quarter):
+        def project_table(g, quarter, number):
             cols = slice(P * quarter, P * (quarter + 1))
-            b_bank = bank(f"b_bank{g}{quarter}", [P, PACK, P], 2 + quarter)
+            b_bank = bank(f"b_bank{g}{quarter}", [P, PACK, P], number)
             for a in range(2):
                 for t in range(PACK):
-                    rows = slice(PASS * g + P * t, PASS * g + P * (t + 1))
-                    multiply(
-                        b_bank[:, t, :],
-                        (wb_w[:, a, rows], wb_sc[:, a, rows]),
-                        FP4X4,
-                        (v_w[a][:, cols], v_sc[:, a, cols]),
-                        a == 0 and t == 0,
-                        a == 1 and t == PACK - 1,
+                    r0 = PASS * g + P * t
+                    nc.tensor.matmul_mx(
+                        out=b_bank[:, t, :],
+                        lhsT=wb_w[:, a, r0 : r0 + P].bitcast(FP4X4),
+                        lhsT_scale=wb_sc[:, a, r0 : r0 + P],
+                        rhs=v_w[a][:, cols].bitcast(FP8X4),
+                        rhs_scale=v_sc[:, a, cols],
+                        start=(a == 0 and t == 0),
+                        stop=(a == 1 and t == PACK - 1),
                     )
             b_banks[g, quarter] = b_bank
 
-        cal_b = {(g, h): sb([P, PACK, HALF], F32, f"cal_b{g}{h}") for g in range(2) for h in range(2)}
-        pairs = {(g, h): sb([P, 2, HALF], F32, f"pairs{g}{h}") for g in range(2) for h in range(2)}
+        def calibrate(g, h, tiles, quarters):
+            for c in quarters:
+                for t in tiles:
+                    nc.scalar.activation(
+                        out=cal_b[g, 2 * h + c][:, t, :],
+                        in_=b_banks[g, 2 * h + c][:, t, :],
+                        func=ACT.Copy,
+                        scale=cal_sb[:, g, t : t + 1],
+                    )
 
-        def calibrate(g, h, t):
-            for c in range(2):
-                nc.scalar.activation(
-                    out=cal_b[g, h][:, t, P * c : P * (c + 1)],
-                    in_=b_banks[g, 2 * h + c][:, t, :],
-                    func=ACT.Copy,
-                    scale=cal_sb[:, g, t : t + 1],
-                )
+        x_bf = {}
 
-        def difference(g, h, t):
-            values = pairs[g, h][:, t // 2, :].bitcast(BF16).rearrange("p (c e) -> p c e", e=2)
-            nc.gpsimd.tensor_tensor(
-                out=values[:, :, t % 2],
-                in0=at[g][:, t, HALF * h : HALF * (h + 1)],
-                in1=cal_b[g, h][:, t, :],
+        def compare(engine, kind, g, quarter, first, second, op):
+            engine.tensor_tensor(
+                out=x_bf[kind, g, quarter].rearrange(walk_out, e=LINE, t=PACK),
+                in0=first.rearrange(walk_in, e=LINE),
+                in1=second.rearrange(walk_in, e=LINE),
+                op=op,
+            )
+
+        def values_tile(name, pieces, tag):
+            tile = sb([P, PASS * len(pieces)], BF16, name, tag=tag)
+            for place, piece in enumerate(pieces):
+                x_bf[piece] = tile[:, PASS * place : PASS * (place + 1)]
+            return tile
+
+        def product(g, quarter):
+            picked = at[g][:, :, P * quarter : P * (quarter + 1)]
+            compare(nc.vector, 1, g, quarter, b_banks[g, quarter][:], picked, ALU.mult)
+
+        def difference(engine, target, g, h, tiles, cols, scaled):
+            engine.tensor_tensor(
+                out=target[:, PACK * cols.start : PACK * cols.stop].rearrange(walk_out, e=LINE, t=PACK)[:, :, tiles, :],
+                in0=at[g][:, tiles, HALF * h + cols.start : HALF * h + cols.stop].rearrange(walk_in, e=LINE),
+                in1=scaled[:, tiles, :].rearrange(walk_in, e=LINE),
                 op=ALU.subtract,
             )
 
-        x1_bf = [sb([P, PAIRS * PACK], BF16, f"x1_bf{g}") for g in range(2)]
-        x2_bf = {(g, h): sb([P, HALF, 2], F32, f"x2_bf{g}{h}") for g in range(2) for h in range(2)}
-
-        def weave(g, h):
-            nc.scalar.copy(out=x2_bf[g, h][:], in_=pairs[g, h][:].rearrange("p w c -> p c w"))
-
-        def x2_values(g, h):
-            return x2_bf[g, h][:].rearrange("p c w -> p (c w)").bitcast(BF16)
-
-        def product(g, quarter):
-            nc.vector.tensor_tensor(
-                out=x1_bf[g][:, PASS * quarter : PASS * (quarter + 1)].rearrange("p (c e t) -> p c t e", e=LINE, t=PACK),
-                in0=b_banks[g, quarter][:].rearrange("p t (c e) -> p c t e", e=LINE),
-                in1=at[g][:, :, P * quarter : P * (quarter + 1)].rearrange("p t (c e) -> p c t e", e=LINE),
-                op=ALU.mult,
-            )
-
-        for quarter in range(2):
-            project_table(0, quarter)
-        for t in range(PACK):
-            project_page(0, t)
-            pick(0, t)
-        for quarter in range(2, 4):
-            project_table(0, quarter)
-        for h in range(2):
-            for t in range(PACK):
-                calibrate(0, h, t)
-                difference(0, h, t)
-                if h == 0 and t in (1, 2):
-                    cols = slice(P * (t - 1), P * t)
-                    round_on_gpsimd(wp_bf1_low[:, cols, :], wp_raw[1][:, :, cols].rearrange("p i c -> p c i"))
+        cal_half = [sb([P, PACK, HALF], F32, f"cal_b0{h}") for h in range(2)]
         for quarter in range(4):
-            product(0, quarter)
-            project_table(1, quarter)
+            cal_b[0, quarter] = cal_half[quarter // 2][:, :, P * (quarter % 2) : P * (quarter % 2 + 1)]
+            cal_b[1, quarter] = sb([P, PACK, P], F32, f"cal_b1{quarter}")[:]
+        first_half = slice(0, HALF)
+        low, high, every = slice(0, 2), slice(2, 4), slice(0, 4)
 
-        project_page(1, 0)
-        pick(1, 0)
-        first_half, second_half = slice(0, HALF), slice(HALF, PAIRS)
-        mid_sc = sb([P, PAIRS], U8, "mid_sc")
-        x1_codes0 = sb([P, PAIRS], U32, "x1_codes0")
-        quantise(x1_codes0[:, first_half], mid_sc[:, first_half], x1_bf[0][:, 0 : 2 * PASS])
-        wp_0 = quantise(sb([P, N], U32, "wp_codes0")[:], mid_sc[4:P, :], wp_bf0[:].rearrange("p c i -> p (c i)"))
-        quantise(x1_codes0[:, second_half], mid_sc[:, second_half], x1_bf[0][:, 2 * PASS :])
-        x1_0 = (x1_codes0[:], mid_sc[:])
-        wp_1 = (sb([P, N], U32, "wp_codes1")[:], sb([P, N], U8, "wp_sc1", tag="a_sb10")[:])
-        quantise(*columns(wp_1, first_half), wp_bf1_low[:].rearrange("p c i -> p (c i)"))
-
-        x2_codes0 = sb([P, PAIRS], U32, "x2_codes0")
-        x2_sc0 = sb([P, PAIRS], U8, "x2_sc0")
-        for t in range(1, PACK):
-            project_page(1, t)
-            if t == 1:
-                for h, cols in enumerate((first_half, second_half)):
-                    weave(0, h)
-                    quantise(x2_codes0[:, cols], x2_sc0[:, cols], x2_values(0, h))
-            pick(1, t)
-            for h in range(2):
-                calibrate(1, h, t - 1)
-                difference(1, h, t - 1)
-        x2_0 = (x2_codes0[:], x2_sc0[:])
-        for h in range(2):
-            calibrate(1, h, PACK - 1)
-            difference(1, h, PACK - 1)
-        wp_bf1_high = sb([P, HALF, PACK], BF16, "wp_bf1_high", tag="a_sb12")
-        nc.scalar.copy(
-            out=wp_bf1_high[:].rearrange("p (c e) i -> p c i e", e=2),
-            in_=wp_raw[1][:, :, second_half].rearrange("p i (c e) -> p c i e", e=2),
-        )
-        for h in range(2):
-            weave(1, h)
-
-        out_rows = out.rearrange("(u p) j -> p u j", p=P)
-        y_half = [bank(f"y_half{w}", [P, 2, HALF], w) for w in range(2)]
-        y_third = bank("y_third", [P, N // P, P], 6)
-        y_last = [bank(f"y_last{w}", [P, 2, P], number) for w, number in enumerate((7, 2))]
-        half_targets = [(y_half[u // 2][:, u % 2, :], u % 2 == 0, u % 2 == 1) for u in range(4)]
-        third_targets = [(y_third[:, u, :], u == 0, u == 3) for u in range(4)]
-        last_targets = [(y_last[u // 2][:, u % 2, :], u % 2 == 0, u % 2 == 1) for u in range(4)]
-        third, last = slice(HALF, HALF + P), slice(HALF + P, PAIRS)
-        wd_q = [(wd_w[:, g, :], wd_sc[4 * g : P, :]) for g in range(2)]
-
-        def accumulate(targets, weights, x, first, final):
-            for u, (target, opens, closes) in enumerate(targets):
-                multiply(target, columns(weights, slice(P * u, P * (u + 1))), FP8X4, x, first and opens, final and closes)
-
-        for targets, cols in ((third_targets, third), (half_targets, first_half)):
-            accumulate(targets, wp_0, columns(x1_0, cols), True, False)
-            accumulate(targets, wd_q[0], columns(x2_0, cols), False, False)
-
+        bf_0 = values_tile("x_bf0", [(kind, 0, q) for kind in (1, 2) for q in range(4)], "x_bf")
+        x2_half = [bf_0[:, (4 + 2 * h) * PASS : (6 + 2 * h) * PASS] for h in range(2)]
         for quarter in range(2):
+            project_table(0, quarter, 2 + quarter)
+        for t in range(3):
+            project_page(0, t)
+        for quarter in range(2, 4):
+            project_table(0, quarter, 2 + quarter)
+        calibrate(0, 0, (0, 1), (0, 1))
+        difference(nc.gpsimd, x2_half[0], 0, 0, low, first_half, cal_half[0])
+        project_page(0, 3)
+        calibrate(0, 0, (2, 3), (0, 1))
+        difference(nc.gpsimd, x2_half[0], 0, 0, high, first_half, cal_half[0])
+        for c in range(2):
+            product(0, c)
+        for c in range(2):
+            project_page(1, c)
+            calibrate(0, 1, range(PACK), (c,))
+            cols = slice(P * c, P * (c + 1))
+            difference(nc.gpsimd, x2_half[1], 0, 1, every, cols, cal_b[0, 2 + c])
+            product(0, 2 + c)
+        for t in range(2, PACK):
+            project_page(1, t)
+        for quarter, number in enumerate((6, 7, 0, 1)):
+            project_table(1, quarter, number)
+        for h in range(2):
+            calibrate(1, h, range(PACK), (0, 1))
+        wp_bf1 = [round_wp_piece(part, f"cal_b0{part}") for part in range(2)]
+        early_sc = sb([P, 3 * PAIRS], U8, "early_sc", tag="a_sb7")
+        x2_0 = quantise("x2_codes0", bf_0[:, 4 * PASS :], early_sc[:, N + PAIRS :])
+        wp_0 = quantise("wp_codes0", wp_bf0[:], early_sc[:, 0:N])
+        x1_0 = quantise("x1_codes0", bf_0[:, 0 : 4 * PASS], early_sc[:, N : N + PAIRS])
+
+        bf_10 = values_tile("x_bf10", [(kind, 1, c) for kind in (1, 2) for c in range(2)], "x_bf")
+        last_bf = values_tile("last_bf", [(1, 1, 2), (2, 1, 2), (1, 1, 3), (2, 1, 3)], "page_bf1")
+        difference(nc.gpsimd, bf_10[:, 2 * PASS :], 1, 0, every, slice(0, P), cal_b[1, 0])
+        for quarter in range(3):
             product(1, quarter)
-        accumulate(last_targets, wp_0, columns(x1_0, last), True, False)
-        accumulate(last_targets, wd_q[0], columns(x2_0, last), False, False)
-        late_sc = sb([P, 2, PAIRS], U8, "late_sc")
-        x1_1 = (sb([P, PAIRS], U32, "x1_codes1")[:], late_sc[:, 0, :])
-        x2_1 = (sb([P, PAIRS], U32, "x2_codes1")[:], late_sc[:, 1, :])
-        quantise(*columns(wp_1, second_half), wp_bf1_high[:].rearrange("p c i -> p (c i)"))
-        quantise(*columns(x1_1, first_half), x1_bf[1][:, 0 : 2 * PASS])
-        accumulate(half_targets, wp_1, columns(x1_1, first_half), False, False)
+        difference(nc.vector, bf_10[:, 2 * PASS :], 1, 0, every, slice(P, HALF), cal_b[1, 1])
+
+        y_half = [bank(f"y_half{w}", [P, 2, HALF], 2 + w) for w in range(2)]
+        y_third = bank("y_third", [P, N // P, P], 4)
+        y_last = [bank(f"y_last{w}", [P, 2, P], number) for w, number in enumerate((5, 6))]
+
+        def accumulate(targets, weights, x, cols, first, last):
+            w_codes, w_sc = weights
+            codes, scales = x
+            for u, (target, opens, closes) in enumerate(targets):
+                n_cols = slice(P * u, P * (u + 1))
+                nc.tensor.matmul_mx(
+                    out=target,
+                    lhsT=w_codes[:, n_cols].bitcast(FP8X4),
+                    lhsT_scale=w_sc[:, n_cols],
+                    rhs=codes[:, cols].bitcast(FP8X4),
+                    rhs_scale=scales[:, cols],
+                    start=(first and opens),
+                    stop=(last and closes),
+                )
+
+        half_targets = [(y_half[u // 2][:, u % 2, :], u % 2 == 0, u % 2 == 1) for u in range(4)]
+        quarter_targets = [
+            [(y_third[:, u, :], u == 0, u == 3) for u in range(4)],
+            [(y_last[u // 2][:, u % 2, :], u % 2 == 0, u % 2 == 1) for u in range(4)],
+        ]
+        wd_pass = [(wd_w[:, g, :], wd_sc[4 * g : P, :]) for g in range(2)]
 
         def add_bias(result, target, u):
             nc.scalar.activation(out=result, in_=target, func=ACT.Identity, bias=bo_sb[:, u : u + 1], scale=1.0)
 
-        quantise(*columns(x2_1, first_half), x2_values(1, 0))
-        accumulate(half_targets, wd_q[1], columns(x2_1, first_half), False, True)
+        second_half = slice(HALF, PAIRS)
+        for weights, x, first in ((wd_pass[0], x2_0, True), (wp_0, x1_0, False)):
+            accumulate(half_targets, weights, x, first_half, first, False)
+            for c in range(2):
+                accumulate(quarter_targets[c], weights, x, slice(HALF + P * c, HALF + P * (c + 1)), first, False)
+
+        late_sc = sb([P, 4, PAIRS], U8, "late_sc", tag="cal_b10")
+        wp_codes1 = sb([P, N], U32, "wp_codes1")
+        for part in range(2):
+            cols = slice(HALF * part, HALF * (part + 1))
+            nc.vector.quantize_mx(out=wp_codes1[:, cols].bitcast(FP8X4), scales=late_sc[:, 0, cols], in_=wp_bf1[part][:])
+        wp_1 = (wp_codes1, late_sc[:, 0, :])
+        x_10 = quantise("x_codes10", bf_10[:], late_sc[:, 1, :])
+        accumulate(half_targets, wp_1, x_10, first_half, False, False)
+        accumulate(half_targets, wd_pass[1], x_10, second_half, False, True)
         for w in range(2):
             result = sb([P, 2, HALF], F32, f"result_half{w}")
             for e in range(2):
                 add_bias(result[:, e, :], y_half[w][:, e, :], 2 * w + e)
             nc.sync.dma_start(out=out_rows[:, 2 * w : 2 * w + 2, first_half], in_=result[:])
-        for c, (targets, cols) in enumerate(((third_targets, third), (last_targets, last))):
-            product(1, 2 + c)
-            quantise(*columns(x2_1, cols), x2_values(1, 1)[:, PASS * c : PASS * (c + 1)])
-            accumulate(targets, wd_q[1], columns(x2_1, cols), False, False)
-            quantise(*columns(x1_1, cols), x1_bf[1][:, PASS * (2 + c) : PASS * (3 + c)])
-            accumulate(targets, wp_1, columns(x1_1, cols), False, True)
+        difference(nc.vector, last_bf[:, PASS:], 1, 1, every, slice(0, P), cal_b[1, 2])
+        product(1, 3)
+        three = quantise("x_codes_three", last_bf[:, 0 : 2 * PASS], late_sc[:, 3, 0:HALF])
+        x1_last = quantise("x1_codes_last", last_bf[:, 2 * PASS : 3 * PASS], late_sc[:, 3, HALF : HALF + P])
+        difference(nc.vector, last_bf[:, 2 * PASS :], 1, 1, every, slice(P, HALF), cal_b[1, 3])
+        x2_last = quantise("x2_codes_last", last_bf[:, 3 * PASS :], late_sc[:, 3, HALF + P :])
+        accumulate(quarter_targets[0], wp_1, three, slice(0, P), False, False)
+        accumulate(quarter_targets[0], wd_pass[1], three, slice(P, 2 * P), False, True)
+        accumulate(quarter_targets[1], wp_1, x1_last, slice(0, P), False, False)
+        accumulate(quarter_targets[1], wd_pass[1], x2_last, slice(0, P), False, True)
         result = sb([P, N // P, P], F32, "result_third")
         for u in range(N // P):
             add_bias(result[:, u, :], y_third[:, u, :], u)
-        nc.sync.dma_start(out=out_rows[:, :, third], in_=result[:])
+        nc.sync.dma_start(out=out_rows[:, :, HALF : HALF + P], in_=result[:])
         for w in range(2):
             result = sb([P, 2, P], F32, f"result_last{w}")
             if w == 0:
@@ -365,4 +394,4 @@ def tile_list_sonobuoy_bearing_pairs_kernel(
             else:
                 for e in range(2):
                     add_bias(result[:, e, :], y_last[1][:, e, :], 2 + e)
-            nc.sync.dma_start(out=out_rows[:, 2 * w : 2 * w + 2, last], in_=result[:])
+            nc.sync.dma_start(out=out_rows[:, 2 * w : 2 * w + 2, HALF + P :], in_=result[:])

@@ -187,7 +187,7 @@ def tile_list_sonobuoy_bearing_pairs_kernel(
             )
             return wp_bf
 
-        wp_bf0 = sb([P, N * PACK], BF16, "wp_bf0", tag="page_bf1")
+        wp_bf0 = sb([P, N * PACK], BF16, "wp_bf0", tag="wa_bf1")
         nc.gpsimd.tensor_scalar(
             out=wp_bf0[:].rearrange("p (c i) -> p c i", i=PACK),
             in0=wp_raw[0][:].rearrange("p i c -> p c i"),

@@ -44,8 +44,7 @@ def tile_list_sonobuoy_bearing_pairs_kernel(
         idx3 = keep.tile([P, PAIRS // 16], U16, name="idx3")
 
         tab_sc = sb([P, T], U8, "tab_sc")
-        for rows in (slice(32, 64), slice(64, P)):
-            nc.vector.memset(tab_sc[rows, :].bitcast(I32), 0)
+        nc.vector.memset(tab_sc[0:96, :].bitcast(I32), 0)
         wb_sc_raw = sb([P, 2, H], U8, "wb_sc_raw")
         v_sc = sb([P, 2, PAIRS], U8, "v_sc")
         wd_sc = sb([P, N], U8, "wd_sc")
@@ -72,7 +71,7 @@ def tile_list_sonobuoy_bearing_pairs_kernel(
         def load_wa(g):
             nc.sync.dma_start(out=wa_raw[g][:], in_=wa_rows[:, :, PASS * g : PASS * (g + 1)])
 
-        nc.sync.dma_start(out=tab_sc[0:32, :].bitcast(I32), in_=tab_scales.rearrange("a q t -> q a t").bitcast(I32))
+        nc.sync.dma_start(out=tab_sc[96:P, :].bitcast(I32), in_=tab_scales.rearrange("a q t -> q a t").bitcast(I32))
         nc.sync.dma_start(idx[:], offs)
         nc.sync.dma_start(idx2[:], offs2)
         load_page_rows(0)
@@ -91,7 +90,7 @@ def tile_list_sonobuoy_bearing_pairs_kernel(
         for quadrant in range(4):
             nc.sync.dma_start(
                 out=v_sc[32 * quadrant : 32 * quadrant + 4, :, :].bitcast(I32),
-                in_=picked_sc[8 * quadrant : 8 * quadrant + 8, :].bitcast(I32),
+                in_=picked_sc[96 + 8 * quadrant : 96 + 8 * quadrant + 8, :].bitcast(I32),
             )
 
         load_wa(1)
@@ -149,28 +148,27 @@ def tile_list_sonobuoy_bearing_pairs_kernel(
             for t in range(tiles.start, tiles.stop):
                 wa_codes[g, t] = codes[:, P * (t - tiles.start) : P * (t - tiles.start + 1)]
 
-        page_bf = [sb([P, PASS, PACK], BF16, f"page_bf{h}") for h in range(2)]
+        page_bf = [sb([P, PASS, PACK], BF16, f"page_bf{h}", tag=("page_bf0", "wb_raw")[h]) for h in range(2)]
         for i in range(PACK):
             nc.vector.tensor_copy(page[i][:].indirect(idx2[:]), incoming[i][:])
             nc.scalar.copy(out=page_bf[0][:, :, i], in_=page[i][:, 0:PASS])
             round_on_gpsimd(page_bf[1][:, :, i], page[i][:, PASS:])
             if i in (1, 2):
                 round_wa(i - 1)
-            if i == 2:
-                quantise_wa(0, slice(0, 1), sb([P, P], U32, "wa_codes0", tag="incoming2")[:])
 
         v_w = [sb([P, PAIRS], U32, f"v_w{a}") for a in range(2)]
         for a in range(2):
             nc.vector.tensor_copy(v_w[a][:], tab_w[a][:].bitcast(U32).indirect(idx[:]))
 
-        late_codes = sb([P, T2 + H - P], U32, "late_codes", tag="tab_w1")
+        late_codes = sb([P, T2 + H], U32, "late_codes", tag="tab_w1")
         page_sc = sb([P, T2], U8, "page_sc")
         page_q = []
+        quantise_wa(0, slice(0, 1), late_codes[:, T2 : T2 + P])
         for h in range(2):
             cols = slice(PASS * h, PASS * (h + 1))
             page_q.append(quantise_into(late_codes[:, cols], page_sc[:, cols], page_bf[h][:].rearrange("p c i -> p (c i)")))
         for g, tiles in ((0, slice(1, 3)), (0, slice(3, 4)), (1, slice(0, 4))):
-            first = T2 + PASS * g + P * (tiles.start - 1)
+            first = T2 + PASS * g + P * tiles.start
             quantise_wa(g, tiles, late_codes[:, first : first + P * (tiles.stop - tiles.start)])
 
         def quantise(name, source, scales):
@@ -317,7 +315,7 @@ def tile_list_sonobuoy_bearing_pairs_kernel(
         x1_0 = quantise("x1_codes0", bf_0[:, 0 : 4 * PASS], early_sc[:, N : N + PAIRS])
 
         bf_10 = values_tile("x_bf10", [(kind, 1, c) for kind in (1, 2) for c in range(2)], "x_bf")
-        last_bf = values_tile("last_bf", [(1, 1, 2), (2, 1, 2), (1, 1, 3), (2, 1, 3)], "page_bf1")
+        last_bf = values_tile("last_bf", [(1, 1, 2), (2, 1, 2), (1, 1, 3), (2, 1, 3)], "wb_raw")
         difference(nc.gpsimd, bf_10[:, 2 * PASS :], 1, 0, every, slice(0, P), cal_b[1, 0])
         for quarter in range(3):
             product(1, quarter)

@@ -22,6 +22,7 @@ PACK = 4
 PASS = P * PACK
 HALF = PAIRS // 2
 A_BANKS = ((4, 6, 0, 6), (0, 0, 0, 0))
+WA_PIECES = (slice(0, PASS), slice(PASS, PASS + HALF), slice(PASS + HALF, H))
 LINE = 4
 
 
@@ -56,7 +57,7 @@ def tile_list_sonobuoy_bearing_pairs_kernel(
         wa_rows = wa.rearrange("(p i) r -> p i r", i=PACK)
         page = [sb([P, T2], F32, f"page{i}") for i in range(PACK)]
         incoming = [sb([P, S], F32, f"incoming{i}") for i in range(PACK)]
-        wa_raw = [sb([P, PACK, PASS], F32, f"wa_raw{g}") for g in range(2)]
+        wa_raw = [sb([P, PACK, r.stop - r.start], F32, f"wa_raw{n}") for n, r in enumerate(WA_PIECES)]
         wp_raw = [sb([P, PACK, N], F32, f"wp_raw{g}") for g in range(2)]
         tab_w = [sb([P, T], I32, f"tab_w{a}") for a in range(2)]
         wb_raw = sb([P, 2, H], U16, "wb_raw")
@@ -68,8 +69,8 @@ def tile_list_sonobuoy_bearing_pairs_kernel(
             nc.sync.dma_start(out=page[i][:], in_=base_rows[:, i, :])
             nc.sync.dma_start(out=incoming[i][:], in_=xs_rows[:, i, :])
 
-        def load_wa(g):
-            nc.sync.dma_start(out=wa_raw[g][:], in_=wa_rows[:, :, PASS * g : PASS * (g + 1)])
+        def load_wa(n):
+            nc.sync.dma_start(out=wa_raw[n][:], in_=wa_rows[:, :, WA_PIECES[n]])
 
         nc.sync.dma_start(out=tab_sc[96:P, :].bitcast(I32), in_=tab_scales.rearrange("a q t -> q a t").bitcast(I32))
         nc.sync.dma_start(idx[:], offs)
@@ -97,6 +98,7 @@ def tile_list_sonobuoy_bearing_pairs_kernel(
         load_page_rows(3)
         for a in range(2):
             nc.sync.dma_start(out=tab_w[a][:], in_=tab_words[a].rearrange("p t i -> p (t i)").bitcast(I32))
+        load_wa(2)
         nc.sync.dma_start(idx3[:], offs3)
         nc.sync.dma_start(out=cal_sb[:], in_=cal.rearrange("(g p t) -> p g t", g=2, t=PACK))
         for g in range(2):
@@ -128,10 +130,12 @@ def tile_list_sonobuoy_bearing_pairs_kernel(
 
         wa_bf = [sb([P, PACK, P, PACK], BF16, f"wa_bf{g}") for g in range(2)]
 
-        def round_wa(g):
+        def round_wa(n):
+            g, first = divmod(WA_PIECES[n].start, PASS)
+            width = WA_PIECES[n].stop - WA_PIECES[n].start
             nc.scalar.copy(
-                out=wa_bf[g][:].rearrange("p t c i -> p c i t"),
-                in_=wa_raw[g][:].rearrange("p i (c t) -> p c i t", t=PACK),
+                out=wa_bf[g][:, :, first // PACK : (first + width) // PACK, :].rearrange("p t c i -> p c i t"),
+                in_=wa_raw[n][:].rearrange("p i (c t) -> p c i t", t=PACK),
             )
 
         wa_sc = sb([P, H], U8, "wa_sc")
@@ -153,7 +157,7 @@ def tile_list_sonobuoy_bearing_pairs_kernel(
             nc.vector.tensor_copy(page[i][:].indirect(idx2[:]), incoming[i][:])
             nc.scalar.copy(out=page_bf[0][:, :, i], in_=page[i][:, 0:PASS])
             round_on_gpsimd(page_bf[1][:, :, i], page[i][:, PASS:])
-            if i in (1, 2):
+            if i > 0:
                 round_wa(i - 1)
 
         v_w = [sb([P, PAIRS], U32, f"v_w{a}") for a in range(2)]
@@ -321,14 +325,14 @@ def tile_list_sonobuoy_bearing_pairs_kernel(
             product(1, quarter)
         difference(nc.vector, bf_10[:, 2 * PASS :], 1, 0, every, slice(P, HALF), cal_b[1, 1])
 
-        y_half = [bank(f"y_half{w}", [P, 2, HALF], 2 + w) for w in range(2)]
-        y_third = bank("y_third", [P, N // P, P], 4)
-        y_last = [bank(f"y_last{w}", [P, 2, P], number) for w, number in enumerate((5, 6))]
+        y_half = [bank(f"y_half{w}", [P, 2, HALF], number) for w, number in enumerate((7, 0))]
+        y_third = bank("y_third", [P, N // P, P], 2)
+        y_last = [bank(f"y_last{w}", [P, 2, P], number) for w, number in enumerate((3, 4))]
 
-        def accumulate(targets, weights, x, cols, first, last):
+        def accumulate(targets, weights, x, cols, first, last, first_u=0):
             w_codes, w_sc = weights
             codes, scales = x
-            for u, (target, opens, closes) in enumerate(targets):
+            for u, (target, opens, closes) in enumerate(targets, first_u):
                 n_cols = slice(P * u, P * (u + 1))
                 nc.tensor.matmul_mx(
                     out=target,
@@ -352,9 +356,11 @@ def tile_list_sonobuoy_bearing_pairs_kernel(
 
         second_half = slice(HALF, PAIRS)
         for weights, x, first in ((wd_pass[0], x2_0, True), (wp_0, x1_0, False)):
-            accumulate(half_targets, weights, x, first_half, first, False)
             for c in range(2):
                 accumulate(quarter_targets[c], weights, x, slice(HALF + P * c, HALF + P * (c + 1)), first, False)
+        for w in range(2):
+            for weights, x, first in ((wd_pass[0], x2_0, True), (wp_0, x1_0, False)):
+                accumulate(half_targets[2 * w : 2 * w + 2], weights, x, first_half, first, False, 2 * w)
 
         late_sc = sb([P, 4, PAIRS], U8, "late_sc", tag="cal_b10")
         wp_codes1 = sb([P, N], U32, "wp_codes1")

@@ -22,7 +22,7 @@ PACK = 4
 PASS = P * PACK
 HALF = PAIRS // 2
 A_BANKS = ((4, 6, 0, 6), (0, 0, 0, 0))
-WA_PIECES = (slice(0, PASS), slice(PASS, PASS + HALF), slice(PASS + HALF, H))
+WA_PIECES = tuple(slice(HALF * n, HALF * (n + 1)) for n in range(4))
 LINE = 4
 
 
@@ -60,7 +60,7 @@ def tile_list_sonobuoy_bearing_pairs_kernel(
         wa_raw = [sb([P, PACK, r.stop - r.start], F32, f"wa_raw{n}") for n, r in enumerate(WA_PIECES)]
         wp_raw = [sb([P, PACK, N], F32, f"wp_raw{g}") for g in range(2)]
         tab_w = [sb([P, T], I32, f"tab_w{a}") for a in range(2)]
-        wb_raw = sb([P, 2, H], U16, "wb_raw")
+        wb_raw = [sb([P, H], U16, f"wb_raw{a}") for a in range(2)]
         wd_w = sb([P, 2, N], I32, "wd_w")
         cal_sb = sb([P, 2, PACK], F32, "cal_sb")
         bo_sb = sb([P, N // P], F32, "bo_sb")
@@ -76,14 +76,15 @@ def tile_list_sonobuoy_bearing_pairs_kernel(
         nc.sync.dma_start(idx[:], offs)
         nc.sync.dma_start(idx2[:], offs2)
         load_page_rows(0)
-        nc.sync.dma_start(out=wb_raw[:].bitcast(I32), in_=wb_words.rearrange("a p c -> p a c").bitcast(I32))
-        load_page_rows(1)
         for quadrant in range(4):
             nc.sync.dma_start(
                 out=wb_sc_raw[32 * quadrant : 32 * quadrant + 4, :, :].bitcast(I32),
                 in_=wb_scales[:, 4 * quadrant : 4 * quadrant + 4, :].rearrange("a r c -> r a c").bitcast(I32),
             )
         load_wa(0)
+        nc.sync.dma_start(out=wb_raw[0][:].bitcast(I32), in_=wb_words[0].bitcast(I32))
+        load_page_rows(1)
+        load_wa(1)
         load_page_rows(2)
 
         picked_sc = sb([P, PAIRS], U8, "picked_sc")
@@ -94,11 +95,12 @@ def tile_list_sonobuoy_bearing_pairs_kernel(
                 in_=picked_sc[96 + 8 * quadrant : 96 + 8 * quadrant + 8, :].bitcast(I32),
             )
 
-        load_wa(1)
+        nc.sync.dma_start(out=wb_raw[1][:].bitcast(I32), in_=wb_words[1].bitcast(I32))
+        load_wa(2)
         load_page_rows(3)
         for a in range(2):
             nc.sync.dma_start(out=tab_w[a][:], in_=tab_words[a].rearrange("p t i -> p (t i)").bitcast(I32))
-        load_wa(2)
+        load_wa(3)
         nc.sync.dma_start(idx3[:], offs3)
         nc.sync.dma_start(out=cal_sb[:], in_=cal.rearrange("(g p t) -> p g t", g=2, t=PACK))
         for g in range(2):
@@ -117,30 +119,31 @@ def tile_list_sonobuoy_bearing_pairs_kernel(
         def round_on_gpsimd(target, source):
             nc.gpsimd.tensor_scalar(out=target, in0=source, scalar1=1.0, scalar2=0.0, op0=ALU.mult, op1=ALU.add)
 
-        wb_w = sb([P, 2, H], U16, "wb_w")
-        nc.gpsimd.tensor_copy(
-            out=wb_w[:].rearrange("p a c -> p (a c)").rearrange("p (ag t c e) -> p ag c t e", ag=4, t=PACK, e=8),
-            in_=wb_raw[:].rearrange("p a c -> p (a c)").rearrange("p (ag c e t) -> p ag c t e", ag=4, t=PACK, e=8),
-        )
         wb_sc = sb([P, 2, H], U8, "wb_sc")
         nc.gpsimd.tensor_copy(
             out=wb_sc[:].rearrange("p a (g t c) -> p (a g) t c", g=2, t=PACK),
             in_=wb_sc_raw[:].rearrange("p a (g c t) -> p (a g) t c", g=2, t=PACK),
         )
+        wb_w = sb([P, 2, H], U16, "wb_w")
+        for a in range(2):
+            nc.gpsimd.tensor_copy(
+                out=wb_w[:, a, :].rearrange("p (g t c e) -> p g c t e", g=2, t=PACK, e=8),
+                in_=wb_raw[a][:].rearrange("p (g c e t) -> p g c t e", g=2, t=PACK, e=8),
+            )
 
-        wa_bf = [sb([P, PACK, P, PACK], BF16, f"wa_bf{g}") for g in range(2)]
+        wa_bf = sb([P, 2, PACK, P, PACK], BF16, "wa_bf")
 
         def round_wa(n):
             g, first = divmod(WA_PIECES[n].start, PASS)
             width = WA_PIECES[n].stop - WA_PIECES[n].start
             nc.scalar.copy(
-                out=wa_bf[g][:, :, first // PACK : (first + width) // PACK, :].rearrange("p t c i -> p c i t"),
+                out=wa_bf[:, g, :, first // PACK : (first + width) // PACK, :].rearrange("p t c i -> p c i t"),
                 in_=wa_raw[n][:].rearrange("p i (c t) -> p c i t", t=PACK),
             )
 
         wa_sc = sb([P, H], U8, "wa_sc")
 
-        def quantise_into(codes, scales, values):
+        def quantise(codes, scales, values):
             nc.vector.quantize_mx(out=codes.bitcast(FP8X4), scales=scales, in_=values)
             return codes, scales
 
@@ -148,21 +151,24 @@ def tile_list_sonobuoy_bearing_pairs_kernel(
 
         def quantise_wa(g, tiles, codes):
             rows = slice(PASS * g + P * tiles.start, PASS * g + P * tiles.stop)
-            quantise_into(codes, wa_sc[:, rows], wa_bf[g][:, tiles].rearrange("p t c i -> p (t c i)"))
+            quantise(codes, wa_sc[:, rows], wa_bf[:, g, tiles].rearrange("p t c i -> p (t c i)"))
             for t in range(tiles.start, tiles.stop):
                 wa_codes[g, t] = codes[:, P * (t - tiles.start) : P * (t - tiles.start + 1)]
 
-        page_bf = [sb([P, PASS, PACK], BF16, f"page_bf{h}", tag=("page_bf0", "wb_raw")[h]) for h in range(2)]
+        page_bf = [sb([P, PASS, PACK], BF16, f"page_bf{h}", tag=("page_bf0", "wb_sc_raw")[h]) for h in range(2)]
         for i in range(PACK):
             nc.vector.tensor_copy(page[i][:].indirect(idx2[:]), incoming[i][:])
             nc.scalar.copy(out=page_bf[0][:, :, i], in_=page[i][:, 0:PASS])
             round_on_gpsimd(page_bf[1][:, :, i], page[i][:, PASS:])
-            if i > 0:
-                round_wa(i - 1)
+            round_wa(i)
 
         v_w = [sb([P, PAIRS], U32, f"v_w{a}") for a in range(2)]
-        for a in range(2):
+
+        def pick_words(a):
             nc.vector.tensor_copy(v_w[a][:], tab_w[a][:].bitcast(U32).indirect(idx[:]))
+
+        for a in range(2):
+            pick_words(a)
 
         late_codes = sb([P, T2 + H], U32, "late_codes", tag="tab_w1")
         page_sc = sb([P, T2], U8, "page_sc")
@@ -170,232 +176,192 @@ def tile_list_sonobuoy_bearing_pairs_kernel(
         quantise_wa(0, slice(0, 1), late_codes[:, T2 : T2 + P])
         for h in range(2):
             cols = slice(PASS * h, PASS * (h + 1))
-            page_q.append(quantise_into(late_codes[:, cols], page_sc[:, cols], page_bf[h][:].rearrange("p c i -> p (c i)")))
+            page_q.append(quantise(late_codes[:, cols], page_sc[:, cols], page_bf[h][:].rearrange("p c i -> p (c i)")))
         for g, tiles in ((0, slice(1, 3)), (0, slice(3, 4)), (1, slice(0, 4))):
             first = T2 + PASS * g + P * tiles.start
             quantise_wa(g, tiles, late_codes[:, first : first + P * (tiles.stop - tiles.start)])
 
-        def quantise(name, source, scales):
-            codes = sb([P, scales.shape[1]], U32, name)
-            nc.vector.quantize_mx(out=codes[:].bitcast(FP8X4), scales=scales, in_=source)
-            return codes, scales
-
-        def round_wp_piece(part, tag):
-            cols = slice(HALF * part, HALF * (part + 1))
-            wp_bf = sb([P, HALF * PACK], BF16, f"wp_bf1{part}", tag=tag)
-            nc.scalar.copy(
-                out=wp_bf[:].rearrange("p (c e i) -> p c i e", e=2, i=PACK),
-                in_=wp_raw[1][:, :, cols].rearrange("p i (c e) -> p c i e", e=2),
+        def multiply(target, stationary, dtype, moving, start, stop):
+            nc.tensor.matmul_mx(
+                out=target,
+                lhsT=stationary[0].bitcast(dtype),
+                lhsT_scale=stationary[1],
+                rhs=moving[0].bitcast(FP8X4),
+                rhs_scale=moving[1],
+                start=start,
+                stop=stop,
             )
-            return wp_bf
 
-        wp_bf0 = sb([P, N * PACK], BF16, "wp_bf0", tag="wa_bf1")
-        nc.gpsimd.tensor_scalar(
-            out=wp_bf0[:].rearrange("p (c i) -> p c i", i=PACK),
-            in0=wp_raw[0][:].rearrange("p i c -> p c i"),
-            scalar1=1.0,
-            scalar2=0.0,
-            op0=ALU.mult,
-            op1=ALU.add,
-        )
+        def columns(operand, cols):
+            return operand[0][:, cols], operand[1][:, cols]
 
-        out_rows = out.rearrange("(u p) j -> p u j", p=P)
+        wp_bf0 = sb([P, N, PACK], BF16, "wp_bf0", tag="wa_bf")
+        round_on_gpsimd(wp_bf0[:], wp_raw[0][:].rearrange("p i c -> p c i"))
+
         at = [sb([P, PACK, PAIRS], F32, f"at{g}") for g in range(2)]
-        walk_in = "p t (c e) -> p c t e"
-        walk_out = "p (c e t) -> p c t e"
 
-        def project_page(g, t, tag=None):
-            a_sb = sb([P, T2], F32, f"a_sb{PACK * g + t}", tag=tag)
+        def project_page(g, t):
+            a_sb = sb([P, T2], F32, f"a_sb{g}{t}")
             rows = slice(PASS * g + P * t, PASS * g + P * (t + 1))
             for h in range(2):
                 a_bank = bank(f"a_bank{g}{t}{h}", [P, PASS], h + A_BANKS[g][t])
-                nc.tensor.matmul_mx(
-                    out=a_bank[:],
-                    lhsT=wa_codes[g, t].bitcast(FP8X4),
-                    lhsT_scale=wa_sc[:, rows],
-                    rhs=page_q[h][0].bitcast(FP8X4),
-                    rhs_scale=page_q[h][1],
-                    start=True,
-                    stop=True,
-                )
+                multiply(a_bank[:], (wa_codes[g, t], wa_sc[:, rows]), FP8X4, page_q[h], True, True)
                 nc.scalar.copy(out=a_sb[:, PASS * h : PASS * (h + 1)], in_=a_bank[:])
             nc.vector.tensor_copy(at[g][:, t, :], a_sb[:].indirect(idx3[:]))
 
-        b_banks, cal_b = {}, {}
+        b_banks = {}
 
         def project_table(g, quarter, number):
             cols = slice(P * quarter, P * (quarter + 1))
             b_bank = bank(f"b_bank{g}{quarter}", [P, PACK, P], number)
             for a in range(2):
                 for t in range(PACK):
-                    r0 = PASS * g + P * t
-                    nc.tensor.matmul_mx(
-                        out=b_bank[:, t, :],
-                        lhsT=wb_w[:, a, r0 : r0 + P].bitcast(FP4X4),
-                        lhsT_scale=wb_sc[:, a, r0 : r0 + P],
-                        rhs=v_w[a][:, cols].bitcast(FP8X4),
-                        rhs_scale=v_sc[:, a, cols],
-                        start=(a == 0 and t == 0),
-                        stop=(a == 1 and t == PACK - 1),
+                    rows = slice(PASS * g + P * t, PASS * g + P * (t + 1))
+                    multiply(
+                        b_bank[:, t, :],
+                        (wb_w[:, a, rows], wb_sc[:, a, rows]),
+                        FP4X4,
+                        (v_w[a][:, cols], v_sc[:, a, cols]),
+                        a == 0 and t == 0,
+                        a == 1 and t == PACK - 1,
                     )
             b_banks[g, quarter] = b_bank
 
-        def calibrate(g, h, tiles, quarters):
-            for c in quarters:
-                for t in tiles:
-                    nc.scalar.activation(
-                        out=cal_b[g, 2 * h + c][:, t, :],
-                        in_=b_banks[g, 2 * h + c][:, t, :],
-                        func=ACT.Copy,
-                        scale=cal_sb[:, g, t : t + 1],
-                    )
+        cal_b = {}
 
-        x_bf = {}
+        def calibrate(g, quarter):
+            cal_b[g, quarter] = sb([P, PACK, P], F32, f"cal_b{g}{quarter}")
+            for t in range(PACK):
+                nc.scalar.activation(
+                    out=cal_b[g, quarter][:, t, :],
+                    in_=b_banks[g, quarter][:, t, :],
+                    func=ACT.Copy,
+                    scale=cal_sb[:, g, t : t + 1],
+                )
 
-        def compare(engine, kind, g, quarter, first, second, op):
+        def combine(engine, values, first, second, op):
             engine.tensor_tensor(
-                out=x_bf[kind, g, quarter].rearrange(walk_out, e=LINE, t=PACK),
-                in0=first.rearrange(walk_in, e=LINE),
-                in1=second.rearrange(walk_in, e=LINE),
+                out=values.rearrange("p (c e t) -> p c t e", e=LINE, t=PACK),
+                in0=first.rearrange("p t (c e) -> p c t e", e=LINE),
+                in1=second.rearrange("p t (c e) -> p c t e", e=LINE),
                 op=op,
             )
 
-        def values_tile(name, pieces, tag):
-            tile = sb([P, PASS * len(pieces)], BF16, name, tag=tag)
-            for place, piece in enumerate(pieces):
-                x_bf[piece] = tile[:, PASS * place : PASS * (place + 1)]
-            return tile
+        def piece(tile, place, count=1):
+            return tile[:, PASS * place : PASS * (place + count)]
+
+        def picked(g, quarter):
+            return at[g][:, :, P * quarter : P * (quarter + 1)]
+
+        x1_bf = [sb([P, PACK * PAIRS], BF16, f"x1_bf{g}") for g in range(2)]
+        x2_bf = [sb([P, PACK * PAIRS], BF16, "x2_bf0", tag="wp_raw0"), None]
 
         def product(g, quarter):
-            picked = at[g][:, :, P * quarter : P * (quarter + 1)]
-            compare(nc.vector, 1, g, quarter, b_banks[g, quarter][:], picked, ALU.mult)
+            combine(nc.vector, piece(x1_bf[g], quarter), b_banks[g, quarter][:], picked(g, quarter), ALU.mult)
 
-        def difference(engine, target, g, h, tiles, cols, scaled):
-            engine.tensor_tensor(
-                out=target[:, PACK * cols.start : PACK * cols.stop].rearrange(walk_out, e=LINE, t=PACK)[:, :, tiles, :],
-                in0=at[g][:, tiles, HALF * h + cols.start : HALF * h + cols.stop].rearrange(walk_in, e=LINE),
-                in1=scaled[:, tiles, :].rearrange(walk_in, e=LINE),
-                op=ALU.subtract,
-            )
+        def difference(engine, g, quarter):
+            combine(engine, piece(x2_bf[g], quarter), picked(g, quarter), cal_b[g, quarter][:], ALU.subtract)
 
-        cal_half = [sb([P, PACK, HALF], F32, f"cal_b0{h}") for h in range(2)]
-        for quarter in range(4):
-            cal_b[0, quarter] = cal_half[quarter // 2][:, :, P * (quarter % 2) : P * (quarter % 2 + 1)]
-            cal_b[1, quarter] = sb([P, PACK, P], F32, f"cal_b1{quarter}")[:]
-        first_half = slice(0, HALF)
-        low, high, every = slice(0, 2), slice(2, 4), slice(0, 4)
-
-        bf_0 = values_tile("x_bf0", [(kind, 0, q) for kind in (1, 2) for q in range(4)], "x_bf")
-        x2_half = [bf_0[:, (4 + 2 * h) * PASS : (6 + 2 * h) * PASS] for h in range(2)]
         for quarter in range(2):
             project_table(0, quarter, 2 + quarter)
-        for t in range(3):
+        for t in range(PACK):
             project_page(0, t)
         for quarter in range(2, 4):
             project_table(0, quarter, 2 + quarter)
-        calibrate(0, 0, (0, 1), (0, 1))
-        difference(nc.gpsimd, x2_half[0], 0, 0, low, first_half, cal_half[0])
-        project_page(0, 3)
-        calibrate(0, 0, (2, 3), (0, 1))
-        difference(nc.gpsimd, x2_half[0], 0, 0, high, first_half, cal_half[0])
-        for c in range(2):
-            product(0, c)
-        for c in range(2):
-            project_page(1, c)
-            calibrate(0, 1, range(PACK), (c,))
-            cols = slice(P * c, P * (c + 1))
-            difference(nc.gpsimd, x2_half[1], 0, 1, every, cols, cal_b[0, 2 + c])
-            product(0, 2 + c)
-        for t in range(2, PACK):
-            project_page(1, t)
+        calibrate(0, 0)
+        difference(nc.gpsimd, 0, 0)
+        product(0, 0)
+        product(0, 1)
+        project_page(1, 0)
+        calibrate(0, 1)
+        difference(nc.gpsimd, 0, 1)
+        product(0, 2)
+        project_page(1, 1)
+        calibrate(0, 2)
+        difference(nc.gpsimd, 0, 2)
+        product(0, 3)
+        project_page(1, 2)
+        calibrate(0, 3)
+        difference(nc.gpsimd, 0, 3)
+        project_page(1, 3)
+        wp_bf1 = sb([P, N, PACK], BF16, "wp_bf1", tag="a_sb11")
+        nc.scalar.copy(
+            out=wp_bf1[:].rearrange("p (c e) i -> p c i e", e=2),
+            in_=wp_raw[1][:].rearrange("p i (c e) -> p c i e", e=2),
+        )
         for quarter, number in enumerate((6, 7, 0, 1)):
             project_table(1, quarter, number)
-        for h in range(2):
-            calibrate(1, h, range(PACK), (0, 1))
-        wp_bf1 = [round_wp_piece(part, f"cal_b0{part}") for part in range(2)]
-        early_sc = sb([P, 3 * PAIRS], U8, "early_sc", tag="a_sb7")
-        x2_0 = quantise("x2_codes0", bf_0[:, 4 * PASS :], early_sc[:, N + PAIRS :])
-        wp_0 = quantise("wp_codes0", wp_bf0[:], early_sc[:, 0:N])
-        x1_0 = quantise("x1_codes0", bf_0[:, 0 : 4 * PASS], early_sc[:, N : N + PAIRS])
+            calibrate(1, quarter)
+        product(1, 0)
 
-        bf_10 = values_tile("x_bf10", [(kind, 1, c) for kind in (1, 2) for c in range(2)], "x_bf")
-        last_bf = values_tile("last_bf", [(1, 1, 2), (2, 1, 2), (1, 1, 3), (2, 1, 3)], "wb_raw")
-        difference(nc.gpsimd, bf_10[:, 2 * PASS :], 1, 0, every, slice(0, P), cal_b[1, 0])
-        for quarter in range(3):
-            product(1, quarter)
-        difference(nc.vector, bf_10[:, 2 * PASS :], 1, 0, every, slice(P, HALF), cal_b[1, 1])
+        def quarter_cols(quarter, count=1):
+            return slice(P * quarter, P * (quarter + count))
 
-        y_half = [bank(f"y_half{w}", [P, 2, HALF], number) for w, number in enumerate((7, 0))]
-        y_third = bank("y_third", [P, N // P, P], 2)
-        y_last = [bank(f"y_last{w}", [P, 2, P], number) for w, number in enumerate((3, 4))]
-
-        def accumulate(targets, weights, x, cols, first, last, first_u=0):
-            w_codes, w_sc = weights
-            codes, scales = x
-            for u, (target, opens, closes) in enumerate(targets, first_u):
-                n_cols = slice(P * u, P * (u + 1))
-                nc.tensor.matmul_mx(
-                    out=target,
-                    lhsT=w_codes[:, n_cols].bitcast(FP8X4),
-                    lhsT_scale=w_sc[:, n_cols],
-                    rhs=codes[:, cols].bitcast(FP8X4),
-                    rhs_scale=scales[:, cols],
-                    start=(first and opens),
-                    stop=(last and closes),
-                )
-
-        half_targets = [(y_half[u // 2][:, u % 2, :], u % 2 == 0, u % 2 == 1) for u in range(4)]
-        quarter_targets = [
-            [(y_third[:, u, :], u == 0, u == 3) for u in range(4)],
-            [(y_last[u // 2][:, u % 2, :], u % 2 == 0, u % 2 == 1) for u in range(4)],
+        early_sc = sb([P, 5, PAIRS], U8, "early_sc", tag="a_sb13")
+        x2_0 = quantise(sb([P, PAIRS], U32, "x2_codes0")[:], early_sc[:, 0, :], x2_bf[0][:])
+        wp_q = [
+            quantise(sb([P, N], U32, f"wp_codes{g}")[:], early_sc[:, 1 + g, :], values[:].rearrange("p c i -> p (c i)"))
+            for g, values in enumerate((wp_bf0, wp_bf1))
         ]
-        wd_pass = [(wd_w[:, g, :], wd_sc[4 * g : P, :]) for g in range(2)]
+        x1_1 = (sb([P, PAIRS], U32, "x1_codes1")[:], early_sc[:, 4, :])
+        x2_1 = (sb([P, PAIRS], U32, "x2_codes1")[:], sb([P, PAIRS], U8, "x2_sc1")[:])
 
-        def add_bias(result, target, u):
-            nc.scalar.activation(out=result, in_=target, func=ACT.Identity, bias=bo_sb[:, u : u + 1], scale=1.0)
+        def quantise_quarters(x, values, quarter, count=1):
+            quantise(*columns(x, quarter_cols(quarter, count)), piece(values, quarter, count))
 
-        second_half = slice(HALF, PAIRS)
-        for weights, x, first in ((wd_pass[0], x2_0, True), (wp_0, x1_0, False)):
-            for c in range(2):
-                accumulate(quarter_targets[c], weights, x, slice(HALF + P * c, HALF + P * (c + 1)), first, False)
-        for w in range(2):
-            for weights, x, first in ((wd_pass[0], x2_0, True), (wp_0, x1_0, False)):
-                accumulate(half_targets[2 * w : 2 * w + 2], weights, x, first_half, first, False, 2 * w)
+        quantise_quarters(x1_1, x1_bf[1], 0)
+        x1_0 = quantise(sb([P, PAIRS], U32, "x1_codes0")[:], early_sc[:, 3, :], x1_bf[0][:])
 
-        late_sc = sb([P, 4, PAIRS], U8, "late_sc", tag="cal_b10")
-        wp_codes1 = sb([P, N], U32, "wp_codes1")
-        for part in range(2):
-            cols = slice(HALF * part, HALF * (part + 1))
-            nc.vector.quantize_mx(out=wp_codes1[:, cols].bitcast(FP8X4), scales=late_sc[:, 0, cols], in_=wp_bf1[part][:])
-        wp_1 = (wp_codes1, late_sc[:, 0, :])
-        x_10 = quantise("x_codes10", bf_10[:], late_sc[:, 1, :])
-        accumulate(half_targets, wp_1, x_10, first_half, False, False)
-        accumulate(half_targets, wd_pass[1], x_10, second_half, False, True)
-        for w in range(2):
-            result = sb([P, 2, HALF], F32, f"result_half{w}")
-            for e in range(2):
-                add_bias(result[:, e, :], y_half[w][:, e, :], 2 * w + e)
-            nc.sync.dma_start(out=out_rows[:, 2 * w : 2 * w + 2, first_half], in_=result[:])
-        difference(nc.vector, last_bf[:, PASS:], 1, 1, every, slice(0, P), cal_b[1, 2])
-        product(1, 3)
-        three = quantise("x_codes_three", last_bf[:, 0 : 2 * PASS], late_sc[:, 3, 0:HALF])
-        x1_last = quantise("x1_codes_last", last_bf[:, 2 * PASS : 3 * PASS], late_sc[:, 3, HALF : HALF + P])
-        difference(nc.vector, last_bf[:, 2 * PASS :], 1, 1, every, slice(P, HALF), cal_b[1, 3])
-        x2_last = quantise("x2_codes_last", last_bf[:, 3 * PASS :], late_sc[:, 3, HALF + P :])
-        accumulate(quarter_targets[0], wp_1, three, slice(0, P), False, False)
-        accumulate(quarter_targets[0], wd_pass[1], three, slice(P, 2 * P), False, True)
-        accumulate(quarter_targets[1], wp_1, x1_last, slice(0, P), False, False)
-        accumulate(quarter_targets[1], wd_pass[1], x2_last, slice(0, P), False, True)
-        result = sb([P, N // P, P], F32, "result_third")
-        for u in range(N // P):
-            add_bias(result[:, u, :], y_third[:, u, :], u)
-        nc.sync.dma_start(out=out_rows[:, :, HALF : HALF + P], in_=result[:])
-        for w in range(2):
-            result = sb([P, 2, P], F32, f"result_last{w}")
-            if w == 0:
-                bias = bo_sb[:, 0:2].unsqueeze(2).to_broadcast([P, 2, P])
-                nc.vector.tensor_tensor(out=result[:], in0=y_last[0][:], in1=bias, op=ALU.add)
+
+        out_rows = out.rearrange("(u p) j -> p u j", p=P)
+        y_banks = [bank(f"y{quarter}", [P, N // P, P], 2 + quarter) for quarter in range(3)]
+        y_last = [bank(f"y_last{w}", [P, 2, P], 5 + w) for w in range(2)]
+        targets = [[(u, y[:, u, :], u == 0, u == 3) for u in range(4)] for y in y_banks]
+        targets.append([(u, y_last[u // 2][:, u % 2, :], u % 2 == 0, u % 2 == 1) for u in range(4)])
+        wd_q = [(wd_w[:, g, :], wd_sc[4 * g : P, :]) for g in range(2)]
+
+        def accumulate(quarter, weights, x, first=False, final=False):
+            for u, target, opens, closes in targets[quarter]:
+                stationary = columns(weights, slice(P * u, P * (u + 1)))
+                multiply(target, stationary, FP8X4, columns(x, quarter_cols(quarter)), first and opens, final and closes)
+
+        for quarter in range(4):
+            accumulate(quarter, wd_q[0], x2_0, first=True)
+        for quarter in range(4):
+            accumulate(quarter, wp_q[0], x1_0)
+        accumulate(0, wp_q[1], x1_1)
+
+        def finish(quarter, w, on_vector=False):
+            result = sb([P, 2, P], F32, f"result{quarter}{w}")
+            if on_vector:
+                bias = bo_sb[:, 2 * w : 2 * w + 2].unsqueeze(2).to_broadcast([P, 2, P])
+                nc.vector.tensor_tensor(out=result[:], in0=y_last[w][:], in1=bias, op=ALU.add)
             else:
-                for e in range(2):
-                    add_bias(result[:, e, :], y_last[1][:, e, :], 2 + e)
-            nc.sync.dma_start(out=out_rows[:, 2 * w : 2 * w + 2, HALF + P :], in_=result[:])
+                for u, target, opens, closes in targets[quarter][2 * w : 2 * w + 2]:
+                    nc.scalar.activation(
+                        out=result[:, u % 2, :], in_=target, func=ACT.Identity, bias=bo_sb[:, u : u + 1], scale=1.0
+                    )
+            nc.sync.dma_start(out=out_rows[:, 2 * w : 2 * w + 2, quarter_cols(quarter)], in_=result[:])
+
+        def close(quarter):
+            quantise_quarters(x2_1, x2_bf[1], quarter)
+            accumulate(quarter, wd_q[1], x2_1, final=True)
+            for w in range(2):
+                finish(quarter, w, on_vector=(quarter, w) == (3, 0))
+
+        x2_bf[1] = sb([P, PACK * PAIRS], BF16, "x2_bf1", tag="x1_bf0")
+        difference(nc.gpsimd, 1, 0)
+        for quarter in range(1, 4):
+            product(1, quarter)
+        close(0)
+        difference(nc.vector, 1, 1)
+        quantise_quarters(x1_1, x1_bf[1], 1)
+        accumulate(1, wp_q[1], x1_1)
+        close(1)
+        difference(nc.vector, 1, 2)
+        quantise_quarters(x1_1, x1_bf[1], 2, 2)
+        accumulate(2, wp_q[1], x1_1)
+        close(2)
+        accumulate(3, wp_q[1], x1_1)
+        difference(nc.vector, 1, 3)
+        close(3)

@@ -82,7 +82,6 @@ def tile_list_sonobuoy_bearing_pairs_kernel(
                 in_=wb_scales[:, 4 * quadrant : 4 * quadrant + 4, :].rearrange("a r c -> r a c").bitcast(I32),
             )
         load_wa(0)
-        nc.sync.dma_start(out=wb_raw[0][:].bitcast(I32), in_=wb_words[0].bitcast(I32))
         load_page_rows(1)
         load_wa(1)
         load_page_rows(2)
@@ -95,12 +94,13 @@ def tile_list_sonobuoy_bearing_pairs_kernel(
                 in_=picked_sc[96 + 8 * quadrant : 96 + 8 * quadrant + 8, :].bitcast(I32),
             )
 
-        nc.sync.dma_start(out=wb_raw[1][:].bitcast(I32), in_=wb_words[1].bitcast(I32))
+        nc.sync.dma_start(out=wb_raw[0][:].bitcast(I32), in_=wb_words[0].bitcast(I32))
         load_wa(2)
         load_page_rows(3)
         for a in range(2):
             nc.sync.dma_start(out=tab_w[a][:], in_=tab_words[a].rearrange("p t i -> p (t i)").bitcast(I32))
         load_wa(3)
+        nc.sync.dma_start(out=wb_raw[1][:].bitcast(I32), in_=wb_words[1].bitcast(I32))
         nc.sync.dma_start(idx3[:], offs3)
         nc.sync.dma_start(out=cal_sb[:], in_=cal.rearrange("(g p t) -> p g t", g=2, t=PACK))
         for g in range(2):
@@ -124,12 +124,16 @@ def tile_list_sonobuoy_bearing_pairs_kernel(
             out=wb_sc[:].rearrange("p a (g t c) -> p (a g) t c", g=2, t=PACK),
             in_=wb_sc_raw[:].rearrange("p a (g c t) -> p (a g) t c", g=2, t=PACK),
         )
-        wb_w = sb([P, 2, H], U16, "wb_w")
-        for a in range(2):
+        wb_w = []
+
+        def reorder_wb(a, tag):
+            wb_w.append(sb([P, H], U16, f"wb_w{a}", tag=tag))
             nc.gpsimd.tensor_copy(
-                out=wb_w[:, a, :].rearrange("p (g t c e) -> p g c t e", g=2, t=PACK, e=8),
+                out=wb_w[a][:].rearrange("p (g t c e) -> p g c t e", g=2, t=PACK, e=8),
                 in_=wb_raw[a][:].rearrange("p (g c e t) -> p g c t e", g=2, t=PACK, e=8),
             )
+
+        reorder_wb(0, None)
 
         wa_bf = sb([P, 2, PACK, P, PACK], BF16, "wa_bf")
 
@@ -195,7 +199,8 @@ def tile_list_sonobuoy_bearing_pairs_kernel(
         def columns(operand, cols):
             return operand[0][:, cols], operand[1][:, cols]
 
-        wp_bf0 = sb([P, N, PACK], BF16, "wp_bf0", tag="wa_bf")
+        reorder_wb(1, "wa_bf")
+        wp_bf0 = sb([P, N, PACK], BF16, "wp_bf0", tag="wb_raw1")
         round_on_gpsimd(wp_bf0[:], wp_raw[0][:].rearrange("p i c -> p c i"))
 
         at = [sb([P, PACK, PAIRS], F32, f"at{g}") for g in range(2)]
@@ -219,7 +224,7 @@ def tile_list_sonobuoy_bearing_pairs_kernel(
                     rows = slice(PASS * g + P * t, PASS * g + P * (t + 1))
                     multiply(
                         b_bank[:, t, :],
-                        (wb_w[:, a, rows], wb_sc[:, a, rows]),
+                        (wb_w[a][:, rows], wb_sc[:, a, rows]),
                         FP4X4,
                         (v_w[a][:, cols], v_sc[:, a, cols]),
                         a == 0 and t == 0,

@@ -212,7 +212,9 @@ def tile_list_sonobuoy_bearing_pairs_kernel(
                 a_bank = bank(f"a_bank{g}{t}{h}", [P, PASS], h + A_BANKS[g][t])
                 multiply(a_bank[:], (wa_codes[g, t], wa_sc[:, rows]), FP8X4, page_q[h], True, True)
                 nc.scalar.copy(out=a_sb[:, PASS * h : PASS * (h + 1)], in_=a_bank[:])
-            nc.vector.tensor_copy(at[g][:, t, :], a_sb[:].indirect(idx3[:]))
+            for cols in (slice(0, P), slice(P, PAIRS)) if (g, t) == (0, PACK - 1) else (slice(0, PAIRS),):
+                offsets = idx3[:, cols.start // 16 : cols.stop // 16]
+                nc.vector.tensor_copy(at[g][:, t, cols], a_sb[:].indirect(offsets))
 
         b_banks = {}
 
@@ -289,32 +291,32 @@ def tile_list_sonobuoy_bearing_pairs_kernel(
         calibrate(0, 3)
         difference(nc.gpsimd, 0, 3)
         project_page(1, 3)
-        wp_bf1 = sb([P, N, PACK], BF16, "wp_bf1", tag="a_sb11")
+        for quarter, number in enumerate((6, 7, 0, 1)):
+            project_table(1, quarter, number)
+            calibrate(1, quarter)
+        wp_bf1 = sb([P, N, PACK], BF16, "wp_bf1", tag="a_sb12")
         nc.scalar.copy(
             out=wp_bf1[:].rearrange("p (c e) i -> p c i e", e=2),
             in_=wp_raw[1][:].rearrange("p i (c e) -> p c i e", e=2),
         )
-        for quarter, number in enumerate((6, 7, 0, 1)):
-            project_table(1, quarter, number)
-            calibrate(1, quarter)
-        product(1, 0)
 
         def quarter_cols(quarter, count=1):
             return slice(P * quarter, P * (quarter + count))
 
         early_sc = sb([P, 5, PAIRS], U8, "early_sc", tag="a_sb13")
         x2_0 = quantise(sb([P, PAIRS], U32, "x2_codes0")[:], early_sc[:, 0, :], x2_bf[0][:])
-        wp_q = [
-            quantise(sb([P, N], U32, f"wp_codes{g}")[:], early_sc[:, 1 + g, :], values[:].rearrange("p c i -> p (c i)"))
-            for g, values in enumerate((wp_bf0, wp_bf1))
-        ]
+
+        def quantise_wp(g, values):
+            codes = sb([P, N], U32, f"wp_codes{g}")
+            return quantise(codes[:], early_sc[:, 1 + g, :], values[:].rearrange("p c i -> p (c i)"))
+
+        wp_q = [quantise_wp(0, wp_bf0)]
         x1_1 = (sb([P, PAIRS], U32, "x1_codes1")[:], early_sc[:, 4, :])
         x2_1 = (sb([P, PAIRS], U32, "x2_codes1")[:], sb([P, PAIRS], U8, "x2_sc1")[:])
 
         def quantise_quarters(x, values, quarter, count=1):
             quantise(*columns(x, quarter_cols(quarter, count)), piece(values, quarter, count))
 
-        quantise_quarters(x1_1, x1_bf[1], 0)
         x1_0 = quantise(sb([P, PAIRS], U32, "x1_codes0")[:], early_sc[:, 3, :], x1_bf[0][:])
 
 
@@ -334,7 +336,6 @@ def tile_list_sonobuoy_bearing_pairs_kernel(
             accumulate(quarter, wd_q[0], x2_0, first=True)
         for quarter in range(4):
             accumulate(quarter, wp_q[0], x1_0)
-        accumulate(0, wp_q[1], x1_1)
 
         def finish(quarter, w, on_vector=False):
             result = sb([P, 2, P], F32, f"result{quarter}{w}")
@@ -356,14 +357,19 @@ def tile_list_sonobuoy_bearing_pairs_kernel(
 
         x2_bf[1] = sb([P, PACK * PAIRS], BF16, "x2_bf1", tag="x1_bf0")
         difference(nc.gpsimd, 1, 0)
-        for quarter in range(1, 4):
+        for quarter in range(4):
             product(1, quarter)
-        close(0)
+        quantise_quarters(x2_1, x2_bf[1], 0)
+        accumulate(0, wd_q[1], x2_1)
+        quantise_quarters(x1_1, x1_bf[1], 0, 2)
+        wp_q.append(quantise_wp(1, wp_bf1))
+        accumulate(0, wp_q[1], x1_1, final=True)
+        for w in range(2):
+            finish(0, w)
         difference(nc.vector, 1, 1)
-        quantise_quarters(x1_1, x1_bf[1], 1)
         accumulate(1, wp_q[1], x1_1)
-        close(1)
         difference(nc.vector, 1, 2)
+        close(1)
         quantise_quarters(x1_1, x1_bf[1], 2, 2)
         accumulate(2, wp_q[1], x1_1)
         close(2)

@@ -1,6 +1,7 @@
 from contextlib import ExitStack
 
 import concourse.mybir as mybir
+from concourse.masks import make_identity
 
 K, T, S, K2, T2, H, N = 1024, 2048, 512, 512, 1024, 1024, 512
 PAIRS = 512
@@ -20,10 +21,13 @@ ACT = mybir.ActivationFunctionType
 P = 128
 PACK = 4
 PASS = P * PACK
-HALF = PAIRS // 2
-A_BANKS = ((4, 6, 0, 6), (0, 0, 0, 0))
-WA_PIECES = tuple(slice(HALF * n, HALF * (n + 1)) for n in range(4))
+WA_QUARTER = H // 4
 LINE = 4
+SCALE_ROWS_AT = 96
+A_BANKS = ((4, 6, 0, 6), (0, 6, 0, 6))
+B_BANKS = ((2, 3, 4, 5), (2, 3, 6, 7))
+Y_BANKS, Y_LAST_BANKS = (4, 5, 1), (2, 3)
+TURNED, TURN_BANK = 2, 0
 
 
 def tile_list_sonobuoy_bearing_pairs_kernel(
@@ -45,7 +49,7 @@ def tile_list_sonobuoy_bearing_pairs_kernel(
         idx3 = keep.tile([P, PAIRS // 16], U16, name="idx3")
 
         tab_sc = sb([P, T], U8, "tab_sc")
-        nc.vector.memset(tab_sc[0:96, :].bitcast(I32), 0)
+        nc.vector.memset(tab_sc[0:SCALE_ROWS_AT, :].bitcast(I32), 0)
         wb_sc_raw = sb([P, 2, H], U8, "wb_sc_raw")
         v_sc = sb([P, 2, PAIRS], U8, "v_sc")
         wd_sc = sb([P, N], U8, "wd_sc")
@@ -57,7 +61,7 @@ def tile_list_sonobuoy_bearing_pairs_kernel(
         wa_rows = wa.rearrange("(p i) r -> p i r", i=PACK)
         page = [sb([P, T2], F32, f"page{i}") for i in range(PACK)]
         incoming = [sb([P, S], F32, f"incoming{i}") for i in range(PACK)]
-        wa_raw = [sb([P, PACK, r.stop - r.start], F32, f"wa_raw{n}") for n, r in enumerate(WA_PIECES)]
+        wa_raw = [sb([P, PACK, WA_QUARTER], F32, f"wa_raw{n}") for n in range(4)]
         wp_raw = [sb([P, PACK, N], F32, f"wp_raw{g}") for g in range(2)]
         tab_w = [sb([P, T], I32, f"tab_w{a}") for a in range(2)]
         wb_raw = [sb([P, H], U16, f"wb_raw{a}") for a in range(2)]
@@ -70,9 +74,14 @@ def tile_list_sonobuoy_bearing_pairs_kernel(
             nc.sync.dma_start(out=incoming[i][:], in_=xs_rows[:, i, :])
 
         def load_wa(n):
-            nc.sync.dma_start(out=wa_raw[n][:], in_=wa_rows[:, :, WA_PIECES[n]])
+            nc.sync.dma_start(out=wa_raw[n][:], in_=wa_rows[:, :, WA_QUARTER * n : WA_QUARTER * (n + 1)])
 
-        nc.sync.dma_start(out=tab_sc[96:P, :].bitcast(I32), in_=tab_scales.rearrange("a q t -> q a t").bitcast(I32))
+        def load_wb(a):
+            nc.sync.dma_start(out=wb_raw[a][:].bitcast(I32), in_=wb_words[a].bitcast(I32))
+
+        nc.sync.dma_start(
+            out=tab_sc[SCALE_ROWS_AT:P, :].bitcast(I32), in_=tab_scales.rearrange("a q t -> q a t").bitcast(I32)
+        )
         nc.sync.dma_start(idx[:], offs)
         nc.sync.dma_start(idx2[:], offs2)
         load_page_rows(0)
@@ -89,18 +98,19 @@ def tile_list_sonobuoy_bearing_pairs_kernel(
         picked_sc = sb([P, PAIRS], U8, "picked_sc")
         nc.vector.tensor_copy(picked_sc[:], tab_sc[:].indirect(idx[:]))
         for quadrant in range(4):
+            first = SCALE_ROWS_AT + 8 * quadrant
             nc.sync.dma_start(
                 out=v_sc[32 * quadrant : 32 * quadrant + 4, :, :].bitcast(I32),
-                in_=picked_sc[96 + 8 * quadrant : 96 + 8 * quadrant + 8, :].bitcast(I32),
+                in_=picked_sc[first : first + 8, :].bitcast(I32),
             )
 
-        nc.sync.dma_start(out=wb_raw[0][:].bitcast(I32), in_=wb_words[0].bitcast(I32))
+        load_wb(0)
         load_wa(2)
         load_page_rows(3)
         for a in range(2):
             nc.sync.dma_start(out=tab_w[a][:], in_=tab_words[a].rearrange("p t i -> p (t i)").bitcast(I32))
         load_wa(3)
-        nc.sync.dma_start(out=wb_raw[1][:].bitcast(I32), in_=wb_words[1].bitcast(I32))
+        load_wb(1)
         nc.sync.dma_start(idx3[:], offs3)
         nc.sync.dma_start(out=cal_sb[:], in_=cal.rearrange("(g p t) -> p g t", g=2, t=PACK))
         for g in range(2):
@@ -118,6 +128,9 @@ def tile_list_sonobuoy_bearing_pairs_kernel(
 
         def round_on_gpsimd(target, source):
             nc.gpsimd.tensor_scalar(out=target, in0=source, scalar1=1.0, scalar2=0.0, op0=ALU.mult, op1=ALU.add)
+
+        identity = sb([P, P], F32, "identity")
+        make_identity(nc, identity[:])
 
         wb_sc = sb([P, 2, H], U8, "wb_sc")
         nc.gpsimd.tensor_copy(
@@ -138,10 +151,9 @@ def tile_list_sonobuoy_bearing_pairs_kernel(
         wa_bf = sb([P, 2, PACK, P, PACK], BF16, "wa_bf")
 
         def round_wa(n):
-            g, first = divmod(WA_PIECES[n].start, PASS)
-            width = WA_PIECES[n].stop - WA_PIECES[n].start
+            g, part = divmod(n, 2)
             nc.scalar.copy(
-                out=wa_bf[:, g, :, first // PACK : (first + width) // PACK, :].rearrange("p t c i -> p c i t"),
+                out=wa_bf[:, g, :, (P // 2) * part : (P // 2) * (part + 1), :].rearrange("p t c i -> p c i t"),
                 in_=wa_raw[n][:].rearrange("p i (c t) -> p c i t", t=PACK),
             )
 
@@ -151,15 +163,7 @@ def tile_list_sonobuoy_bearing_pairs_kernel(
             nc.vector.quantize_mx(out=codes.bitcast(FP8X4), scales=scales, in_=values)
             return codes, scales
 
-        wa_codes = {}
-
-        def quantise_wa(g, tiles, codes):
-            rows = slice(PASS * g + P * tiles.start, PASS * g + P * tiles.stop)
-            quantise(codes, wa_sc[:, rows], wa_bf[:, g, tiles].rearrange("p t c i -> p (t c i)"))
-            for t in range(tiles.start, tiles.stop):
-                wa_codes[g, t] = codes[:, P * (t - tiles.start) : P * (t - tiles.start + 1)]
-
-        page_bf = [sb([P, PASS, PACK], BF16, f"page_bf{h}", tag=("page_bf0", "wb_sc_raw")[h]) for h in range(2)]
+        page_bf = [sb([P, PASS, PACK], BF16, "page_bf0"), sb([P, PASS, PACK], BF16, "page_bf1", tag="wb_sc_raw")]
         for i in range(PACK):
             nc.vector.tensor_copy(page[i][:].indirect(idx2[:]), incoming[i][:])
             nc.scalar.copy(out=page_bf[0][:, :, i], in_=page[i][:, 0:PASS])
@@ -167,23 +171,25 @@ def tile_list_sonobuoy_bearing_pairs_kernel(
             round_wa(i)
 
         v_w = [sb([P, PAIRS], U32, f"v_w{a}") for a in range(2)]
-
-        def pick_words(a):
+        for a in range(2):
             nc.vector.tensor_copy(v_w[a][:], tab_w[a][:].bitcast(U32).indirect(idx[:]))
 
-        for a in range(2):
-            pick_words(a)
-
-        late_codes = sb([P, T2 + H], U32, "late_codes", tag="tab_w1")
+        first_codes = sb([P, T2 + H], U32, "first_codes", tag="tab_w1")
         page_sc = sb([P, T2], U8, "page_sc")
+
+        def quantise_wa(g, tiles):
+            rows = slice(PASS * g + P * tiles.start, PASS * g + P * tiles.stop)
+            values = wa_bf[:, g, tiles].rearrange("p t c i -> p (t c i)")
+            quantise(first_codes[:, T2 + rows.start : T2 + rows.stop], wa_sc[:, rows], values)
+
+        quantise_wa(0, slice(0, 1))
         page_q = []
-        quantise_wa(0, slice(0, 1), late_codes[:, T2 : T2 + P])
         for h in range(2):
             cols = slice(PASS * h, PASS * (h + 1))
-            page_q.append(quantise(late_codes[:, cols], page_sc[:, cols], page_bf[h][:].rearrange("p c i -> p (c i)")))
+            page_q.append(quantise(first_codes[:, cols], page_sc[:, cols], page_bf[h][:].rearrange("p c i -> p (c i)")))
         for g, tiles in ((0, slice(1, 3)), (0, slice(3, 4)), (1, slice(0, 4))):
-            first = T2 + PASS * g + P * tiles.start
-            quantise_wa(g, tiles, late_codes[:, first : first + P * (tiles.stop - tiles.start)])
+            quantise_wa(g, tiles)
+        wa_q = (first_codes[:, T2:], wa_sc[:])
 
         def multiply(target, stationary, dtype, moving, start, stop):
             nc.tensor.matmul_mx(
@@ -199,6 +205,12 @@ def tile_list_sonobuoy_bearing_pairs_kernel(
         def columns(operand, cols):
             return operand[0][:, cols], operand[1][:, cols]
 
+        def quarter_cols(quarter, count=1):
+            return slice(P * quarter, P * (quarter + count))
+
+        def tile_rows(g, t):
+            return slice(PASS * g + P * t, PASS * g + P * (t + 1))
+
         reorder_wb(1, "wa_bf")
         wp_bf0 = sb([P, N, PACK], BF16, "wp_bf0", tag="wb_raw1")
         round_on_gpsimd(wp_bf0[:], wp_raw[0][:].rearrange("p i c -> p c i"))
@@ -207,26 +219,25 @@ def tile_list_sonobuoy_bearing_pairs_kernel(
 
         def project_page(g, t):
             a_sb = sb([P, T2], F32, f"a_sb{g}{t}")
-            rows = slice(PASS * g + P * t, PASS * g + P * (t + 1))
             for h in range(2):
                 a_bank = bank(f"a_bank{g}{t}{h}", [P, PASS], h + A_BANKS[g][t])
-                multiply(a_bank[:], (wa_codes[g, t], wa_sc[:, rows]), FP8X4, page_q[h], True, True)
+                multiply(a_bank[:], columns(wa_q, tile_rows(g, t)), FP8X4, page_q[h], True, True)
                 nc.scalar.copy(out=a_sb[:, PASS * h : PASS * (h + 1)], in_=a_bank[:])
-            for cols in (slice(0, P), slice(P, PAIRS)) if (g, t) == (0, PACK - 1) else (slice(0, PAIRS),):
+            last_of_group_0 = (g, t) == (0, PACK - 1)
+            for cols in (quarter_cols(0), quarter_cols(1, 3)) if last_of_group_0 else (quarter_cols(0, 4),):
                 offsets = idx3[:, cols.start // 16 : cols.stop // 16]
                 nc.vector.tensor_copy(at[g][:, t, cols], a_sb[:].indirect(offsets))
 
         b_banks = {}
 
-        def project_table(g, quarter, number):
-            cols = slice(P * quarter, P * (quarter + 1))
-            b_bank = bank(f"b_bank{g}{quarter}", [P, PACK, P], number)
+        def project_table(g, quarter):
+            cols = quarter_cols(quarter)
+            b_bank = bank(f"b_bank{g}{quarter}", [P, PACK, P], B_BANKS[g][quarter])
             for a in range(2):
                 for t in range(PACK):
-                    rows = slice(PASS * g + P * t, PASS * g + P * (t + 1))
                     multiply(
                         b_bank[:, t, :],
-                        (wb_w[a][:, rows], wb_sc[:, a, rows]),
+                        columns((wb_w[a][:], wb_sc[:, a, :]), tile_rows(g, t)),
                         FP4X4,
                         (v_w[a][:, cols], v_sc[:, a, cols]),
                         a == 0 and t == 0,
@@ -236,14 +247,14 @@ def tile_list_sonobuoy_bearing_pairs_kernel(
 
         cal_b = {}
 
-        def calibrate(g, quarter):
+        def calibrate(g, quarter, gains):
             cal_b[g, quarter] = sb([P, PACK, P], F32, f"cal_b{g}{quarter}")
             for t in range(PACK):
                 nc.scalar.activation(
                     out=cal_b[g, quarter][:, t, :],
                     in_=b_banks[g, quarter][:, t, :],
                     func=ACT.Copy,
-                    scale=cal_sb[:, g, t : t + 1],
+                    scale=gains[:, t : t + 1],
                 )
 
         def combine(engine, values, first, second, op):
@@ -254,75 +265,82 @@ def tile_list_sonobuoy_bearing_pairs_kernel(
                 op=op,
             )
 
-        def piece(tile, place, count=1):
-            return tile[:, PASS * place : PASS * (place + count)]
-
-        def picked(g, quarter):
-            return at[g][:, :, P * quarter : P * (quarter + 1)]
+        def values_of(tile, quarter, count=1):
+            return tile[:, PASS * quarter : PASS * (quarter + count)]
 
         x1_bf = [sb([P, PACK * PAIRS], BF16, f"x1_bf{g}") for g in range(2)]
-        x2_bf = [sb([P, PACK * PAIRS], BF16, "x2_bf0", tag="wp_raw0"), None]
+        x2_bf = [sb([P, PACK * PAIRS], BF16, "x2_bf0", tag="wp_raw0")]
 
         def product(g, quarter):
-            combine(nc.vector, piece(x1_bf[g], quarter), b_banks[g, quarter][:], picked(g, quarter), ALU.mult)
+            picked = at[g][:, :, quarter_cols(quarter)]
+            combine(nc.vector, values_of(x1_bf[g], quarter), b_banks[g, quarter][:], picked, ALU.mult)
 
         def difference(engine, g, quarter):
-            combine(engine, piece(x2_bf[g], quarter), picked(g, quarter), cal_b[g, quarter][:], ALU.subtract)
+            picked = at[g][:, :, quarter_cols(quarter)]
+            combine(engine, values_of(x2_bf[g], quarter), picked, cal_b[g, quarter][:], ALU.subtract)
 
         for quarter in range(2):
-            project_table(0, quarter, 2 + quarter)
+            project_table(0, quarter)
         for t in range(PACK):
             project_page(0, t)
         for quarter in range(2, 4):
-            project_table(0, quarter, 2 + quarter)
-        calibrate(0, 0)
-        difference(nc.gpsimd, 0, 0)
-        product(0, 0)
-        product(0, 1)
-        project_page(1, 0)
-        calibrate(0, 1)
-        difference(nc.gpsimd, 0, 1)
-        product(0, 2)
-        project_page(1, 1)
-        calibrate(0, 2)
-        difference(nc.gpsimd, 0, 2)
-        product(0, 3)
-        project_page(1, 2)
-        calibrate(0, 3)
-        difference(nc.gpsimd, 0, 3)
-        project_page(1, 3)
-        for quarter, number in enumerate((6, 7, 0, 1)):
-            project_table(1, quarter, number)
-            calibrate(1, quarter)
+            project_table(0, quarter)
+        for step, products in enumerate(((0, 1), (2,), (3,), ())):
+            calibrate(0, step, cal_sb[:, 0, :])
+            difference(nc.gpsimd, 0, step)
+            for quarter in products:
+                product(0, quarter)
+            project_page(1, step)
+        minus_cal = sb([P, PACK], F32, "minus_cal")
+        nc.scalar.activation(out=minus_cal[:], in_=cal_sb[:, 1, :], func=ACT.Copy, scale=-1.0)
+        for quarter in range(4):
+            project_table(1, quarter)
+            calibrate(1, quarter, minus_cal[:] if quarter == TURNED else cal_sb[:, 1, :])
+
+        turned = bank("turned", [P, PACK, P], TURN_BANK)
+        sources = (at[1][:, :, quarter_cols(TURNED)], cal_b[1, TURNED][:])
+        for place, source in enumerate(sources):
+            for t in range(PACK):
+                nc.tensor.matmul(
+                    turned[:, t, :],
+                    source[:, t, :],
+                    identity[:],
+                    start=(place, t) == (0, 0),
+                    stop=(place, t) == (1, PACK - 1),
+                    is_transpose=True,
+                )
         wp_bf1 = sb([P, N, PACK], BF16, "wp_bf1", tag="a_sb12")
         nc.scalar.copy(
             out=wp_bf1[:].rearrange("p (c e) i -> p c i e", e=2),
             in_=wp_raw[1][:].rearrange("p i (c e) -> p c i e", e=2),
         )
+        turned_bf = sb([P, 2, P, 2], BF16, "turned_bf")
+        nc.scalar.copy(out=turned_bf[:], in_=turned[:].rearrange("j (w e) p -> j w p e", e=2))
+        turned_words = turned_bf[:].rearrange("j w p e -> j (w p e)").bitcast(F32)
+        back = bank("back", [P, 2, P], TURN_BANK)
+        for w in range(2):
+            nc.tensor.transpose(back[:, w, :], turned_words[:, P * w : P * (w + 1)], identity[:])
+        x2_turned = sb([P, P, 2], F32, "x2_turned")
+        nc.scalar.copy(out=x2_turned[:], in_=back[:].rearrange("p w j -> p j w"))
 
-        def quarter_cols(quarter, count=1):
-            return slice(P * quarter, P * (quarter + count))
-
-        early_sc = sb([P, 5, PAIRS], U8, "early_sc", tag="a_sb13")
-        x2_0 = quantise(sb([P, PAIRS], U32, "x2_codes0")[:], early_sc[:, 0, :], x2_bf[0][:])
+        second_sc = sb([P, 5, PAIRS], U8, "second_sc", tag="a_sb13")
 
         def quantise_wp(g, values):
             codes = sb([P, N], U32, f"wp_codes{g}")
-            return quantise(codes[:], early_sc[:, 1 + g, :], values[:].rearrange("p c i -> p (c i)"))
+            return quantise(codes[:], second_sc[:, 1 + g, :], values[:].rearrange("p c i -> p (c i)"))
 
-        wp_q = [quantise_wp(0, wp_bf0)]
-        x1_1 = (sb([P, PAIRS], U32, "x1_codes1")[:], early_sc[:, 4, :])
+        x2_0 = quantise(sb([P, PAIRS], U32, "x2_codes0")[:], second_sc[:, 0, :], x2_bf[0][:])
+        wp_0 = quantise_wp(0, wp_bf0)
+        x1_1 = (sb([P, PAIRS], U32, "x1_codes1")[:], second_sc[:, 4, :])
         x2_1 = (sb([P, PAIRS], U32, "x2_codes1")[:], sb([P, PAIRS], U8, "x2_sc1")[:])
+        x1_0 = quantise(sb([P, PAIRS], U32, "x1_codes0")[:], second_sc[:, 3, :], x1_bf[0][:])
 
         def quantise_quarters(x, values, quarter, count=1):
-            quantise(*columns(x, quarter_cols(quarter, count)), piece(values, quarter, count))
-
-        x1_0 = quantise(sb([P, PAIRS], U32, "x1_codes0")[:], early_sc[:, 3, :], x1_bf[0][:])
-
+            quantise(*columns(x, quarter_cols(quarter, count)), values_of(values, quarter, count))
 
         out_rows = out.rearrange("(u p) j -> p u j", p=P)
-        y_banks = [bank(f"y{quarter}", [P, N // P, P], 2 + quarter) for quarter in range(3)]
-        y_last = [bank(f"y_last{w}", [P, 2, P], 5 + w) for w in range(2)]
+        y_banks = [bank(f"y{quarter}", [P, N // P, P], number) for quarter, number in enumerate(Y_BANKS)]
+        y_last = [bank(f"y_last{w}", [P, 2, P], number) for w, number in enumerate(Y_LAST_BANKS)]
         targets = [[(u, y[:, u, :], u == 0, u == 3) for u in range(4)] for y in y_banks]
         targets.append([(u, y_last[u // 2][:, u % 2, :], u % 2 == 0, u % 2 == 1) for u in range(4)])
         wd_q = [(wd_w[:, g, :], wd_sc[4 * g : P, :]) for g in range(2)]
@@ -335,44 +353,44 @@ def tile_list_sonobuoy_bearing_pairs_kernel(
         for quarter in range(4):
             accumulate(quarter, wd_q[0], x2_0, first=True)
         for quarter in range(4):
-            accumulate(quarter, wp_q[0], x1_0)
+            accumulate(quarter, wp_0, x1_0)
 
-        def finish(quarter, w, on_vector=False):
-            result = sb([P, 2, P], F32, f"result{quarter}{w}")
-            if on_vector:
-                bias = bo_sb[:, 2 * w : 2 * w + 2].unsqueeze(2).to_broadcast([P, 2, P])
-                nc.vector.tensor_tensor(out=result[:], in0=y_last[w][:], in1=bias, op=ALU.add)
-            else:
-                for u, target, opens, closes in targets[quarter][2 * w : 2 * w + 2]:
-                    nc.scalar.activation(
-                        out=result[:, u % 2, :], in_=target, func=ACT.Identity, bias=bo_sb[:, u : u + 1], scale=1.0
-                    )
-            nc.sync.dma_start(out=out_rows[:, 2 * w : 2 * w + 2, quarter_cols(quarter)], in_=result[:])
+        def finish(quarter):
+            for w in range(2):
+                result = sb([P, 2, P], F32, f"result{quarter}{w}")
+                if (quarter, w) == (3, 0):
+                    bias = bo_sb[:, 0:2].unsqueeze(2).to_broadcast([P, 2, P])
+                    nc.vector.tensor_tensor(out=result[:], in0=y_last[0][:], in1=bias, op=ALU.add)
+                else:
+                    for u, target, opens, closes in targets[quarter][2 * w : 2 * w + 2]:
+                        nc.scalar.activation(
+                            out=result[:, u % 2, :], in_=target, func=ACT.Identity, bias=bo_sb[:, u : u + 1], scale=1.0
+                        )
+                nc.sync.dma_start(out=out_rows[:, 2 * w : 2 * w + 2, quarter_cols(quarter)], in_=result[:])
 
         def close(quarter):
             quantise_quarters(x2_1, x2_bf[1], quarter)
             accumulate(quarter, wd_q[1], x2_1, final=True)
-            for w in range(2):
-                finish(quarter, w, on_vector=(quarter, w) == (3, 0))
+            finish(quarter)
 
-        x2_bf[1] = sb([P, PACK * PAIRS], BF16, "x2_bf1", tag="x1_bf0")
+        x2_bf.append(sb([P, PACK * PAIRS], BF16, "x2_bf1", tag="x1_bf0"))
         difference(nc.gpsimd, 1, 0)
         for quarter in range(4):
             product(1, quarter)
         quantise_quarters(x2_1, x2_bf[1], 0)
         accumulate(0, wd_q[1], x2_1)
         quantise_quarters(x1_1, x1_bf[1], 0, 2)
-        wp_q.append(quantise_wp(1, wp_bf1))
-        accumulate(0, wp_q[1], x1_1, final=True)
-        for w in range(2):
-            finish(0, w)
+        wp_1 = quantise_wp(1, wp_bf1)
+        accumulate(0, wp_1, x1_1, final=True)
+        finish(0)
+        accumulate(1, wp_1, x1_1)
         difference(nc.vector, 1, 1)
-        accumulate(1, wp_q[1], x1_1)
-        difference(nc.vector, 1, 2)
-        close(1)
         quantise_quarters(x1_1, x1_bf[1], 2, 2)
-        accumulate(2, wp_q[1], x1_1)
-        close(2)
-        accumulate(3, wp_q[1], x1_1)
+        close(1)
+        accumulate(TURNED, wp_1, x1_1)
+        quantise(*columns(x2_1, quarter_cols(TURNED)), x2_turned[:].rearrange("p j w -> p (j w)").bitcast(BF16))
+        accumulate(TURNED, wd_q[1], x2_1, final=True)
+        finish(TURNED)
+        accumulate(3, wp_1, x1_1)
         difference(nc.vector, 1, 3)
         close(3)

@@ -18,13 +18,15 @@ FP4X4 = mybir.dt.float4_e2m1fn_x4
 ALU = mybir.AluOpType
 ACT = mybir.ActivationFunctionType
 
+SCATTER_ORDER = (2, 0, 1, 3)
+PIECE = 256
 P = 128
 PACK = 4
 PASS = P * PACK
 WA_QUARTER = H // 4
 LINE = 4
 SCALE_ROWS_AT = 96
-A_BANKS = ((4, 6, 0, 6), (0, 6, 0, 6))
+A_BANKS = ((4, 6, 4, 6), (0, 6, 0, 6))
 B_BANKS = ((2, 3, 4, 5), (2, 3, 6, 7))
 Y_BANKS, Y_LAST_BANKS = (4, 5, 1), (2, 3)
 TURNED, TURN_BANK = 2, 0
@@ -84,31 +86,34 @@ def tile_list_sonobuoy_bearing_pairs_kernel(
         )
         nc.sync.dma_start(idx[:], offs)
         nc.sync.dma_start(idx2[:], offs2)
-        load_page_rows(0)
+        load_page_rows(SCATTER_ORDER[0])
         for quadrant in range(4):
             nc.sync.dma_start(
                 out=wb_sc_raw[32 * quadrant : 32 * quadrant + 4, :, :].bitcast(I32),
                 in_=wb_scales[:, 4 * quadrant : 4 * quadrant + 4, :].rearrange("a r c -> r a c").bitcast(I32),
             )
         load_wa(0)
-        load_page_rows(1)
+        load_page_rows(SCATTER_ORDER[1])
         load_wa(1)
-        load_page_rows(2)
+        load_page_rows(SCATTER_ORDER[2])
 
         picked_sc = sb([P, PAIRS], U8, "picked_sc")
         nc.vector.tensor_copy(picked_sc[:], tab_sc[:].indirect(idx[:]))
+
+        def load_table(a):
+            nc.sync.dma_start(out=tab_w[a][:], in_=tab_words[a].rearrange("p t i -> p (t i)").bitcast(I32))
+
+        load_wb(0)
+        load_wa(2)
+        load_page_rows(SCATTER_ORDER[3])
+        load_table(0)
         for quadrant in range(4):
             first = SCALE_ROWS_AT + 8 * quadrant
             nc.sync.dma_start(
                 out=v_sc[32 * quadrant : 32 * quadrant + 4, :, :].bitcast(I32),
                 in_=picked_sc[first : first + 8, :].bitcast(I32),
             )
-
-        load_wb(0)
-        load_wa(2)
-        load_page_rows(3)
-        for a in range(2):
-            nc.sync.dma_start(out=tab_w[a][:], in_=tab_words[a].rearrange("p t i -> p (t i)").bitcast(I32))
+        load_table(1)
         load_wa(3)
         load_wb(1)
         nc.sync.dma_start(idx3[:], offs3)
@@ -157,39 +162,45 @@ def tile_list_sonobuoy_bearing_pairs_kernel(
                 in_=wa_raw[n][:].rearrange("p i (c t) -> p c i t", t=PACK),
             )
 
-        wa_sc = sb([P, H], U8, "wa_sc")
-
         def quantise(codes, scales, values):
             nc.vector.quantize_mx(out=codes.bitcast(FP8X4), scales=scales, in_=values)
             return codes, scales
 
-        page_bf = [sb([P, PASS, PACK], BF16, "page_bf0"), sb([P, PASS, PACK], BF16, "page_bf1", tag="wb_sc_raw")]
-        for i in range(PACK):
+        page_bf = [sb([P, PIECE, PACK], BF16, f"page_bf{n}", tag="wb_sc_raw" if n == 3 else None) for n in range(4)]
+        for step, i in enumerate(SCATTER_ORDER):
             nc.vector.tensor_copy(page[i][:].indirect(idx2[:]), incoming[i][:])
-            nc.scalar.copy(out=page_bf[0][:, :, i], in_=page[i][:, 0:PASS])
-            round_on_gpsimd(page_bf[1][:, :, i], page[i][:, PASS:])
-            round_wa(i)
+            for n in range(4):
+                source = page[i][:, PIECE * n : PIECE * (n + 1)]
+                if n < (2 if i < 2 else 3):
+                    nc.scalar.copy(out=page_bf[n][:, :, i], in_=source)
+                else:
+                    round_on_gpsimd(page_bf[n][:, :, i], source)
+            round_wa(step)
 
         v_w = [sb([P, PAIRS], U32, f"v_w{a}") for a in range(2)]
-        for a in range(2):
+
+        def gather_table(a):
             nc.vector.tensor_copy(v_w[a][:], tab_w[a][:].bitcast(U32).indirect(idx[:]))
 
-        first_codes = sb([P, T2 + H], U32, "first_codes", tag="tab_w1")
-        page_sc = sb([P, T2], U8, "page_sc")
+        gather_table(0)
+
+        first_codes = sb([P, T2 + H], U32, "first_codes")
+        first_sc = sb([P, T2 + H], U8, "first_sc", tag="picked_sc")
+        page_sc, wa_sc = first_sc[:, 0:T2], first_sc[:, T2:]
 
         def quantise_wa(g, tiles):
             rows = slice(PASS * g + P * tiles.start, PASS * g + P * tiles.stop)
             values = wa_bf[:, g, tiles].rearrange("p t c i -> p (t c i)")
             quantise(first_codes[:, T2 + rows.start : T2 + rows.stop], wa_sc[:, rows], values)
 
-        quantise_wa(0, slice(0, 1))
-        page_q = []
-        for h in range(2):
-            cols = slice(PASS * h, PASS * (h + 1))
-            page_q.append(quantise(first_codes[:, cols], page_sc[:, cols], page_bf[h][:].rearrange("p c i -> p (c i)")))
-        for g, tiles in ((0, slice(1, 3)), (0, slice(3, 4)), (1, slice(0, 4))):
-            quantise_wa(g, tiles)
-        wa_q = (first_codes[:, T2:], wa_sc[:])
+        quantise_wa(0, slice(0, 4))
+        for n in (0, 1, 3, 2):
+            cols = slice(PIECE * n, PIECE * (n + 1))
+            quantise(first_codes[:, cols], page_sc[:, cols], page_bf[n][:].rearrange("p c i -> p (c i)"))
+        page_q = [(first_codes[:, PASS * h : PASS * (h + 1)], page_sc[:, PASS * h : PASS * (h + 1)]) for h in range(2)]
+        gather_table(1)
+        quantise_wa(1, slice(0, 4))
+        wa_q = (first_codes[:, T2:], wa_sc)
 
         def multiply(target, stationary, dtype, moving, start, stop):
             nc.tensor.matmul_mx(
@@ -217,8 +228,10 @@ def tile_list_sonobuoy_bearing_pairs_kernel(
 
         at = [sb([P, PACK, PAIRS], F32, f"at{g}") for g in range(2)]
 
+        first_tiles = sb([P, 2, T2], F32, "first_tiles", tag="wa_raw3")
+
         def project_page(g, t):
-            a_sb = sb([P, T2], F32, f"a_sb{g}{t}")
+            a_sb = first_tiles[:, t, :] if g == 0 and t < 2 else sb([P, T2], F32, f"a_sb{g}{t}")[:]
             for h in range(2):
                 a_bank = bank(f"a_bank{g}{t}{h}", [P, PASS], h + A_BANKS[g][t])
                 multiply(a_bank[:], columns(wa_q, tile_rows(g, t)), FP8X4, page_q[h], True, True)
@@ -226,7 +239,7 @@ def tile_list_sonobuoy_bearing_pairs_kernel(
             last_of_group_0 = (g, t) == (0, PACK - 1)
             for cols in (quarter_cols(0), quarter_cols(1, 3)) if last_of_group_0 else (quarter_cols(0, 4),):
                 offsets = idx3[:, cols.start // 16 : cols.stop // 16]
-                nc.vector.tensor_copy(at[g][:, t, cols], a_sb[:].indirect(offsets))
+                nc.vector.tensor_copy(at[g][:, t, cols], a_sb.indirect(offsets))
 
         b_banks = {}
 

@@ -99,6 +99,12 @@ def tile_list_sonobuoy_bearing_pairs_kernel(
 
         picked_sc = sb([P, PAIRS], U8, "picked_sc")
         nc.vector.tensor_copy(picked_sc[:], tab_sc[:].indirect(idx[:]))
+        for quadrant in range(4):
+            first = SCALE_ROWS_AT + 8 * quadrant
+            nc.sync.dma_start(
+                out=v_sc[32 * quadrant : 32 * quadrant + 4, :, :].bitcast(I32),
+                in_=picked_sc[first : first + 8, :].bitcast(I32),
+            )
 
         def load_table(a):
             nc.sync.dma_start(out=tab_w[a][:], in_=tab_words[a].rearrange("p t i -> p (t i)").bitcast(I32))
@@ -107,14 +113,8 @@ def tile_list_sonobuoy_bearing_pairs_kernel(
         load_wa(2)
         load_page_rows(SCATTER_ORDER[3])
         load_table(0)
-        for quadrant in range(4):
-            first = SCALE_ROWS_AT + 8 * quadrant
-            nc.sync.dma_start(
-                out=v_sc[32 * quadrant : 32 * quadrant + 4, :, :].bitcast(I32),
-                in_=picked_sc[first : first + 8, :].bitcast(I32),
-            )
-        load_table(1)
         load_wa(3)
+        load_table(1)
         load_wb(1)
         nc.sync.dma_start(idx3[:], offs3)
         nc.sync.dma_start(out=cal_sb[:], in_=cal.rearrange("(g p t) -> p g t", g=2, t=PACK))
@@ -184,23 +184,22 @@ def tile_list_sonobuoy_bearing_pairs_kernel(
 
         gather_table(0)
 
-        first_codes = sb([P, T2 + H], U32, "first_codes")
-        first_sc = sb([P, T2 + H], U8, "first_sc", tag="picked_sc")
-        page_sc, wa_sc = first_sc[:, 0:T2], first_sc[:, T2:]
+        first_codes = sb([P, T2 + PASS], U32, "first_codes", tag="tab_w0")
+        wa_codes = (first_codes[:, T2:], sb([P, PASS], U32, "late_codes", tag="tab_w1")[:])
+        page_sc = sb([P, T2], U8, "page_sc")
+        wa_sc = sb([P, H], U8, "wa_sc")
 
         def quantise_wa(g, tiles):
-            rows = slice(PASS * g + P * tiles.start, PASS * g + P * tiles.stop)
             values = wa_bf[:, g, tiles].rearrange("p t c i -> p (t c i)")
-            quantise(first_codes[:, T2 + rows.start : T2 + rows.stop], wa_sc[:, rows], values)
+            return quantise(wa_codes[g], wa_sc[:, PASS * g : PASS * (g + 1)], values)
 
-        quantise_wa(0, slice(0, 4))
+        wa_q = [quantise_wa(0, slice(0, 4))]
         for n in (0, 1, 3, 2):
             cols = slice(PIECE * n, PIECE * (n + 1))
             quantise(first_codes[:, cols], page_sc[:, cols], page_bf[n][:].rearrange("p c i -> p (c i)"))
         page_q = [(first_codes[:, PASS * h : PASS * (h + 1)], page_sc[:, PASS * h : PASS * (h + 1)]) for h in range(2)]
         gather_table(1)
-        quantise_wa(1, slice(0, 4))
-        wa_q = (first_codes[:, T2:], wa_sc)
+        wa_q.append(quantise_wa(1, slice(0, 4)))
 
         def multiply(target, stationary, dtype, moving, start, stop):
             nc.tensor.matmul_mx(
@@ -234,7 +233,7 @@ def tile_list_sonobuoy_bearing_pairs_kernel(
             a_sb = first_tiles[:, t, :] if g == 0 and t < 2 else sb([P, T2], F32, f"a_sb{g}{t}")[:]
             for h in range(2):
                 a_bank = bank(f"a_bank{g}{t}{h}", [P, PASS], h + A_BANKS[g][t])
-                multiply(a_bank[:], columns(wa_q, tile_rows(g, t)), FP8X4, page_q[h], True, True)
+                multiply(a_bank[:], columns(wa_q[g], tile_rows(0, t)), FP8X4, page_q[h], True, True)
                 nc.scalar.copy(out=a_sb[:, PASS * h : PASS * (h + 1)], in_=a_bank[:])
             last_of_group_0 = (g, t) == (0, PACK - 1)
             for cols in (quarter_cols(0), quarter_cols(1, 3)) if last_of_group_0 else (quarter_cols(0, 4),):

@@ -63,7 +63,8 @@ def tile_list_sonobuoy_bearing_pairs_kernel(
         wa_rows = wa.rearrange("(p i) r -> p i r", i=PACK)
         page = [sb([P, T2], F32, f"page{i}") for i in range(PACK)]
         incoming = [sb([P, S], F32, f"incoming{i}") for i in range(PACK)]
-        wa_raw = [sb([P, PACK, WA_QUARTER], F32, f"wa_raw{n}") for n in range(4)]
+        wa_early = sb([P, PACK, H - WA_QUARTER], F32, "wa_early")
+        wa_late = sb([P, PACK, WA_QUARTER], F32, "wa_late")
         wp_raw = [sb([P, PACK, N], F32, f"wp_raw{g}") for g in range(2)]
         tab_w = [sb([P, T], I32, f"tab_w{a}") for a in range(2)]
         wb_raw = [sb([P, H], U16, f"wb_raw{a}") for a in range(2)]
@@ -74,9 +75,6 @@ def tile_list_sonobuoy_bearing_pairs_kernel(
         def load_page_rows(i):
             nc.sync.dma_start(out=page[i][:], in_=base_rows[:, i, :])
             nc.sync.dma_start(out=incoming[i][:], in_=xs_rows[:, i, :])
-
-        def load_wa(n):
-            nc.sync.dma_start(out=wa_raw[n][:], in_=wa_rows[:, :, WA_QUARTER * n : WA_QUARTER * (n + 1)])
 
         def load_wb(a):
             nc.sync.dma_start(out=wb_raw[a][:].bitcast(I32), in_=wb_words[a].bitcast(I32))
@@ -92,9 +90,8 @@ def tile_list_sonobuoy_bearing_pairs_kernel(
                 out=wb_sc_raw[32 * quadrant : 32 * quadrant + 4, :, :].bitcast(I32),
                 in_=wb_scales[:, 4 * quadrant : 4 * quadrant + 4, :].rearrange("a r c -> r a c").bitcast(I32),
             )
-        load_wa(0)
+        load_wb(0)
         load_page_rows(SCATTER_ORDER[1])
-        load_wa(1)
         load_page_rows(SCATTER_ORDER[2])
 
         picked_sc = sb([P, PAIRS], U8, "picked_sc")
@@ -109,19 +106,17 @@ def tile_list_sonobuoy_bearing_pairs_kernel(
         def load_table(a):
             nc.sync.dma_start(out=tab_w[a][:], in_=tab_words[a].rearrange("p t i -> p (t i)").bitcast(I32))
 
-        load_wb(0)
-        load_wa(2)
+        nc.sync.dma_start(out=wa_early[:], in_=wa_rows[:, :, 0 : H - WA_QUARTER])
         load_page_rows(SCATTER_ORDER[3])
         load_table(0)
-        load_wa(3)
+        nc.sync.dma_start(out=wa_late[:], in_=wa_rows[:, :, H - WA_QUARTER :])
         load_table(1)
         load_wb(1)
         nc.sync.dma_start(idx3[:], offs3)
+        wp_rows = wp.rearrange("(g p i) n -> g p i n", g=2, i=PACK)
+        nc.sync.dma_start(out=wp_raw[0][:], in_=wp_rows[0])
         nc.sync.dma_start(out=cal_sb[:], in_=cal.rearrange("(g p t) -> p g t", g=2, t=PACK))
-        for g in range(2):
-            nc.sync.dma_start(
-                out=wp_raw[g][:], in_=wp[PASS * g : PASS * (g + 1), :].rearrange("(p i) n -> p i n", i=PACK)
-            )
+        nc.sync.dma_start(out=wp_raw[1][:], in_=wp_rows[1])
         nc.sync.dma_start(out=wd_w[:], in_=wd_words.rearrange("a p c i -> p a (c i)").bitcast(I32))
         for quadrant in range(4):
             nc.sync.dma_start(
@@ -157,25 +152,26 @@ def tile_list_sonobuoy_bearing_pairs_kernel(
 
         def round_wa(n):
             g, part = divmod(n, 2)
+            source = wa_late[:] if n == 3 else wa_early[:, :, WA_QUARTER * n : WA_QUARTER * (n + 1)]
             nc.scalar.copy(
                 out=wa_bf[:, g, :, (P // 2) * part : (P // 2) * (part + 1), :].rearrange("p t c i -> p c i t"),
-                in_=wa_raw[n][:].rearrange("p i (c t) -> p c i t", t=PACK),
+                in_=source.rearrange("p i (c t) -> p c i t", t=PACK),
             )
 
         def quantise(codes, scales, values):
             nc.vector.quantize_mx(out=codes.bitcast(FP8X4), scales=scales, in_=values)
             return codes, scales
 
-        page_bf = [sb([P, PIECE, PACK], BF16, f"page_bf{n}", tag="wb_sc_raw" if n == 3 else None) for n in range(4)]
-        for step, i in enumerate(SCATTER_ORDER):
+        page_flat = sb([P, T2 * PACK], BF16, "page_flat", tag="wb_sc_raw")
+        page_bf = page_flat[:].rearrange("p (c i) -> p c i", i=PACK)
+        for i, quarters in zip(SCATTER_ORDER, ((), (0, 1, 2), (), (3,))):
             nc.vector.tensor_copy(page[i][:].indirect(idx2[:]), incoming[i][:])
-            for n in range(4):
-                source = page[i][:, PIECE * n : PIECE * (n + 1)]
-                if n < (2 if i < 2 else 3):
-                    nc.scalar.copy(out=page_bf[n][:, :, i], in_=source)
-                else:
-                    round_on_gpsimd(page_bf[n][:, :, i], source)
-            round_wa(step)
+            shared = 3 * PIECE if i >= 2 else 0
+            for first in range(0, shared, PIECE):
+                nc.scalar.copy(out=page_bf[:, first : first + PIECE, i], in_=page[i][:, first : first + PIECE])
+            round_on_gpsimd(page_bf[:, shared:, i], page[i][:, shared:])
+            for n in quarters:
+                round_wa(n)
 
         v_w = [sb([P, PAIRS], U32, f"v_w{a}") for a in range(2)]
 
@@ -185,7 +181,7 @@ def tile_list_sonobuoy_bearing_pairs_kernel(
         gather_table(0)
 
         first_codes = sb([P, T2 + PASS], U32, "first_codes", tag="tab_w0")
-        wa_codes = (first_codes[:, T2:], sb([P, PASS], U32, "late_codes", tag="tab_w1")[:])
+        wa_codes = (first_codes[:, T2:], sb([P, PASS], U32, "late_codes")[:])
         page_sc = sb([P, T2], U8, "page_sc")
         wa_sc = sb([P, H], U8, "wa_sc")
 
@@ -196,10 +192,10 @@ def tile_list_sonobuoy_bearing_pairs_kernel(
         wa_q = [quantise_wa(0, slice(0, 4))]
         for n in (0, 1, 3, 2):
             cols = slice(PIECE * n, PIECE * (n + 1))
-            quantise(first_codes[:, cols], page_sc[:, cols], page_bf[n][:].rearrange("p c i -> p (c i)"))
+            quantise(first_codes[:, cols], page_sc[:, cols], page_flat[:, PACK * cols.start : PACK * cols.stop])
         page_q = [(first_codes[:, PASS * h : PASS * (h + 1)], page_sc[:, PASS * h : PASS * (h + 1)]) for h in range(2)]
-        gather_table(1)
         wa_q.append(quantise_wa(1, slice(0, 4)))
+        gather_table(1)
 
         def multiply(target, stationary, dtype, moving, start, stop):
             nc.tensor.matmul_mx(
@@ -227,7 +223,7 @@ def tile_list_sonobuoy_bearing_pairs_kernel(
 
         at = [sb([P, PACK, PAIRS], F32, f"at{g}") for g in range(2)]
 
-        first_tiles = sb([P, 2, T2], F32, "first_tiles", tag="wa_raw3")
+        first_tiles = sb([P, 2, T2], F32, "first_tiles", tag="wa_late")
 
         def project_page(g, t):
             a_sb = first_tiles[:, t, :] if g == 0 and t < 2 else sb([P, T2], F32, f"a_sb{g}{t}")[:]

@@ -18,7 +18,8 @@ FP4X4 = mybir.dt.float4_e2m1fn_x4
 ALU = mybir.AluOpType
 ACT = mybir.ActivationFunctionType
 
-SCATTER_ORDER = (2, 0, 1, 3)
+SCATTER_ORDER = (0, 2, 1, 3)
+SCALAR_COLUMNS = 768
 PIECE = 256
 P = 128
 PACK = 4
@@ -39,6 +40,7 @@ def tile_list_sonobuoy_bearing_pairs_kernel(
     with ExitStack() as ctx:
         keep = ctx.enter_context(tc.tile_pool(name="keep", bufs=1))
         psum = ctx.enter_context(tc.psum_pool(name="psum", bufs=1))
+        shared_bytes = ctx.enter_context(tc.tile_pool(name="shared_bytes", bufs=1))
 
         def sb(shape, dtype, name, tag=None):
             return keep.tile(shape, dtype, name=name, tag=tag or name, align_bytes=64)
@@ -67,7 +69,11 @@ def tile_list_sonobuoy_bearing_pairs_kernel(
         wa_late = sb([P, PACK, WA_QUARTER], F32, "wa_late")
         wp_raw = [sb([P, PACK, N], F32, f"wp_raw{g}") for g in range(2)]
         tab_w = [sb([P, T], I32, f"tab_w{a}") for a in range(2)]
-        wb_raw = [sb([P, H], U16, f"wb_raw{a}") for a in range(2)]
+        wb_raw = sb([P, H], U16, "wb_raw")
+        wb_late = [
+            shared_bytes.tile([P, PASS], U16, name="wb_late0", align_bytes=64, offset=1536),
+            sb([P, PASS], U16, "wb_late1"),
+        ]
         wd_w = sb([P, 2, N], I32, "wd_w")
         cal_sb = sb([P, 2, PACK], F32, "cal_sb")
         bo_sb = sb([P, N // P], F32, "bo_sb")
@@ -76,8 +82,6 @@ def tile_list_sonobuoy_bearing_pairs_kernel(
             nc.sync.dma_start(out=page[i][:], in_=base_rows[:, i, :])
             nc.sync.dma_start(out=incoming[i][:], in_=xs_rows[:, i, :])
 
-        def load_wb(a):
-            nc.sync.dma_start(out=wb_raw[a][:].bitcast(I32), in_=wb_words[a].bitcast(I32))
 
         nc.sync.dma_start(
             out=tab_sc[SCALE_ROWS_AT:P, :].bitcast(I32), in_=tab_scales.rearrange("a q t -> q a t").bitcast(I32)
@@ -90,18 +94,22 @@ def tile_list_sonobuoy_bearing_pairs_kernel(
                 out=wb_sc_raw[32 * quadrant : 32 * quadrant + 4, :, :].bitcast(I32),
                 in_=wb_scales[:, 4 * quadrant : 4 * quadrant + 4, :].rearrange("a r c -> r a c").bitcast(I32),
             )
-        load_wb(0)
         load_page_rows(SCATTER_ORDER[1])
+        nc.sync.dma_start(out=wb_raw[:].bitcast(I32), in_=wb_words[0].bitcast(I32))
         load_page_rows(SCATTER_ORDER[2])
 
         picked_sc = sb([P, PAIRS], U8, "picked_sc")
         nc.vector.tensor_copy(picked_sc[:], tab_sc[:].indirect(idx[:]))
-        for quadrant in range(4):
+
+        def move_picked_rows(quadrant):
             first = SCALE_ROWS_AT + 8 * quadrant
             nc.sync.dma_start(
                 out=v_sc[32 * quadrant : 32 * quadrant + 4, :, :].bitcast(I32),
                 in_=picked_sc[first : first + 8, :].bitcast(I32),
             )
+
+        for quadrant in range(3):
+            move_picked_rows(quadrant)
 
         def load_table(a):
             nc.sync.dma_start(out=tab_w[a][:], in_=tab_words[a].rearrange("p t i -> p (t i)").bitcast(I32))
@@ -109,13 +117,15 @@ def tile_list_sonobuoy_bearing_pairs_kernel(
         nc.sync.dma_start(out=wa_early[:], in_=wa_rows[:, :, 0 : H - WA_QUARTER])
         load_page_rows(SCATTER_ORDER[3])
         load_table(0)
+        move_picked_rows(3)
         nc.sync.dma_start(out=wa_late[:], in_=wa_rows[:, :, H - WA_QUARTER :])
         load_table(1)
-        load_wb(1)
+        for g in range(2):
+            nc.sync.dma_start(out=wb_late[g][:].bitcast(I32), in_=wb_words[1, :, H * g : H * (g + 1)].bitcast(I32))
         nc.sync.dma_start(idx3[:], offs3)
         wp_rows = wp.rearrange("(g p i) n -> g p i n", g=2, i=PACK)
-        nc.sync.dma_start(out=wp_raw[0][:], in_=wp_rows[0])
         nc.sync.dma_start(out=cal_sb[:], in_=cal.rearrange("(g p t) -> p g t", g=2, t=PACK))
+        nc.sync.dma_start(out=wp_raw[0][:], in_=wp_rows[0])
         nc.sync.dma_start(out=wp_raw[1][:], in_=wp_rows[1])
         nc.sync.dma_start(out=wd_w[:], in_=wd_words.rearrange("a p c i -> p a (c i)").bitcast(I32))
         for quadrant in range(4):
@@ -137,16 +147,18 @@ def tile_list_sonobuoy_bearing_pairs_kernel(
             out=wb_sc[:].rearrange("p a (g t c) -> p (a g) t c", g=2, t=PACK),
             in_=wb_sc_raw[:].rearrange("p a (g c t) -> p (a g) t c", g=2, t=PACK),
         )
-        wb_w = []
+        wb_w = {}
 
-        def reorder_wb(a, tag):
-            wb_w.append(sb([P, H], U16, f"wb_w{a}", tag=tag))
+        def reorder_wb(target, source):
             nc.gpsimd.tensor_copy(
-                out=wb_w[a][:].rearrange("p (g t c e) -> p g c t e", g=2, t=PACK, e=8),
-                in_=wb_raw[a][:].rearrange("p (g c e t) -> p g c t e", g=2, t=PACK, e=8),
+                out=target.rearrange("p (g t c e) -> p g c t e", c=P // 8, t=PACK, e=8),
+                in_=source.rearrange("p (g c e t) -> p g c t e", c=P // 8, t=PACK, e=8),
             )
 
-        reorder_wb(0, None)
+        wb_first = sb([P, H], U16, "wb_first")
+        reorder_wb(wb_first[:], wb_raw[:])
+        for g in range(2):
+            wb_w[0, g] = wb_first[:, PASS * g : PASS * (g + 1)]
 
         wa_bf = sb([P, 2, PACK, P, PACK], BF16, "wa_bf")
 
@@ -162,13 +174,13 @@ def tile_list_sonobuoy_bearing_pairs_kernel(
             nc.vector.quantize_mx(out=codes.bitcast(FP8X4), scales=scales, in_=values)
             return codes, scales
 
-        page_flat = sb([P, T2 * PACK], BF16, "page_flat", tag="wb_sc_raw")
+        page_flat = sb([P, T2 * PACK], BF16, "page_flat")
         page_bf = page_flat[:].rearrange("p (c i) -> p c i", i=PACK)
         for i, quarters in zip(SCATTER_ORDER, ((), (0, 1, 2), (), (3,))):
             nc.vector.tensor_copy(page[i][:].indirect(idx2[:]), incoming[i][:])
-            shared = 3 * PIECE if i >= 2 else 0
-            for first in range(0, shared, PIECE):
-                nc.scalar.copy(out=page_bf[:, first : first + PIECE, i], in_=page[i][:, first : first + PIECE])
+            shared = SCALAR_COLUMNS if i >= 2 else 0
+            for first, last in ((0, PIECE), (PIECE, PASS), (PASS, shared)) if shared else ():
+                nc.scalar.copy(out=page_bf[:, first:last, i], in_=page[i][:, first:last])
             round_on_gpsimd(page_bf[:, shared:, i], page[i][:, shared:])
             for n in quarters:
                 round_wa(n)
@@ -180,8 +192,8 @@ def tile_list_sonobuoy_bearing_pairs_kernel(
 
         gather_table(0)
 
-        first_codes = sb([P, T2 + PASS], U32, "first_codes", tag="tab_w0")
-        wa_codes = (first_codes[:, T2:], sb([P, PASS], U32, "late_codes")[:])
+        first_codes = sb([P, T2 + PASS], U32, "first_codes", tag="picked_sc")
+        wa_codes = (first_codes[:, T2:], shared_bytes.tile([P, PASS], U32, name="late_codes", align_bytes=64, offset=0)[:])
         page_sc = sb([P, T2], U8, "page_sc")
         wa_sc = sb([P, H], U8, "wa_sc")
 
@@ -190,12 +202,14 @@ def tile_list_sonobuoy_bearing_pairs_kernel(
             return quantise(wa_codes[g], wa_sc[:, PASS * g : PASS * (g + 1)], values)
 
         wa_q = [quantise_wa(0, slice(0, 4))]
-        for n in (0, 1, 3, 2):
+        for n in range(4):
             cols = slice(PIECE * n, PIECE * (n + 1))
             quantise(first_codes[:, cols], page_sc[:, cols], page_flat[:, PACK * cols.start : PACK * cols.stop])
         page_q = [(first_codes[:, PASS * h : PASS * (h + 1)], page_sc[:, PASS * h : PASS * (h + 1)]) for h in range(2)]
-        wa_q.append(quantise_wa(1, slice(0, 4)))
         gather_table(1)
+        wb_w[1, 0] = sb([P, PASS], U16, "wb_w10", tag="page_flat")[:]
+        reorder_wb(wb_w[1, 0], wb_late[0][:])
+        wa_q.append(quantise_wa(1, slice(0, 4)))
 
         def multiply(target, stationary, dtype, moving, start, stop):
             nc.tensor.matmul_mx(
@@ -217,11 +231,15 @@ def tile_list_sonobuoy_bearing_pairs_kernel(
         def tile_rows(g, t):
             return slice(PASS * g + P * t, PASS * g + P * (t + 1))
 
-        reorder_wb(1, "wa_bf")
-        wp_bf0 = sb([P, N, PACK], BF16, "wp_bf0", tag="wb_raw1")
+        wb_w[1, 1] = sb([P, PASS], U16, "wb_w11", tag="wa_bf")[:]
+        reorder_wb(wb_w[1, 1], wb_late[1][:])
+        wp_bf0 = sb([P, N, PACK], BF16, "wp_bf0", tag="wb_late1")
         round_on_gpsimd(wp_bf0[:], wp_raw[0][:].rearrange("p i c -> p c i"))
 
-        at = [sb([P, PACK, PAIRS], F32, f"at{g}") for g in range(2)]
+        at = [
+            shared_bytes.tile([P, PACK, PAIRS], F32, name="at0", align_bytes=64, offset=2048),
+            sb([P, PACK, PAIRS], F32, "at1"),
+        ]
 
         first_tiles = sb([P, 2, T2], F32, "first_tiles", tag="wa_late")
 
@@ -238,20 +256,21 @@ def tile_list_sonobuoy_bearing_pairs_kernel(
 
         b_banks = {}
 
-        def project_table(g, quarter):
+        def project_table(g, quarter, passes=(0, 1)):
             cols = quarter_cols(quarter)
-            b_bank = bank(f"b_bank{g}{quarter}", [P, PACK, P], B_BANKS[g][quarter])
-            for a in range(2):
+            if 0 in passes:
+                b_banks[g, quarter] = bank(f"b_bank{g}{quarter}", [P, PACK, P], B_BANKS[g][quarter])
+            b_bank = b_banks[g, quarter]
+            for a in passes:
                 for t in range(PACK):
                     multiply(
                         b_bank[:, t, :],
-                        columns((wb_w[a][:], wb_sc[:, a, :]), tile_rows(g, t)),
+                        (wb_w[a, g][:, tile_rows(0, t)], wb_sc[:, a, tile_rows(g, t)]),
                         FP4X4,
                         (v_w[a][:, cols], v_sc[:, a, cols]),
                         a == 0 and t == 0,
                         a == 1 and t == PACK - 1,
                     )
-            b_banks[g, quarter] = b_bank
 
         cal_b = {}
 
@@ -276,7 +295,7 @@ def tile_list_sonobuoy_bearing_pairs_kernel(
         def values_of(tile, quarter, count=1):
             return tile[:, PASS * quarter : PASS * (quarter + count)]
 
-        x1_bf = [sb([P, PACK * PAIRS], BF16, f"x1_bf{g}") for g in range(2)]
+        x1_bf = [sb([P, PACK * PAIRS], BF16, "x1_bf0")]
         x2_bf = [sb([P, PACK * PAIRS], BF16, "x2_bf0", tag="wp_raw0")]
 
         def product(g, quarter):
@@ -288,9 +307,11 @@ def tile_list_sonobuoy_bearing_pairs_kernel(
             combine(engine, values_of(x2_bf[g], quarter), picked, cal_b[g, quarter][:], ALU.subtract)
 
         for quarter in range(2):
-            project_table(0, quarter)
+            project_table(0, quarter, (0,))
         for t in range(PACK):
             project_page(0, t)
+        for quarter in range(2):
+            project_table(0, quarter, (1,))
         for quarter in range(2, 4):
             project_table(0, quarter)
         for step, products in enumerate(((0, 1), (2,), (3,), ())):
@@ -382,6 +403,7 @@ def tile_list_sonobuoy_bearing_pairs_kernel(
             finish(quarter)
 
         x2_bf.append(sb([P, PACK * PAIRS], BF16, "x2_bf1", tag="x1_bf0"))
+        x1_bf.append(sb([P, PACK * PAIRS], BF16, "x1_bf1"))
         difference(nc.gpsimd, 1, 0)
         for quarter in range(4):
             product(1, quarter)

@@ -20,6 +20,7 @@ ACT = mybir.ActivationFunctionType
 
 SCATTER_ORDER = (0, 2, 1, 3)
 SCALAR_COLUMNS = 768
+SLIVER = 32
 PIECE = 256
 P = 128
 PACK = 4
@@ -64,7 +65,7 @@ def tile_list_sonobuoy_bearing_pairs_kernel(
         xs_rows = xs.rearrange("(p i) j -> p i j", i=PACK)
         wa_rows = wa.rearrange("(p i) r -> p i r", i=PACK)
         page = [sb([P, T2], F32, f"page{i}") for i in range(PACK)]
-        incoming = [sb([P, S], F32, f"incoming{i}") for i in range(PACK)]
+        incoming = {i: sb([P, S], F32, f"incoming{i}") for i in SCATTER_ORDER[1:]}
         wa_early = sb([P, PACK, H - WA_QUARTER], F32, "wa_early")
         wa_late = sb([P, PACK, WA_QUARTER], F32, "wa_late")
         wp_raw = [sb([P, PACK, N], F32, f"wp_raw{g}") for g in range(2)]
@@ -88,12 +89,17 @@ def tile_list_sonobuoy_bearing_pairs_kernel(
         )
         nc.sync.dma_start(idx[:], offs)
         nc.sync.dma_start(idx2[:], offs2)
-        load_page_rows(SCATTER_ORDER[0])
+        first_row = SCATTER_ORDER[0]
+        nc.sync.dma_start(out=page[first_row][:], in_=base_rows[:, first_row, :])
+        first_cuts = (slice(0, P), slice(P, S))
+        first_incoming = [sb([P, cut.stop - cut.start], F32, f"first_incoming{n}") for n, cut in enumerate(first_cuts)]
+        nc.sync.dma_start(out=first_incoming[0][:], in_=xs_rows[:, first_row, first_cuts[0]])
         for quadrant in range(4):
             nc.sync.dma_start(
                 out=wb_sc_raw[32 * quadrant : 32 * quadrant + 4, :, :].bitcast(I32),
                 in_=wb_scales[:, 4 * quadrant : 4 * quadrant + 4, :].rearrange("a r c -> r a c").bitcast(I32),
             )
+        nc.sync.dma_start(out=first_incoming[1][:], in_=xs_rows[:, first_row, first_cuts[1]])
         load_page_rows(SCATTER_ORDER[1])
         nc.sync.dma_start(out=wb_raw[:].bitcast(I32), in_=wb_words[0].bitcast(I32))
         load_page_rows(SCATTER_ORDER[2])
@@ -177,7 +183,11 @@ def tile_list_sonobuoy_bearing_pairs_kernel(
         page_flat = sb([P, T2 * PACK], BF16, "page_flat")
         page_bf = page_flat[:].rearrange("p (c i) -> p c i", i=PACK)
         for i, quarters in zip(SCATTER_ORDER, ((), (0, 1, 2), (), (3,))):
-            nc.vector.tensor_copy(page[i][:].indirect(idx2[:]), incoming[i][:])
+            if i == first_row:
+                for cut, piece in zip(first_cuts, first_incoming):
+                    nc.vector.tensor_copy(page[i][:].indirect(idx2[:, cut.start // 16 : cut.stop // 16]), piece[:])
+            else:
+                nc.vector.tensor_copy(page[i][:].indirect(idx2[:]), incoming[i][:])
             shared = SCALAR_COLUMNS if i >= 2 else 0
             for first, last in ((0, PIECE), (PIECE, PASS), (PASS, shared)) if shared else ():
                 nc.scalar.copy(out=page_bf[:, first:last, i], in_=page[i][:, first:last])
@@ -274,12 +284,12 @@ def tile_list_sonobuoy_bearing_pairs_kernel(
 
         cal_b = {}
 
-        def calibrate(g, quarter, gains):
-            cal_b[g, quarter] = sb([P, PACK, P], F32, f"cal_b{g}{quarter}")
+        def calibrate(g, quarter, gains, part=slice(0, P)):
+            cal_b[g, quarter] = sb([P, PACK, part.stop - part.start], F32, f"cal_b{g}{quarter}_{part.start}")
             for t in range(PACK):
                 nc.scalar.activation(
                     out=cal_b[g, quarter][:, t, :],
-                    in_=b_banks[g, quarter][:, t, :],
+                    in_=b_banks[g, quarter][:, t, part],
                     func=ACT.Copy,
                     scale=gains[:, t : t + 1],
                 )
@@ -302,9 +312,10 @@ def tile_list_sonobuoy_bearing_pairs_kernel(
             picked = at[g][:, :, quarter_cols(quarter)]
             combine(nc.vector, values_of(x1_bf[g], quarter), b_banks[g, quarter][:], picked, ALU.mult)
 
-        def difference(engine, g, quarter):
-            picked = at[g][:, :, quarter_cols(quarter)]
-            combine(engine, values_of(x2_bf[g], quarter), picked, cal_b[g, quarter][:], ALU.subtract)
+        def difference(engine, g, quarter, part=slice(0, P)):
+            cols = slice(P * quarter + part.start, P * quarter + part.stop)
+            values = x2_bf[g][:, PACK * cols.start : PACK * cols.stop]
+            combine(engine, values, at[g][:, :, cols], cal_b[g, quarter][:], ALU.subtract)
 
         for quarter in range(2):
             project_table(0, quarter, (0,))
@@ -315,11 +326,14 @@ def tile_list_sonobuoy_bearing_pairs_kernel(
         for quarter in range(2, 4):
             project_table(0, quarter)
         for step, products in enumerate(((0, 1), (2,), (3,), ())):
-            calibrate(0, step, cal_sb[:, 0, :])
-            difference(nc.gpsimd, 0, step)
+            part = slice(0, P - SLIVER if step == 3 else P)
+            calibrate(0, step, cal_sb[:, 0, :], part)
+            difference(nc.gpsimd, 0, step, part)
             for quarter in products:
                 product(0, quarter)
             project_page(1, step)
+        calibrate(0, 3, cal_sb[:, 0, :], slice(P - SLIVER, P))
+        difference(nc.gpsimd, 0, 3, slice(P - SLIVER, P))
         minus_cal = sb([P, PACK], F32, "minus_cal")
         nc.scalar.activation(out=minus_cal[:], in_=cal_sb[:, 1, :], func=ACT.Copy, scale=-1.0)
         for quarter in range(4):
@@ -352,7 +366,7 @@ def tile_list_sonobuoy_bearing_pairs_kernel(
         x2_turned = sb([P, P, 2], F32, "x2_turned")
         nc.scalar.copy(out=x2_turned[:], in_=back[:].rearrange("p w j -> p j w"))
 
-        second_sc = sb([P, 5, PAIRS], U8, "second_sc", tag="a_sb13")
+        second_sc = sb([P, 5, PAIRS], U8, "second_sc", tag=f"cal_b03_{P - SLIVER}")
 
         def quantise_wp(g, values):
             codes = sb([P, N], U32, f"wp_codes{g}")

@@ -31,7 +31,7 @@ SCALE_ROWS_AT = 96
 A_BANKS = ((4, 6, 4, 6), (0, 6, 0, 6))
 B_BANKS = ((2, 3, 4, 5), (2, 3, 6, 7))
 Y_BANKS, Y_LAST_BANKS = (4, 5, 1), (2, 3)
-TURNED, TURN_BANK = 2, 0
+TURNED, TURN_BANK = 1, 0
 
 
 def tile_list_sonobuoy_bearing_pairs_kernel(
@@ -245,6 +245,8 @@ def tile_list_sonobuoy_bearing_pairs_kernel(
         reorder_wb(wb_w[1, 1], wb_late[1][:])
         wp_bf0 = sb([P, N, PACK], BF16, "wp_bf0", tag="wb_late1")
         round_on_gpsimd(wp_bf0[:], wp_raw[0][:].rearrange("p i c -> p c i"))
+        wp_head = sb([P, P, PACK], BF16, "wp_head")
+        round_on_gpsimd(wp_head[:], wp_raw[1][:, :, 0:P].rearrange("p i c -> p c i"))
 
         at = [
             shared_bytes.tile([P, PACK, PAIRS], F32, name="at0", align_bytes=64, offset=2048),
@@ -315,7 +317,7 @@ def tile_list_sonobuoy_bearing_pairs_kernel(
         def difference(engine, g, quarter, part=slice(0, P)):
             cols = slice(P * quarter + part.start, P * quarter + part.stop)
             values = x2_bf[g][:, PACK * cols.start : PACK * cols.stop]
-            combine(engine, values, at[g][:, :, cols], cal_b[g, quarter][:], ALU.subtract)
+            combine(engine, values, at[g][:, :, cols], cal_b[g, quarter][:, :, part] if g == 1 else cal_b[g, quarter][:], ALU.subtract)
 
         for quarter in range(2):
             project_table(0, quarter, (0,))
@@ -336,12 +338,12 @@ def tile_list_sonobuoy_bearing_pairs_kernel(
         difference(nc.gpsimd, 0, 3, slice(P - SLIVER, P))
         minus_cal = sb([P, PACK], F32, "minus_cal")
         nc.scalar.activation(out=minus_cal[:], in_=cal_sb[:, 1, :], func=ACT.Copy, scale=-1.0)
-        for quarter in range(4):
+        for quarter in (TURNED, 0, 2):
             project_table(1, quarter)
             calibrate(1, quarter, minus_cal[:] if quarter == TURNED else cal_sb[:, 1, :])
 
         turned = bank("turned", [P, PACK, P], TURN_BANK)
-        sources = (at[1][:, :, quarter_cols(TURNED)], cal_b[1, TURNED][:])
+        sources = (cal_b[1, TURNED][:], at[1][:, :, quarter_cols(TURNED)])
         for place, source in enumerate(sources):
             for t in range(PACK):
                 nc.tensor.matmul(
@@ -352,19 +354,22 @@ def tile_list_sonobuoy_bearing_pairs_kernel(
                     stop=(place, t) == (1, PACK - 1),
                     is_transpose=True,
                 )
-        wp_bf1 = sb([P, N, PACK], BF16, "wp_bf1", tag="a_sb12")
-        nc.scalar.copy(
-            out=wp_bf1[:].rearrange("p (c e) i -> p c i e", e=2),
-            in_=wp_raw[1][:].rearrange("p i (c e) -> p c i e", e=2),
-        )
         turned_bf = sb([P, 2, P, 2], BF16, "turned_bf")
         nc.scalar.copy(out=turned_bf[:], in_=turned[:].rearrange("j (w e) p -> j w p e", e=2))
+        project_table(1, 3)
+        calibrate(1, 3, cal_sb[:, 1, :])
         turned_words = turned_bf[:].rearrange("j w p e -> j (w p e)").bitcast(F32)
         back = bank("back", [P, 2, P], TURN_BANK)
         for w in range(2):
             nc.tensor.transpose(back[:, w, :], turned_words[:, P * w : P * (w + 1)], identity[:])
         x2_turned = sb([P, P, 2], F32, "x2_turned")
         nc.scalar.copy(out=x2_turned[:], in_=back[:].rearrange("p w j -> p j w"))
+
+        wp_bf1 = sb([P, N - P, PACK], BF16, "wp_bf1", tag="turned_bf")
+        nc.scalar.copy(
+            out=wp_bf1[:].rearrange("p (c e) i -> p c i e", e=2),
+            in_=wp_raw[1][:, :, P:].rearrange("p i (c e) -> p c i e", e=2),
+        )
 
         second_sc = sb([P, 5, PAIRS], U8, "second_sc", tag=f"cal_b03_{P - SLIVER}")
 
@@ -374,8 +379,10 @@ def tile_list_sonobuoy_bearing_pairs_kernel(
 
         x2_0 = quantise(sb([P, PAIRS], U32, "x2_codes0")[:], second_sc[:, 0, :], x2_bf[0][:])
         wp_0 = quantise_wp(0, wp_bf0)
+        wp_1 = (sb([P, N], U32, "wp_codes1")[:], second_sc[:, 2, :])
+        quantise(*columns(wp_1, slice(0, P)), wp_head[:].rearrange("p c i -> p (c i)"))
         x1_1 = (sb([P, PAIRS], U32, "x1_codes1")[:], second_sc[:, 4, :])
-        x2_1 = (sb([P, PAIRS], U32, "x2_codes1")[:], sb([P, PAIRS], U8, "x2_sc1")[:])
+        x2_1 = (sb([P, PAIRS], U32, "x2_codes1")[:], sb([P, PAIRS], U8, "x2_sc1", tag="cal_b10_0")[:])
         x1_0 = quantise(sb([P, PAIRS], U32, "x1_codes0")[:], second_sc[:, 3, :], x1_bf[0][:])
 
         def quantise_quarters(x, values, quarter, count=1):
@@ -419,22 +426,22 @@ def tile_list_sonobuoy_bearing_pairs_kernel(
         x2_bf.append(sb([P, PACK * PAIRS], BF16, "x2_bf1", tag="x1_bf0"))
         x1_bf.append(sb([P, PACK * PAIRS], BF16, "x1_bf1"))
         difference(nc.gpsimd, 1, 0)
+        difference(nc.gpsimd, 1, 2, slice(0, SLIVER))
         for quarter in range(4):
             product(1, quarter)
+        quantise(*columns(x2_1, quarter_cols(TURNED)), x2_turned[:].rearrange("p j w -> p (j w)").bitcast(BF16))
+        accumulate(TURNED, wd_q[1], x2_1)
         quantise_quarters(x2_1, x2_bf[1], 0)
         accumulate(0, wd_q[1], x2_1)
         quantise_quarters(x1_1, x1_bf[1], 0, 2)
-        wp_1 = quantise_wp(1, wp_bf1)
-        accumulate(0, wp_1, x1_1, final=True)
-        finish(0)
-        accumulate(1, wp_1, x1_1)
-        difference(nc.vector, 1, 1)
+        quantise(*columns(wp_1, slice(P, N)), wp_bf1[:].rearrange("p c i -> p (c i)"))
+        for quarter in range(2):
+            accumulate(quarter, wp_1, x1_1, final=True)
+            finish(quarter)
+        difference(nc.vector, 1, 2, slice(SLIVER, P))
         quantise_quarters(x1_1, x1_bf[1], 2, 2)
-        close(1)
-        accumulate(TURNED, wp_1, x1_1)
-        quantise(*columns(x2_1, quarter_cols(TURNED)), x2_turned[:].rearrange("p j w -> p (j w)").bitcast(BF16))
-        accumulate(TURNED, wd_q[1], x2_1, final=True)
-        finish(TURNED)
+        accumulate(2, wp_1, x1_1)
+        close(2)
         accumulate(3, wp_1, x1_1)
         difference(nc.vector, 1, 3)
         close(3)

@@ -31,7 +31,7 @@ SCALE_ROWS_AT = 96
 A_BANKS = ((4, 6, 4, 6), (0, 6, 0, 6))
 B_BANKS = ((2, 3, 4, 5), (2, 3, 6, 7))
 Y_BANKS, Y_LAST_BANKS = (4, 5, 1), (2, 3)
-TURNED, TURN_BANK = 1, 0
+TURNED, TURN_BANK = 0, 0
 
 
 def tile_list_sonobuoy_bearing_pairs_kernel(
@@ -212,7 +212,7 @@ def tile_list_sonobuoy_bearing_pairs_kernel(
             return quantise(wa_codes[g], wa_sc[:, PASS * g : PASS * (g + 1)], values)
 
         wa_q = [quantise_wa(0, slice(0, 4))]
-        for n in range(4):
+        for n in (0, 1, 3, 2):
             cols = slice(PIECE * n, PIECE * (n + 1))
             quantise(first_codes[:, cols], page_sc[:, cols], page_flat[:, PACK * cols.start : PACK * cols.stop])
         page_q = [(first_codes[:, PASS * h : PASS * (h + 1)], page_sc[:, PASS * h : PASS * (h + 1)]) for h in range(2)]
@@ -285,9 +285,13 @@ def tile_list_sonobuoy_bearing_pairs_kernel(
                     )
 
         cal_b = {}
+        late_cal_b = sb([P, PACK, PAIRS], F32, "late_cal_b")
 
         def calibrate(g, quarter, gains, part=slice(0, P)):
-            cal_b[g, quarter] = sb([P, PACK, part.stop - part.start], F32, f"cal_b{g}{quarter}_{part.start}")
+            if g == 1 and quarter != TURNED:
+                cal_b[g, quarter] = late_cal_b[:, :, quarter_cols(quarter)]
+            else:
+                cal_b[g, quarter] = sb([P, PACK, part.stop - part.start], F32, f"cal_b{g}{quarter}_{part.start}")
             for t in range(PACK):
                 nc.scalar.activation(
                     out=cal_b[g, quarter][:, t, :],
@@ -317,7 +321,7 @@ def tile_list_sonobuoy_bearing_pairs_kernel(
         def difference(engine, g, quarter, part=slice(0, P)):
             cols = slice(P * quarter + part.start, P * quarter + part.stop)
             values = x2_bf[g][:, PACK * cols.start : PACK * cols.stop]
-            combine(engine, values, at[g][:, :, cols], cal_b[g, quarter][:, :, part] if g == 1 else cal_b[g, quarter][:], ALU.subtract)
+            combine(engine, values, at[g][:, :, cols], late_cal_b[:, :, cols] if g == 1 else cal_b[g, quarter][:], ALU.subtract)
 
         for quarter in range(2):
             project_table(0, quarter, (0,))
@@ -338,7 +342,7 @@ def tile_list_sonobuoy_bearing_pairs_kernel(
         difference(nc.gpsimd, 0, 3, slice(P - SLIVER, P))
         minus_cal = sb([P, PACK], F32, "minus_cal")
         nc.scalar.activation(out=minus_cal[:], in_=cal_sb[:, 1, :], func=ACT.Copy, scale=-1.0)
-        for quarter in (TURNED, 0, 2):
+        for quarter in range(3):
             project_table(1, quarter)
             calibrate(1, quarter, minus_cal[:] if quarter == TURNED else cal_sb[:, 1, :])
 
@@ -362,14 +366,13 @@ def tile_list_sonobuoy_bearing_pairs_kernel(
         back = bank("back", [P, 2, P], TURN_BANK)
         for w in range(2):
             nc.tensor.transpose(back[:, w, :], turned_words[:, P * w : P * (w + 1)], identity[:])
-        x2_turned = sb([P, P, 2], F32, "x2_turned")
-        nc.scalar.copy(out=x2_turned[:], in_=back[:].rearrange("p w j -> p j w"))
-
         wp_bf1 = sb([P, N - P, PACK], BF16, "wp_bf1", tag="turned_bf")
         nc.scalar.copy(
             out=wp_bf1[:].rearrange("p (c e) i -> p c i e", e=2),
             in_=wp_raw[1][:, :, P:].rearrange("p i (c e) -> p c i e", e=2),
         )
+        x2_turned = sb([P, P, 2], F32, "x2_turned")
+        nc.scalar.copy(out=x2_turned[:], in_=back[:].rearrange("p w j -> p j w"))
 
         second_sc = sb([P, 5, PAIRS], U8, "second_sc", tag=f"cal_b03_{P - SLIVER}")
 
@@ -382,66 +385,69 @@ def tile_list_sonobuoy_bearing_pairs_kernel(
         wp_1 = (sb([P, N], U32, "wp_codes1")[:], second_sc[:, 2, :])
         quantise(*columns(wp_1, slice(0, P)), wp_head[:].rearrange("p c i -> p (c i)"))
         x1_1 = (sb([P, PAIRS], U32, "x1_codes1")[:], second_sc[:, 4, :])
-        x2_1 = (sb([P, PAIRS], U32, "x2_codes1")[:], sb([P, PAIRS], U8, "x2_sc1", tag="cal_b10_0")[:])
+        x2_1 = (sb([P, PAIRS], U32, "x2_codes1")[:], sb([P, PAIRS], U8, "x2_sc1")[:])
         x1_0 = quantise(sb([P, PAIRS], U32, "x1_codes0")[:], second_sc[:, 3, :], x1_bf[0][:])
 
         def quantise_quarters(x, values, quarter, count=1):
             quantise(*columns(x, quarter_cols(quarter, count)), values_of(values, quarter, count))
 
         out_rows = out.rearrange("(u p) j -> p u j", p=P)
-        y_banks = [bank(f"y{quarter}", [P, N // P, P], number) for quarter, number in enumerate(Y_BANKS)]
-        y_last = [bank(f"y_last{w}", [P, 2, P], number) for w, number in enumerate(Y_LAST_BANKS)]
-        targets = [[(u, y[:, u, :], u == 0, u == 3) for u in range(4)] for y in y_banks]
-        targets.append([(u, y_last[u // 2][:, u % 2, :], u % 2 == 0, u % 2 == 1) for u in range(4)])
+        parts = {}
+        for name, cols, numbers in (("half", quarter_cols(0, 2), (4, 5)), ("third", quarter_cols(2), (1,)), ("fourth", quarter_cols(3), (2, 3))):
+            rows = 4 // len(numbers)
+            tiles = [bank(f"y_{name}{n}", [P, rows, cols.stop - cols.start], n) for n in numbers]
+            parts[name] = (cols, [(tiles[u // rows][:, u % rows, :], u % rows == 0, u % rows == rows - 1) for u in range(4)], tiles)
         wd_q = [(wd_w[:, g, :], wd_sc[4 * g : P, :]) for g in range(2)]
 
-        def accumulate(quarter, weights, x, first=False, final=False):
-            for u, target, opens, closes in targets[quarter]:
+        def accumulate(name, weights, x, first=False, final=False):
+            cols, targets, tiles = parts[name]
+            for u, (target, opens, closes) in enumerate(targets):
                 stationary = columns(weights, slice(P * u, P * (u + 1)))
-                multiply(target, stationary, FP8X4, columns(x, quarter_cols(quarter)), first and opens, final and closes)
+                multiply(target, stationary, FP8X4, columns(x, cols), first and opens, final and closes)
 
-        for quarter in range(4):
-            accumulate(quarter, wd_q[0], x2_0, first=True)
-        for quarter in range(4):
-            accumulate(quarter, wp_0, x1_0)
+        for name in parts:
+            accumulate(name, wd_q[0], x2_0, first=True)
+        for name in parts:
+            accumulate(name, wp_0, x1_0)
 
-        def finish(quarter):
-            for w in range(2):
-                result = sb([P, 2, P], F32, f"result{quarter}{w}")
-                if (quarter, w) == (3, 0):
-                    bias = bo_sb[:, 0:2].unsqueeze(2).to_broadcast([P, 2, P])
-                    nc.vector.tensor_tensor(out=result[:], in0=y_last[0][:], in1=bias, op=ALU.add)
-                else:
-                    for u, target, opens, closes in targets[quarter][2 * w : 2 * w + 2]:
-                        nc.scalar.activation(
-                            out=result[:, u % 2, :], in_=target, func=ACT.Identity, bias=bo_sb[:, u : u + 1], scale=1.0
-                        )
-                nc.sync.dma_start(out=out_rows[:, 2 * w : 2 * w + 2, quarter_cols(quarter)], in_=result[:])
+        def finish_on_scalar(name, rows):
+            cols, targets, tiles = parts[name]
+            result = sb([P, len(rows), cols.stop - cols.start], F32, f"result_{name}{rows[0]}")
+            for place, u in enumerate(rows):
+                nc.scalar.activation(
+                    out=result[:, place, :], in_=targets[u][0], func=ACT.Identity, bias=bo_sb[:, u : u + 1], scale=1.0
+                )
+            nc.sync.dma_start(out=out_rows[:, rows[0] : rows[-1] + 1, cols], in_=result[:])
 
-        def close(quarter):
-            quantise_quarters(x2_1, x2_bf[1], quarter)
-            accumulate(quarter, wd_q[1], x2_1, final=True)
-            finish(quarter)
+        def finish_on_vector(name, source, first):
+            result = sb([P, 2, P], F32, f"result_{name}{first}")
+            bias = bo_sb[:, first : first + 2].unsqueeze(2).to_broadcast([P, 2, P])
+            nc.vector.tensor_tensor(out=result[:], in0=source, in1=bias, op=ALU.add)
+            nc.sync.dma_start(out=out_rows[:, first : first + 2, parts[name][0]], in_=result[:])
 
         x2_bf.append(sb([P, PACK * PAIRS], BF16, "x2_bf1", tag="x1_bf0"))
         x1_bf.append(sb([P, PACK * PAIRS], BF16, "x1_bf1"))
-        difference(nc.gpsimd, 1, 0)
-        difference(nc.gpsimd, 1, 2, slice(0, SLIVER))
+        difference(nc.gpsimd, 1, 1, slice(0, P + SLIVER))
         for quarter in range(4):
             product(1, quarter)
-        quantise(*columns(x2_1, quarter_cols(TURNED)), x2_turned[:].rearrange("p j w -> p (j w)").bitcast(BF16))
-        accumulate(TURNED, wd_q[1], x2_1)
-        quantise_quarters(x2_1, x2_bf[1], 0)
-        accumulate(0, wd_q[1], x2_1)
         quantise_quarters(x1_1, x1_bf[1], 0, 2)
+        quantise_quarters(x2_1, x2_bf[1], 1)
+        quantise(*columns(x2_1, quarter_cols(TURNED)), x2_turned[:].rearrange("p j w -> p (j w)").bitcast(BF16))
+        accumulate("half", wd_q[1], x2_1)
         quantise(*columns(wp_1, slice(P, N)), wp_bf1[:].rearrange("p c i -> p (c i)"))
-        for quarter in range(2):
-            accumulate(quarter, wp_1, x1_1, final=True)
-            finish(quarter)
+        accumulate("half", wp_1, x1_1, final=True)
+        for u in range(4):
+            finish_on_scalar("half", (u,))
         difference(nc.vector, 1, 2, slice(SLIVER, P))
         quantise_quarters(x1_1, x1_bf[1], 2, 2)
-        accumulate(2, wp_1, x1_1)
-        close(2)
-        accumulate(3, wp_1, x1_1)
+        accumulate("third", wp_1, x1_1)
+        quantise_quarters(x2_1, x2_bf[1], 2)
+        accumulate("third", wd_q[1], x2_1, final=True)
+        for rows in ((0, 1), (2, 3)):
+            finish_on_scalar("third", rows)
+        accumulate("fourth", wp_1, x1_1)
         difference(nc.vector, 1, 3)
-        close(3)
+        quantise_quarters(x2_1, x2_bf[1], 3)
+        accumulate("fourth", wd_q[1], x2_1, final=True)
+        finish_on_vector("fourth", parts["fourth"][2][0][:], 0)
+        finish_on_scalar("fourth", (2, 3))

@@ -55,17 +55,21 @@ def tile_list_sonobuoy_bearing_pairs_kernel(
 
         tab_sc = sb([P, T], U8, "tab_sc")
         nc.vector.memset(tab_sc[0:SCALE_ROWS_AT, :].bitcast(I32), 0)
-        wb_sc_raw = sb([P, 2, H], U8, "wb_sc_raw")
+        wb_sc_raw = sb([P, H], U8, "wb_sc_raw")
+        nc.vector.memset(wb_sc_raw[0:SCALE_ROWS_AT, :].bitcast(I32), 0)
+        wb_sc = sb([P, 2, H], U8, "wb_sc")
         v_sc = sb([P, 2, PAIRS], U8, "v_sc")
         wd_sc = sb([P, N], U8, "wd_sc")
-        for scale_tile in (wb_sc_raw, v_sc, wd_sc):
+        for scale_tile in (wb_sc, v_sc, wd_sc):
             nc.vector.memset(scale_tile[:].bitcast(I32), 0)
 
         base_rows = base.rearrange("(p i) t -> p i t", i=PACK)
         xs_rows = xs.rearrange("(p i) j -> p i j", i=PACK)
         wa_rows = wa.rearrange("(p i) r -> p i r", i=PACK)
         page = [sb([P, T2], F32, f"page{i}") for i in range(PACK)]
-        incoming = {i: sb([P, S], F32, f"incoming{i}") for i in SCATTER_ORDER[1:]}
+        first_cuts = (slice(0, P), slice(P, S))
+        first_incoming = [sb([P, cut.stop - cut.start], F32, f"first_incoming{n}") for n, cut in enumerate(first_cuts)]
+        later_incoming = sb([P, PACK - 1, S], F32, "later_incoming")
         wa_early = sb([P, PACK, H - WA_QUARTER], F32, "wa_early")
         wa_late = sb([P, PACK, WA_QUARTER], F32, "wa_late")
         wp_raw = [sb([P, PACK, N], F32, f"wp_raw{g}") for g in range(2)]
@@ -81,49 +85,52 @@ def tile_list_sonobuoy_bearing_pairs_kernel(
 
         def load_page_rows(i):
             nc.sync.dma_start(out=page[i][:], in_=base_rows[:, i, :])
-            nc.sync.dma_start(out=incoming[i][:], in_=xs_rows[:, i, :])
 
 
         nc.sync.dma_start(
             out=tab_sc[SCALE_ROWS_AT:P, :].bitcast(I32), in_=tab_scales.rearrange("a q t -> q a t").bitcast(I32)
         )
         nc.sync.dma_start(idx[:], offs)
+        load_page_rows(SCATTER_ORDER[0])
         nc.sync.dma_start(idx2[:], offs2)
-        first_row = SCATTER_ORDER[0]
-        nc.sync.dma_start(out=page[first_row][:], in_=base_rows[:, first_row, :])
-        first_cuts = (slice(0, P), slice(P, S))
-        first_incoming = [sb([P, cut.stop - cut.start], F32, f"first_incoming{n}") for n, cut in enumerate(first_cuts)]
-        nc.sync.dma_start(out=first_incoming[0][:], in_=xs_rows[:, first_row, first_cuts[0]])
-        for quadrant in range(4):
-            nc.sync.dma_start(
-                out=wb_sc_raw[32 * quadrant : 32 * quadrant + 4, :, :].bitcast(I32),
-                in_=wb_scales[:, 4 * quadrant : 4 * quadrant + 4, :].rearrange("a r c -> r a c").bitcast(I32),
-            )
-        nc.sync.dma_start(out=first_incoming[1][:], in_=xs_rows[:, first_row, first_cuts[1]])
+        for cut, piece in zip(first_cuts, first_incoming):
+            nc.sync.dma_start(out=piece[:], in_=xs_rows[:, 0, cut])
+        nc.sync.dma_start(
+            out=wb_sc_raw[SCALE_ROWS_AT:P, :].bitcast(I32), in_=wb_scales.rearrange("a q c -> q a c").bitcast(I32)
+        )
         load_page_rows(SCATTER_ORDER[1])
+        nc.sync.dma_start(out=later_incoming[:], in_=xs_rows[:, 1:, :])
         nc.sync.dma_start(out=wb_raw[:].bitcast(I32), in_=wb_words[0].bitcast(I32))
         load_page_rows(SCATTER_ORDER[2])
 
         picked_sc = sb([P, PAIRS], U8, "picked_sc")
         nc.vector.tensor_copy(picked_sc[:], tab_sc[:].indirect(idx[:]))
 
-        def move_picked_rows(quadrant):
+        wb_sc_rows = sb([P, H], U8, "wb_sc_rows")
+        nc.gpsimd.tensor_copy(
+            out=wb_sc_rows[:].rearrange("p (g t c) -> p g t c", g=2, t=PACK),
+            in_=wb_sc_raw[:].rearrange("p (g c t) -> p g t c", g=2, t=PACK),
+        )
+
+        def move_rows(target, source, quadrant):
             first = SCALE_ROWS_AT + 8 * quadrant
             nc.sync.dma_start(
-                out=v_sc[32 * quadrant : 32 * quadrant + 4, :, :].bitcast(I32),
-                in_=picked_sc[first : first + 8, :].bitcast(I32),
+                out=target[32 * quadrant : 32 * quadrant + 4, :, :].bitcast(I32),
+                in_=source[first : first + 8, :].bitcast(I32),
             )
 
+        def load_table(a, cols=slice(0, T)):
+            nc.sync.dma_start(out=tab_w[a][:, cols], in_=tab_words[a].rearrange("p t i -> p (t i)").bitcast(I32)[:, cols])
+
         for quadrant in range(3):
-            move_picked_rows(quadrant)
-
-        def load_table(a):
-            nc.sync.dma_start(out=tab_w[a][:], in_=tab_words[a].rearrange("p t i -> p (t i)").bitcast(I32))
-
+            move_rows(v_sc, picked_sc, quadrant)
         nc.sync.dma_start(out=wa_early[:], in_=wa_rows[:, :, 0 : H - WA_QUARTER])
         load_page_rows(SCATTER_ORDER[3])
-        load_table(0)
-        move_picked_rows(3)
+        load_table(0, slice(0, T // 2))
+        for quadrant in range(4):
+            move_rows(wb_sc, wb_sc_rows, quadrant)
+        load_table(0, slice(T // 2, T))
+        move_rows(v_sc, picked_sc, 3)
         nc.sync.dma_start(out=wa_late[:], in_=wa_rows[:, :, H - WA_QUARTER :])
         load_table(1)
         for g in range(2):
@@ -148,11 +155,6 @@ def tile_list_sonobuoy_bearing_pairs_kernel(
         identity = sb([P, P], F32, "identity")
         make_identity(nc, identity[:])
 
-        wb_sc = sb([P, 2, H], U8, "wb_sc")
-        nc.gpsimd.tensor_copy(
-            out=wb_sc[:].rearrange("p a (g t c) -> p (a g) t c", g=2, t=PACK),
-            in_=wb_sc_raw[:].rearrange("p a (g c t) -> p (a g) t c", g=2, t=PACK),
-        )
         wb_w = {}
 
         def reorder_wb(target, source):
@@ -183,11 +185,11 @@ def tile_list_sonobuoy_bearing_pairs_kernel(
         page_flat = sb([P, T2 * PACK], BF16, "page_flat")
         page_bf = page_flat[:].rearrange("p (c i) -> p c i", i=PACK)
         for i, quarters in zip(SCATTER_ORDER, ((), (0, 1, 2), (), (3,))):
-            if i == first_row:
+            if i == 0:
                 for cut, piece in zip(first_cuts, first_incoming):
                     nc.vector.tensor_copy(page[i][:].indirect(idx2[:, cut.start // 16 : cut.stop // 16]), piece[:])
             else:
-                nc.vector.tensor_copy(page[i][:].indirect(idx2[:]), incoming[i][:])
+                nc.vector.tensor_copy(page[i][:].indirect(idx2[:]), later_incoming[:, i - 1, :])
             shared = SCALAR_COLUMNS if i >= 2 else 0
             for first, last in ((0, PIECE), (PIECE, PASS), (PASS, shared)) if shared else ():
                 nc.scalar.copy(out=page_bf[:, first:last, i], in_=page[i][:, first:last])

from contextlib import ExitStack

import concourse.mybir as mybir
from concourse.masks import make_identity

K, T, S, K2, T2, H, N = 1024, 2048, 512, 512, 1024, 1024, 512
PAIRS = 512
FLOPS = 2 * (K2 * H * T2 + K * H * PAIRS + 2 * H * N * PAIRS)

F32 = mybir.dt.float32
BF16 = mybir.dt.bfloat16
I32 = mybir.dt.int32
U32 = mybir.dt.uint32
U16 = mybir.dt.uint16
U8 = mybir.dt.uint8
FP8X4 = mybir.dt.float8_e4m3fn_x4
FP4X4 = mybir.dt.float4_e2m1fn_x4
ALU = mybir.AluOpType
ACT = mybir.ActivationFunctionType

SCATTER_ORDER = (0, 2, 1, 3)
SCALAR_COLUMNS = 768
SLIVER = 32
PIECE = 256
P = 128
PACK = 4
PASS = P * PACK
WA_QUARTER = H // 4
LINE = 4
SCALE_ROWS_AT = 96
A_BANKS = ((4, 6, 4, 6), (0, 6, 0, 6))
B_BANKS = ((2, 3, 4, 5), (2, 3, 6, 7))
Y_BANKS, Y_LAST_BANKS = (4, 5, 1), (2, 3)
TURNED, TURN_BANK = 0, 0


def tile_list_sonobuoy_bearing_pairs_kernel(
    tc, tab_words, tab_scales, offs, offs2, offs3, base, xs, wa, wb_words, wb_scales, cal, wp, wd_words, wd_scales, bo, out
):
    nc = tc.nc
    with ExitStack() as ctx:
        keep = ctx.enter_context(tc.tile_pool(name="keep", bufs=1))
        psum = ctx.enter_context(tc.psum_pool(name="psum", bufs=1))
        shared_bytes = ctx.enter_context(tc.tile_pool(name="shared_bytes", bufs=1))

        def sb(shape, dtype, name, tag=None):
            return keep.tile(shape, dtype, name=name, tag=tag or name, align_bytes=64)

        def bank(name, shape, number):
            return psum.tile(shape, F32, name=name, tag=f"bank{number}")

        idx = keep.tile([P, PAIRS // 16], U16, name="idx")
        idx2 = keep.tile([P, S // 16], U16, name="idx2")
        idx3 = keep.tile([P, PAIRS // 16], U16, name="idx3")

        tab_sc = sb([P, T], U8, "tab_sc")
        nc.vector.memset(tab_sc[0:SCALE_ROWS_AT, :].bitcast(I32), 0)
        wb_sc_raw = sb([P, H], U8, "wb_sc_raw")
        nc.vector.memset(wb_sc_raw[0:SCALE_ROWS_AT, :].bitcast(I32), 0)
        wb_sc = sb([P, 2, H], U8, "wb_sc")
        v_sc = sb([P, 2, PAIRS], U8, "v_sc")
        wd_sc = sb([P, N], U8, "wd_sc")
        for scale_tile in (wb_sc, v_sc, wd_sc):
            nc.vector.memset(scale_tile[:].bitcast(I32), 0)

        base_rows = base.rearrange("(p i) t -> p i t", i=PACK)
        xs_rows = xs.rearrange("(p i) j -> p i j", i=PACK)
        wa_rows = wa.rearrange("(p i) r -> p i r", i=PACK)
        page = [sb([P, T2], F32, f"page{i}") for i in range(PACK)]
        first_cuts = (slice(0, P), slice(P, S))
        first_incoming = [sb([P, cut.stop - cut.start], F32, f"first_incoming{n}") for n, cut in enumerate(first_cuts)]
        later_incoming = sb([P, PACK - 1, S], F32, "later_incoming")
        wa_early = sb([P, PACK, H - WA_QUARTER], F32, "wa_early")
        wa_late = sb([P, PACK, WA_QUARTER], F32, "wa_late")
        wp_raw = [sb([P, PACK, N], F32, f"wp_raw{g}") for g in range(2)]
        tab_w = [sb([P, T], I32, f"tab_w{a}") for a in range(2)]
        wb_raw = sb([P, H], U16, "wb_raw")
        wb_late = [
            shared_bytes.tile([P, PASS], U16, name="wb_late0", align_bytes=64, offset=1536),
            sb([P, PASS], U16, "wb_late1"),
        ]
        wd_w = sb([P, 2, N], I32, "wd_w")
        cal_sb = sb([P, 2, PACK], F32, "cal_sb")
        bo_sb = sb([P, N // P], F32, "bo_sb")

        def load_page_rows(i):
            nc.sync.dma_start(out=page[i][:], in_=base_rows[:, i, :])


        nc.sync.dma_start(
            out=tab_sc[SCALE_ROWS_AT:P, :].bitcast(I32), in_=tab_scales.rearrange("a q t -> q a t").bitcast(I32)
        )
        nc.sync.dma_start(idx[:], offs)
        load_page_rows(SCATTER_ORDER[0])
        nc.sync.dma_start(idx2[:], offs2)
        for cut, piece in zip(first_cuts, first_incoming):
            nc.sync.dma_start(out=piece[:], in_=xs_rows[:, 0, cut])
        nc.sync.dma_start(
            out=wb_sc_raw[SCALE_ROWS_AT:P, :].bitcast(I32), in_=wb_scales.rearrange("a q c -> q a c").bitcast(I32)
        )
        load_page_rows(SCATTER_ORDER[1])
        nc.sync.dma_start(out=later_incoming[:], in_=xs_rows[:, 1:, :])
        nc.sync.dma_start(out=wb_raw[:].bitcast(I32), in_=wb_words[0].bitcast(I32))
        load_page_rows(SCATTER_ORDER[2])

        picked_sc = sb([P, PAIRS], U8, "picked_sc")
        nc.vector.tensor_copy(picked_sc[:], tab_sc[:].indirect(idx[:]))

        wb_sc_rows = sb([P, H], U8, "wb_sc_rows")
        nc.gpsimd.tensor_copy(
            out=wb_sc_rows[:].rearrange("p (g t c) -> p g t c", g=2, t=PACK),
            in_=wb_sc_raw[:].rearrange("p (g c t) -> p g t c", g=2, t=PACK),
        )

        def move_rows(target, source, quadrant):
            first = SCALE_ROWS_AT + 8 * quadrant
            nc.sync.dma_start(
                out=target[32 * quadrant : 32 * quadrant + 4, :, :].bitcast(I32),
                in_=source[first : first + 8, :].bitcast(I32),
            )

        def load_table(a, cols=slice(0, T)):
            nc.sync.dma_start(out=tab_w[a][:, cols], in_=tab_words[a].rearrange("p t i -> p (t i)").bitcast(I32)[:, cols])

        for quadrant in range(3):
            move_rows(v_sc, picked_sc, quadrant)
        nc.sync.dma_start(out=wa_early[:], in_=wa_rows[:, :, 0 : H - WA_QUARTER])
        load_page_rows(SCATTER_ORDER[3])
        load_table(0, slice(0, T // 2))
        for quadrant in range(4):
            move_rows(wb_sc, wb_sc_rows, quadrant)
        load_table(0, slice(T // 2, T))
        move_rows(v_sc, picked_sc, 3)
        nc.sync.dma_start(out=wa_late[:], in_=wa_rows[:, :, H - WA_QUARTER :])
        load_table(1)
        for g in range(2):
            nc.sync.dma_start(out=wb_late[g][:].bitcast(I32), in_=wb_words[1, :, H * g : H * (g + 1)].bitcast(I32))
        nc.sync.dma_start(idx3[:], offs3)
        wp_rows = wp.rearrange("(g p i) n -> g p i n", g=2, i=PACK)
        nc.sync.dma_start(out=cal_sb[:], in_=cal.rearrange("(g p t) -> p g t", g=2, t=PACK))
        nc.sync.dma_start(out=wp_raw[0][:], in_=wp_rows[0])
        nc.sync.dma_start(out=wp_raw[1][:], in_=wp_rows[1])
        nc.sync.dma_start(out=wd_w[:], in_=wd_words.rearrange("a p c i -> p a (c i)").bitcast(I32))
        for quadrant in range(4):
            nc.sync.dma_start(
                out=wd_sc[32 * quadrant : 32 * quadrant + 8, :].bitcast(I32),
                in_=wd_scales[:, 4 * quadrant : 4 * quadrant + 4, :].bitcast(I32),
            )
        with nc.allow_non_contiguous_dma(reason="one bias value a partition"):
            nc.sync.dma_start(out=bo_sb[:], in_=bo.rearrange("(u p) -> p u", p=P))

        def round_on_gpsimd(target, source):
            nc.gpsimd.tensor_scalar(out=target, in0=source, scalar1=1.0, scalar2=0.0, op0=ALU.mult, op1=ALU.add)

        identity = sb([P, P], F32, "identity")
        make_identity(nc, identity[:])

        wb_w = {}

        def reorder_wb(target, source):
            nc.gpsimd.tensor_copy(
                out=target.rearrange("p (g t c e) -> p g c t e", c=P // 8, t=PACK, e=8),
                in_=source.rearrange("p (g c e t) -> p g c t e", c=P // 8, t=PACK, e=8),
            )

        wb_first = sb([P, H], U16, "wb_first")
        reorder_wb(wb_first[:], wb_raw[:])
        for g in range(2):
            wb_w[0, g] = wb_first[:, PASS * g : PASS * (g + 1)]

        wa_bf = sb([P, 2, PACK, P, PACK], BF16, "wa_bf")

        def round_wa(n):
            g, part = divmod(n, 2)
            source = wa_late[:] if n == 3 else wa_early[:, :, WA_QUARTER * n : WA_QUARTER * (n + 1)]
            nc.scalar.copy(
                out=wa_bf[:, g, :, (P // 2) * part : (P // 2) * (part + 1), :].rearrange("p t c i -> p c i t"),
                in_=source.rearrange("p i (c t) -> p c i t", t=PACK),
            )

        def quantise(codes, scales, values):
            nc.vector.quantize_mx(out=codes.bitcast(FP8X4), scales=scales, in_=values)
            return codes, scales

        page_flat = sb([P, T2 * PACK], BF16, "page_flat")
        page_bf = page_flat[:].rearrange("p (c i) -> p c i", i=PACK)
        for i, quarters in zip(SCATTER_ORDER, ((), (0, 1, 2), (), (3,))):
            if i == 0:
                for cut, piece in zip(first_cuts, first_incoming):
                    nc.vector.tensor_copy(page[i][:].indirect(idx2[:, cut.start // 16 : cut.stop // 16]), piece[:])
            else:
                nc.vector.tensor_copy(page[i][:].indirect(idx2[:]), later_incoming[:, i - 1, :])
            shared = SCALAR_COLUMNS if i >= 2 else 0
            for first, last in ((0, PIECE), (PIECE, PASS), (PASS, shared)) if shared else ():
                nc.scalar.copy(out=page_bf[:, first:last, i], in_=page[i][:, first:last])
            round_on_gpsimd(page_bf[:, shared:, i], page[i][:, shared:])
            for n in quarters:
                round_wa(n)

        v_w = [sb([P, PAIRS], U32, f"v_w{a}") for a in range(2)]

        def gather_table(a):
            nc.vector.tensor_copy(v_w[a][:], tab_w[a][:].bitcast(U32).indirect(idx[:]))

        gather_table(0)

        first_codes = sb([P, T2 + PASS], U32, "first_codes", tag="picked_sc")
        wa_codes = (first_codes[:, T2:], shared_bytes.tile([P, PASS], U32, name="late_codes", align_bytes=64, offset=0)[:])
        page_sc = sb([P, T2], U8, "page_sc")
        wa_sc = sb([P, H], U8, "wa_sc")

        def quantise_wa(g, tiles):
            values = wa_bf[:, g, tiles].rearrange("p t c i -> p (t c i)")
            return quantise(wa_codes[g], wa_sc[:, PASS * g : PASS * (g + 1)], values)

        wa_q = [quantise_wa(0, slice(0, 4))]
        for n in (0, 1, 3, 2):
            cols = slice(PIECE * n, PIECE * (n + 1))
            quantise(first_codes[:, cols], page_sc[:, cols], page_flat[:, PACK * cols.start : PACK * cols.stop])
        page_q = [(first_codes[:, PASS * h : PASS * (h + 1)], page_sc[:, PASS * h : PASS * (h + 1)]) for h in range(2)]
        gather_table(1)
        wb_w[1, 0] = sb([P, PASS], U16, "wb_w10", tag="page_flat")[:]
        reorder_wb(wb_w[1, 0], wb_late[0][:])
        wa_q.append(quantise_wa(1, slice(0, 4)))

        def multiply(target, stationary, dtype, moving, start, stop):
            nc.tensor.matmul_mx(
                out=target,
                lhsT=stationary[0].bitcast(dtype),
                lhsT_scale=stationary[1],
                rhs=moving[0].bitcast(FP8X4),
                rhs_scale=moving[1],
                start=start,
                stop=stop,
            )

        def columns(operand, cols):
            return operand[0][:, cols], operand[1][:, cols]

        def quarter_cols(quarter, count=1):
            return slice(P * quarter, P * (quarter + count))

        def tile_rows(g, t):
            return slice(PASS * g + P * t, PASS * g + P * (t + 1))

        wb_w[1, 1] = sb([P, PASS], U16, "wb_w11", tag="wa_bf")[:]
        reorder_wb(wb_w[1, 1], wb_late[1][:])
        wp_bf0 = sb([P, N, PACK], BF16, "wp_bf0", tag="wb_late1")
        round_on_gpsimd(wp_bf0[:], wp_raw[0][:].rearrange("p i c -> p c i"))
        wp_head = sb([P, P, PACK], BF16, "wp_head")
        round_on_gpsimd(wp_head[:], wp_raw[1][:, :, 0:P].rearrange("p i c -> p c i"))

        at = [
            shared_bytes.tile([P, PACK, PAIRS], F32, name="at0", align_bytes=64, offset=2048),
            sb([P, PACK, PAIRS], F32, "at1"),
        ]

        first_tiles = sb([P, 2, T2], F32, "first_tiles", tag="wa_late")

        def project_page(g, t):
            a_sb = first_tiles[:, t, :] if g == 0 and t < 2 else sb([P, T2], F32, f"a_sb{g}{t}")[:]
            for h in range(2):
                a_bank = bank(f"a_bank{g}{t}{h}", [P, PASS], h + A_BANKS[g][t])
                multiply(a_bank[:], columns(wa_q[g], tile_rows(0, t)), FP8X4, page_q[h], True, True)
                nc.scalar.copy(out=a_sb[:, PASS * h : PASS * (h + 1)], in_=a_bank[:])
            last_of_group_0 = (g, t) == (0, PACK - 1)
            for cols in (quarter_cols(0), quarter_cols(1, 3)) if last_of_group_0 else (quarter_cols(0, 4),):
                offsets = idx3[:, cols.start // 16 : cols.stop // 16]
                nc.vector.tensor_copy(at[g][:, t, cols], a_sb.indirect(offsets))

        b_banks = {}

        def project_table(g, quarter, passes=(0, 1)):
            cols = quarter_cols(quarter)
            if 0 in passes:
                b_banks[g, quarter] = bank(f"b_bank{g}{quarter}", [P, PACK, P], B_BANKS[g][quarter])
            b_bank = b_banks[g, quarter]
            for a in passes:
                for t in range(PACK):
                    multiply(
                        b_bank[:, t, :],
                        (wb_w[a, g][:, tile_rows(0, t)], wb_sc[:, a, tile_rows(g, t)]),
                        FP4X4,
                        (v_w[a][:, cols], v_sc[:, a, cols]),
                        a == 0 and t == 0,
                        a == 1 and t == PACK - 1,
                    )

        cal_b = {}
        late_cal_b = sb([P, PACK, PAIRS], F32, "late_cal_b")

        def calibrate(g, quarter, gains, part=slice(0, P)):
            if g == 1 and quarter != TURNED:
                cal_b[g, quarter] = late_cal_b[:, :, quarter_cols(quarter)]
            else:
                cal_b[g, quarter] = sb([P, PACK, part.stop - part.start], F32, f"cal_b{g}{quarter}_{part.start}")
            for t in range(PACK):
                nc.scalar.activation(
                    out=cal_b[g, quarter][:, t, :],
                    in_=b_banks[g, quarter][:, t, part],
                    func=ACT.Copy,
                    scale=gains[:, t : t + 1],
                )

        def combine(engine, values, first, second, op):
            engine.tensor_tensor(
                out=values.rearrange("p (c e t) -> p c t e", e=LINE, t=PACK),
                in0=first.rearrange("p t (c e) -> p c t e", e=LINE),
                in1=second.rearrange("p t (c e) -> p c t e", e=LINE),
                op=op,
            )

        def values_of(tile, quarter, count=1):
            return tile[:, PASS * quarter : PASS * (quarter + count)]

        x1_bf = [sb([P, PACK * PAIRS], BF16, "x1_bf0")]
        x2_bf = [sb([P, PACK * PAIRS], BF16, "x2_bf0", tag="wp_raw0")]

        def product(g, quarter):
            picked = at[g][:, :, quarter_cols(quarter)]
            combine(nc.vector, values_of(x1_bf[g], quarter), b_banks[g, quarter][:], picked, ALU.mult)

        def difference(engine, g, quarter, part=slice(0, P)):
            cols = slice(P * quarter + part.start, P * quarter + part.stop)
            values = x2_bf[g][:, PACK * cols.start : PACK * cols.stop]
            combine(engine, values, at[g][:, :, cols], late_cal_b[:, :, cols] if g == 1 else cal_b[g, quarter][:], ALU.subtract)

        for quarter in range(2):
            project_table(0, quarter, (0,))
        for t in range(PACK):
            project_page(0, t)
        for quarter in range(2):
            project_table(0, quarter, (1,))
        for quarter in range(2, 4):
            project_table(0, quarter)
        for step, products in enumerate(((0, 1), (2,), (3,), ())):
            part = slice(0, P - SLIVER if step == 3 else P)
            calibrate(0, step, cal_sb[:, 0, :], part)
            difference(nc.gpsimd, 0, step, part)
            for quarter in products:
                product(0, quarter)
            project_page(1, step)
        calibrate(0, 3, cal_sb[:, 0, :], slice(P - SLIVER, P))
        difference(nc.gpsimd, 0, 3, slice(P - SLIVER, P))
        minus_cal = sb([P, PACK], F32, "minus_cal")
        nc.scalar.activation(out=minus_cal[:], in_=cal_sb[:, 1, :], func=ACT.Copy, scale=-1.0)
        for quarter in range(3):
            project_table(1, quarter)
            calibrate(1, quarter, minus_cal[:] if quarter == TURNED else cal_sb[:, 1, :])

        turned = bank("turned", [P, PACK, P], TURN_BANK)
        sources = (cal_b[1, TURNED][:], at[1][:, :, quarter_cols(TURNED)])
        for place, source in enumerate(sources):
            for t in range(PACK):
                nc.tensor.matmul(
                    turned[:, t, :],
                    source[:, t, :],
                    identity[:],
                    start=(place, t) == (0, 0),
                    stop=(place, t) == (1, PACK - 1),
                    is_transpose=True,
                )
        turned_bf = sb([P, 2, P, 2], BF16, "turned_bf")
        nc.scalar.copy(out=turned_bf[:], in_=turned[:].rearrange("j (w e) p -> j w p e", e=2))
        project_table(1, 3)
        calibrate(1, 3, cal_sb[:, 1, :])
        turned_words = turned_bf[:].rearrange("j w p e -> j (w p e)").bitcast(F32)
        back = bank("back", [P, 2, P], TURN_BANK)
        for w in range(2):
            nc.tensor.transpose(back[:, w, :], turned_words[:, P * w : P * (w + 1)], identity[:])
        wp_bf1 = sb([P, N - P, PACK], BF16, "wp_bf1", tag="turned_bf")
        nc.scalar.copy(
            out=wp_bf1[:].rearrange("p (c e) i -> p c i e", e=2),
            in_=wp_raw[1][:, :, P:].rearrange("p i (c e) -> p c i e", e=2),
        )
        x2_turned = sb([P, P, 2], F32, "x2_turned")
        nc.scalar.copy(out=x2_turned[:], in_=back[:].rearrange("p w j -> p j w"))

        second_sc = sb([P, 5, PAIRS], U8, "second_sc", tag=f"cal_b03_{P - SLIVER}")

        def quantise_wp(g, values):
            codes = sb([P, N], U32, f"wp_codes{g}")
            return quantise(codes[:], second_sc[:, 1 + g, :], values[:].rearrange("p c i -> p (c i)"))

        x2_0 = quantise(sb([P, PAIRS], U32, "x2_codes0")[:], second_sc[:, 0, :], x2_bf[0][:])
        wp_0 = quantise_wp(0, wp_bf0)
        wp_1 = (sb([P, N], U32, "wp_codes1")[:], second_sc[:, 2, :])
        quantise(*columns(wp_1, slice(0, P)), wp_head[:].rearrange("p c i -> p (c i)"))
        x1_1 = (sb([P, PAIRS], U32, "x1_codes1")[:], second_sc[:, 4, :])
        x2_1 = (sb([P, PAIRS], U32, "x2_codes1")[:], sb([P, PAIRS], U8, "x2_sc1")[:])
        x1_0 = quantise(sb([P, PAIRS], U32, "x1_codes0")[:], second_sc[:, 3, :], x1_bf[0][:])

        def quantise_quarters(x, values, quarter, count=1):
            quantise(*columns(x, quarter_cols(quarter, count)), values_of(values, quarter, count))

        out_rows = out.rearrange("(u p) j -> p u j", p=P)
        parts = {}
        for name, cols, numbers in (("half", quarter_cols(0, 2), (4, 5)), ("third", quarter_cols(2), (1,)), ("fourth", quarter_cols(3), (2, 3))):
            rows = 4 // len(numbers)
            tiles = [bank(f"y_{name}{n}", [P, rows, cols.stop - cols.start], n) for n in numbers]
            parts[name] = (cols, [(tiles[u // rows][:, u % rows, :], u % rows == 0, u % rows == rows - 1) for u in range(4)], tiles)
        wd_q = [(wd_w[:, g, :], wd_sc[4 * g : P, :]) for g in range(2)]

        def accumulate(name, weights, x, first=False, final=False):
            cols, targets, tiles = parts[name]
            for u, (target, opens, closes) in enumerate(targets):
                stationary = columns(weights, slice(P * u, P * (u + 1)))
                multiply(target, stationary, FP8X4, columns(x, cols), first and opens, final and closes)

        for name in parts:
            accumulate(name, wd_q[0], x2_0, first=True)
        for name in parts:
            accumulate(name, wp_0, x1_0)

        def finish_on_scalar(name, rows):
            cols, targets, tiles = parts[name]
            result = sb([P, len(rows), cols.stop - cols.start], F32, f"result_{name}{rows[0]}")
            for place, u in enumerate(rows):
                nc.scalar.activation(
                    out=result[:, place, :], in_=targets[u][0], func=ACT.Identity, bias=bo_sb[:, u : u + 1], scale=1.0
                )
            nc.sync.dma_start(out=out_rows[:, rows[0] : rows[-1] + 1, cols], in_=result[:])

        def finish_on_vector(name, source, first):
            result = sb([P, 2, P], F32, f"result_{name}{first}")
            bias = bo_sb[:, first : first + 2].unsqueeze(2).to_broadcast([P, 2, P])
            nc.vector.tensor_tensor(out=result[:], in0=source, in1=bias, op=ALU.add)
            nc.sync.dma_start(out=out_rows[:, first : first + 2, parts[name][0]], in_=result[:])

        x2_bf.append(sb([P, PACK * PAIRS], BF16, "x2_bf1", tag="x1_bf0"))
        x1_bf.append(sb([P, PACK * PAIRS], BF16, "x1_bf1"))
        difference(nc.gpsimd, 1, 1, slice(0, P + SLIVER))
        for quarter in range(4):
            product(1, quarter)
        quantise_quarters(x1_1, x1_bf[1], 0, 2)
        quantise_quarters(x2_1, x2_bf[1], 1)
        quantise(*columns(x2_1, quarter_cols(TURNED)), x2_turned[:].rearrange("p j w -> p (j w)").bitcast(BF16))
        accumulate("half", wd_q[1], x2_1)
        quantise(*columns(wp_1, slice(P, N)), wp_bf1[:].rearrange("p c i -> p (c i)"))
        accumulate("half", wp_1, x1_1, final=True)
        for u in range(4):
            finish_on_scalar("half", (u,))
        difference(nc.vector, 1, 2, slice(SLIVER, P))
        quantise_quarters(x1_1, x1_bf[1], 2, 2)
        accumulate("third", wp_1, x1_1)
        quantise_quarters(x2_1, x2_bf[1], 2)
        accumulate("third", wd_q[1], x2_1, final=True)
        for rows in ((0, 1), (2, 3)):
            finish_on_scalar("third", rows)
        accumulate("fourth", wp_1, x1_1)
        difference(nc.vector, 1, 3)
        quantise_quarters(x2_1, x2_bf[1], 3)
        accumulate("fourth", wd_q[1], x2_1, final=True)
        finish_on_vector("fourth", parts["fourth"][2][0][:], 0)
        finish_on_scalar("fourth", (2, 3))
